import numpy as np
import ml_dtypes


def mxq(x, axis, fmt="e4m3"):
    dtype, down = {"e4m3": (ml_dtypes.float8_e4m3fn, 7), "e5m2": (ml_dtypes.float8_e5m2, 14)}[fmt]
    v = np.moveaxis(np.asarray(x, np.float32).astype(ml_dtypes.bfloat16).astype(np.float64), axis, -1)
    blocks = v.reshape(v.shape[:-1] + (-1, 32))
    amax = np.abs(blocks).max(-1, keepdims=True)
    byte = np.maximum(np.where(amax > 0, np.frexp(amax)[1] - 1 + 127, 0) - down, 1)
    scale = np.exp2(byte - 127.0)
    codes = (blocks / scale).astype(np.float32).astype(dtype).astype(np.float64)
    return np.moveaxis((codes * scale).reshape(v.shape), -1, axis)


WIDE = False


def mx_kscale(k):
    if not WIDE:
        return np.ones(k)
    levels = np.array([10, -10, 5, -5, 0])
    if k % 512:
        return np.exp2(np.random.permutation(np.resize(levels, k // 32))).repeat(32)
    a = np.empty((k // 512, 16))
    for p in range(k // 512):
        a[p, :8] = np.random.permutation(np.resize(levels, 8))
        for g in range(8):
            far = levels[np.abs(levels - a[p, g]) >= 10]
            a[p, g + 8] = far[np.random.randint(len(far))]
    return np.exp2(a.ravel()).repeat(32)


def f64(x):
    return np.asarray(x).astype(np.float64)


def striped(idx):
    return np.tile(idx.reshape(-1, 16).T, (8, 1)).astype(np.uint16)


def unstriped(offs):
    return offs[:16].T.reshape(-1).astype(np.int64)


def pack_weight(w):
    k, n = w.shape
    w = f64(np.asarray(w, np.float32).astype(ml_dtypes.bfloat16)).reshape(k // 32, 32, n)
    amax = np.abs(w).max(1)
    byte = np.clip(np.where(amax > 0, np.frexp(amax)[1] - 1 + 127 - 7, 1), 1, 254)
    scaled = (w * np.exp2(127.0 - byte)[:, None, :]).reshape(k, n).astype(np.float32)
    words = np.ascontiguousarray(scaled.reshape(k // 512, 128, 4, n).transpose(0, 1, 3, 2)).astype(ml_dtypes.float8_e4m3fn).view(np.uint8)
    return words, np.ascontiguousarray(byte.astype(np.uint8).reshape(k // 512, 16, n))


def unpack_weight(words, scales):
    g, p, n, _ = words.shape
    vals = np.ascontiguousarray(words).view(ml_dtypes.float8_e4m3fn).astype(np.float64) * np.repeat(np.exp2(scales.astype(np.float64) - 127.0), 8, axis=1)[..., None]
    return vals.transpose(0, 1, 3, 2).reshape(g * 512, n)


def planes(y):
    n, m = y.shape
    v = y.astype(np.float32).astype(ml_dtypes.bfloat16).astype(np.float64).reshape(n // 32, 32, m)
    top = np.abs(v).max(1)
    byte = np.clip(np.where(top > 0, np.frexp(top)[1] - 1 + 127 - 7, 1), 1, 254)
    codes = (v * np.exp2(127.0 - byte)[:, None, :]).reshape(n, m).astype(np.float32).astype(ml_dtypes.float8_e4m3fn).view(np.uint8)
    words = codes.reshape(n // 512, 128, 4, m).transpose(0, 1, 3, 2)
    return np.ascontiguousarray(words), np.ascontiguousarray(byte.astype(np.uint8).reshape(n // 512, 16, m))


K, T, S, V, H, N = 1024, 1024, 512, 256, 512, 512


def setup_inputs():
    n = np.random.standard_normal
    s = mx_kscale(K)[:, None]
    u = mx_kscale(H)
    near = np.random.permutation(S)
    packed_xT = pack_weight(n((K, T)) * s)
    return {
        "x_words": packed_xT[0],
        "x_scales": packed_xT[1],
        "w1": (n((K, N)) / np.sqrt(K) / s).astype(np.float32),
        "w2": (n((K, N)) / np.sqrt(K) / s).astype(np.float32),
        "w3": (n((K, H)) / np.sqrt(K) / s * u).astype(np.float32),
        "w4": (n((H, N)) / np.sqrt(H) / u[:, None]).astype(np.float32),
        "offs": striped(np.random.permutation(T)[:S]),
        "cen": striped(np.random.permutation(S)[:V]),
        "pos1": striped(near[:V]),
        "pos2": striped(near[V:]),
    }


def reference(x_words, x_scales, w1, w2, w3, w4, offs, cen, pos1, pos2):
    xq = unpack_weight(x_words, x_scales)[:, unstriped(offs)]
    h = mxq(f64(w3), 0, "e4m3").T @ xq
    y = mxq(f64(w1), 0, "e4m3").T @ xq
    yc = y[:, unstriped(cen)]
    e = mxq(f64(w2), 0, "e4m3").T @ xq
    a0 = np.exp(np.tanh(yc - e[:, unstriped(pos1)]))
    a1 = np.exp(np.tanh(yc - e[:, unstriped(pos2)]))
    num = h[:, unstriped(pos1)] * a0 + h[:, unstriped(pos2)] * a1
    den = a0 + a1
    z = num / den
    out_0 = mxq(f64(w4), 0, "e4m3").T @ mxq(z, 0, "e4m3")
    return (out_0,) + planes(out_0)

@@ -1,0 +1,228 @@
+from contextlib import ExitStack
+
+import concourse.mybir as mybir
+
+K, T, S, V, H, N = 1024, 1024, 512, 256, 512, 512
+FLOPS = 2 * (3 * K * N * S + H * N * V)
+
+F32 = mybir.dt.float32
+BF16 = mybir.dt.bfloat16
+I32 = mybir.dt.int32
+U32 = mybir.dt.uint32
+U16 = mybir.dt.uint16
+U8 = mybir.dt.uint8
+FP8X4 = mybir.dt.float8_e4m3fn_x4
+SIGMOID = mybir.ActivationFunctionType.Sigmoid
+ADD = mybir.AluOpType.add
+SUB = mybir.AluOpType.subtract
+MULT = mybir.AluOpType.mult
+
+P = 128
+PACK = 4
+K_PASS = P * PACK
+PASSES = K // K_PASS
+HALF = V // 2
+ON_VECTOR = [0,2,2,2,4,0]
+FULL = 0
+
+
+def tile_picked_zpt_tanh_po_kernel(
+    tc, x_words, x_scales, w1, w2, w3, w4, offs, cen, pos1, pos2, out_0, out_1, out_2
+):
+    nc = tc.nc
+    with ExitStack() as ctx:
+        keep = ctx.enter_context(tc.tile_pool(name="keep", bufs=1))
+        psum = ctx.enter_context(tc.psum_pool(name="psum", bufs=8))
+
+        def sbuf(shape, dtype, name):
+            return keep.tile(shape, dtype, name=name, align_bytes=64)
+
+        def load_list(src, name):
+            lst = sbuf(list(src.shape), U16, name)
+            nc.sync.dma_start(lst[:], src)
+            return lst
+
+        def load_words(o):
+            words = sbuf([P, T], I32, "x_words%d" % o)
+            nc.sync.dma_start(words[:], x_words[o].rearrange("p c r -> p (c r)").bitcast(I32))
+            return words
+
+        def load_pass(w, o, name):
+            raw = sbuf([P, PACK, N], F32, name)
+            nc.sync.dma_start(raw[:], w[o * K_PASS : (o + 1) * K_PASS, :].rearrange("(p j) n -> p j n", j=PACK))
+            return raw
+
+        x_bytes = sbuf([P, T], U8, "x_bytes")
+        nc.gpsimd.memset(x_bytes[:].bitcast(I32), 0)
+        offs_t = load_list(offs, "offs")
+        xw = [load_words(0)]
+        for q in range(4):
+            nc.sync.dma_start(
+                x_bytes[32 * q : 32 * q + 4 * PASSES, :].bitcast(I32),
+                x_scales[:, 4 * q : 4 * q + 4, :].bitcast(I32),
+            )
+        raw = {(0, 0): load_pass(w1, 0, "w1_raw0")}
+        xw.append(load_words(1))
+        raw[(0, 1)] = load_pass(w1, 1, "w1_raw1")
+        cen_t = load_list(cen, "cen")
+        raw[(1, 0)] = load_pass(w2, 0, "w2_raw0")
+        raw[(1, 1)] = load_pass(w2, 1, "w2_raw1")
+        pos_t = [load_list(pos1, "pos1"), load_list(pos2, "pos2")]
+        raw[(2, 0)] = load_pass(w3, 0, "w3_raw0")
+        raw[(2, 1)] = load_pass(w3, 1, "w3_raw1")
+        w4_raw = sbuf([P, PACK, N], F32, "w4_raw")
+        w4_rows = w4.rearrange("(u t i) n -> t u i n", t=PACK, i=4)
+        for t in range(PACK):
+            nc.sync.dma_start(w4_raw[:, t, :], w4_rows[t])
+
+        xq = [sbuf([P, S], U32, "xq%d" % o) for o in range(PASSES)]
+        xq_scales = sbuf([P, S], U8, "xq_scales")
+        nc.vector.tensor_copy(xq[0][:], xw[0][:].bitcast(U32).indirect(offs_t[:]))
+        nc.vector.tensor_copy(xq_scales[:], x_bytes[:].indirect(offs_t[:]))
+        nc.vector.tensor_copy(xq[1][:], xw[1][:].bitcast(U32).indirect(offs_t[:]))
+
+        codes, scales, rounded, banks = {}, {}, {}, {}
+
+        def round_pass(m, o):
+            split = ON_VECTOR[PASSES * m + o]
+            dst = sbuf([P, N * PACK], BF16, "w_bf16_%d_%d" % (m, o))
+            src = raw[(m, o)][:].rearrange("p j (u t i) -> p u t j i", t=PACK, i=4)
+            view = dst[:].rearrange("p (t u i j) -> p u t j i", t=PACK, i=4, j=PACK)
+            if split > 0:
+                nc.vector.tensor_copy(view[:, :, :split], src[:, :, :split])
+            if split < PACK:
+                nc.scalar.copy(view[:, :, split:], src[:, :, split:])
+            rounded[(m, o)] = dst
+            codes[(m, o)] = sbuf([P, N], U32, "codes_%d_%d" % (m, o))
+            scales[(m, o)] = sbuf([P, N], U8, "scales_%d_%d" % (m, o))
+
+        def quantise(m, o, t0, t1):
+            nc.vector.quantize_mx(
+                out=codes[(m, o)][:, t0 * P : t1 * P].bitcast(FP8X4),
+                scales=scales[(m, o)][:, t0 * P : t1 * P],
+                in_=rounded[(m, o)][:, t0 * P * PACK : t1 * P * PACK],
+            )
+
+        def multiply(m, o, t):
+            if o == 0:
+                banks[(m, t)] = psum.tile([P, S], F32, name="bank")
+            nc.tensor.matmul_mx(
+                out=banks[(m, t)][:],
+                lhsT=codes[(m, o)][:, t * P : (t + 1) * P].bitcast(FP8X4),
+                lhsT_scale=scales[(m, o)][:, t * P : (t + 1) * P],
+                rhs=xq[o][:].bitcast(FP8X4),
+                rhs_scale=xq_scales[4 * o : P, :],
+                start=(o == 0),
+                stop=(o == PASSES - 1),
+            )
+
+        def first_pass(m):
+            quantise(m, 0, 0, PACK)
+            for t in range(PACK):
+                multiply(m, 0, t)
+
+        def last_pass(m):
+            results = []
+            for t0 in (0, 2):
+                quantise(m, 1, t0, t0 + 2)
+                for t in (t0, t0 + 1):
+                    multiply(m, 1, t)
+                    res = sbuf([P, S], F32, "res_%d_%d" % (m, t))
+                    nc.scalar.copy(res[:], banks[(m, t)][:])
+                    results.append(res)
+            return results
+
+        round_pass(0, 0)
+        first_pass(0)
+        round_pass(0, 1)
+        y = last_pass(0)
+        round_pass(1, 0)
+        first_pass(1)
+        round_pass(1, 1)
+        e = last_pass(1)
+        yc = [sbuf([P, V], F32, "yc%d" % t) for t in range(PACK)]
+        for t in range(PACK):
+            nc.vector.tensor_copy(yc[t][:], y[t][:].indirect(cen_t[:]))
+        round_pass(2, 0)
+        first_pass(2)
+        round_pass(2, 1)
+        diff = [sbuf([P, 2, V], F32, "diff%d" % t) for t in range(PACK)]
+        for t in range(PACK):
+            for d in range(2):
+                nc.vector.tensor_tensor(diff[t][:, d, :], e[t][:].indirect(pos_t[d][:]), yc[t][:], SUB)
+
+        def round_w4():
+            w4_bf16 = sbuf([P, N * PACK], BF16, "w4_bf16")
+            nc.scalar.copy(
+                w4_bf16[:].rearrange("p (t m j) -> p m j t", t=PACK, j=PACK),
+                w4_raw[:].rearrange("p j (m t) -> p m j t", t=PACK),
+            )
+            nc.vector.quantize_mx(out=w4_codes[:].bitcast(FP8X4), scales=w4_scales[:], in_=w4_bf16[:])
+
+        w4_codes = sbuf([P, N], U32, "w4_codes")
+        w4_scales = sbuf([P, N], U8, "w4_scales")
+
+        h = last_pass(2)
+
+        share = []
+        for t in range(PACK):
+            squashed = sbuf([P, 2, V], F32, "squashed%d" % t)
+            nc.scalar.activation(squashed[:], diff[t][:], SIGMOID, scale=-2.0)
+            lead = sbuf([P, V], F32, "lead%d" % t)
+            nc.vector.tensor_tensor(lead[:], squashed[:, 0, :], squashed[:, 1, :], SUB)
+            pair = sbuf([P, 2, V], F32, "share%d" % t)
+            nc.scalar.activation(pair[:, 0, :], lead[:], SIGMOID, scale=2.0)
+            nc.scalar.activation(pair[:, 1, :], lead[:], SIGMOID, scale=-2.0)
+            share.append(pair)
+        round_w4()
+
+        out_scales = sbuf([P, V], U8, "out_scales")
+        for g in range(2):
+            cols = slice(g * HALF, (g + 1) * HALF)
+            lists = slice(g * HALF // 16, (g + 1) * HALF // 16)
+            terms = [sbuf([P, PACK, HALF], F32, "term%d" % d) for d in range(2)]
+            for t in range(PACK):
+                for d in range(2):
+                    nc.vector.tensor_tensor(
+                        terms[d][:, t, :], h[t][:].indirect(pos_t[d][:, lists]), share[t][:, d, cols], MULT
+                    )
+            z = sbuf([P, HALF * PACK], BF16, "z%d" % g)
+            nc.vector.tensor_tensor(
+                z[:].rearrange("p (c i t) -> p c t i", i=4, t=PACK),
+                terms[0][:].rearrange("p t (c i) -> p c t i", i=4),
+                terms[1][:].rearrange("p t (c i) -> p c t i", i=4),
+                ADD,
+            )
+            z_codes = sbuf([P, HALF], U32, "z_codes%d" % g)
+            z_scales = sbuf([P, HALF], U8, "z_scales%d" % g)
+            nc.vector.quantize_mx(out=z_codes[:].bitcast(FP8X4), scales=z_scales[:], in_=z[:])
+            bank = psum.tile([P, S], F32, name="bank")
+            for t in range(PACK):
+                nc.tensor.matmul_mx(
+                    out=bank[:, t * HALF : (t + 1) * HALF],
+                    lhsT=w4_codes[:, t * P : (t + 1) * P].bitcast(FP8X4),
+                    lhsT_scale=w4_scales[:, t * P : (t + 1) * P],
+                    rhs=z_codes[:].bitcast(FP8X4),
+                    rhs_scale=z_scales[:],
+                    start=True,
+                    stop=True,
+                )
+            res_bf16 = sbuf([P, HALF * PACK], BF16, "res_bf16_%d" % g)
+            src = bank[:].rearrange("p (t v) -> p v t", t=PACK)
+            dst = res_bf16[:].rearrange("p (v t) -> p v t", t=PACK)
+            if g == 0:
+                nc.scalar.copy(dst, src)
+            else:
+                nc.vector.tensor_copy(dst, src)
+            res = sbuf([P, PACK, HALF], F32, "out%d" % g)
+            nc.scalar.copy(res[:].rearrange("p t v -> p (t v)"), bank[:])
+            nc.scalar.dma_start(out_0.rearrange("(p t) v -> p t v", t=PACK)[:, :, cols], res[:])
+            out_codes = sbuf([P, HALF], U32, "out_codes%d" % g)
+            nc.vector.quantize_mx(out=out_codes[:].bitcast(FP8X4), scales=out_scales[:, cols], in_=res_bf16[:])
+            nc.sync.dma_start(
+                out_1[0].rearrange("p c r -> p (c r)").bitcast(I32)[:, cols], out_codes[:].bitcast(I32)
+            )
+        for q in range(4):
+            nc.sync.dma_start(
+                out_2[0, 4 * q : 4 * q + 4, :].bitcast(I32), out_scales[32 * q : 32 * q + 4, :].bitcast(I32)
+            )

@@ -22,8 +22,8 @@ PACK = 4
 K_PASS = P * PACK
 PASSES = K // K_PASS
 HALF = V // 2
-ON_VECTOR = [0,2,2,2,4,0]
-FULL = 0
+ON_VECTOR = [0,2,4,1,0,1]
+FULL = 3
 
 
 def tile_picked_zpt_tanh_po_kernel(
@@ -53,15 +53,15 @@ def tile_picked_zpt_tanh_po_kernel(
             return raw
 
         x_bytes = sbuf([P, T], U8, "x_bytes")
-        nc.gpsimd.memset(x_bytes[:].bitcast(I32), 0)
+        nc.vector.memset(x_bytes[:].bitcast(I32), 0)
         offs_t = load_list(offs, "offs")
         xw = [load_words(0)]
+        raw = {(0, 0): load_pass(w1, 0, "w1_raw0")}
         for q in range(4):
             nc.sync.dma_start(
                 x_bytes[32 * q : 32 * q + 4 * PASSES, :].bitcast(I32),
                 x_scales[:, 4 * q : 4 * q + 4, :].bitcast(I32),
             )
-        raw = {(0, 0): load_pass(w1, 0, "w1_raw0")}
         xw.append(load_words(1))
         raw[(0, 1)] = load_pass(w1, 1, "w1_raw1")
         cen_t = load_list(cen, "cen")
@@ -75,6 +75,8 @@ def tile_picked_zpt_tanh_po_kernel(
         for t in range(PACK):
             nc.sync.dma_start(w4_raw[:, t, :], w4_rows[t])
 
+        warm = sbuf([P, 1], F32, "warm")
+        nc.scalar.activation(warm[:], raw[(0, 0)][:, 0, 0:1], SIGMOID)
         xq = [sbuf([P, S], U32, "xq%d" % o) for o in range(PASSES)]
         xq_scales = sbuf([P, S], U8, "xq_scales")
         nc.vector.tensor_copy(xq[0][:], xw[0][:].bitcast(U32).indirect(offs_t[:]))
@@ -86,12 +88,13 @@ def tile_picked_zpt_tanh_po_kernel(
         def round_pass(m, o):
             split = ON_VECTOR[PASSES * m + o]
             dst = sbuf([P, N * PACK], BF16, "w_bf16_%d_%d" % (m, o))
-            src = raw[(m, o)][:].rearrange("p j (u t i) -> p u t j i", t=PACK, i=4)
-            view = dst[:].rearrange("p (t u i j) -> p u t j i", t=PACK, i=4, j=PACK)
-            if split > 0:
-                nc.vector.tensor_copy(view[:, :, :split], src[:, :, :split])
-            if split < PACK:
-                nc.scalar.copy(view[:, :, split:], src[:, :, split:])
+            src = raw[(m, o)][:].rearrange("p j (u t i) -> p t u j i", t=PACK, i=4)
+            view = dst[:].rearrange("p (t u i j) -> p t u j i", t=PACK, i=4, j=PACK)
+            for t0 in range(0, split, 2):
+                t1 = min(split, t0 + 2)
+                nc.vector.tensor_copy(view[:, t0:t1], src[:, t0:t1])
+            for t in range(split, PACK):
+                nc.scalar.copy(view[:, t], src[:, t])
             rounded[(m, o)] = dst
             codes[(m, o)] = sbuf([P, N], U32, "codes_%d_%d" % (m, o))
             scales[(m, o)] = sbuf([P, N], U8, "scales_%d_%d" % (m, o))
@@ -117,19 +120,23 @@ def tile_picked_zpt_tanh_po_kernel(
             )
 
         def first_pass(m):
-            quantise(m, 0, 0, PACK)
-            for t in range(PACK):
-                multiply(m, 0, t)
-
-        def last_pass(m):
-            results = []
             for t0 in (0, 2):
-                quantise(m, 1, t0, t0 + 2)
+                quantise(m, 0, t0, t0 + 2)
                 for t in (t0, t0 + 1):
+                    multiply(m, 0, t)
+
+        def last_pass(m, then=None):
+            results = []
+            step = 2 if m == 2 else 1
+            for t0 in range(0, PACK, step):
+                quantise(m, 1, t0, t0 + step)
+                for t in range(t0, t0 + step):
                     multiply(m, 1, t)
-                    res = sbuf([P, S], F32, "res_%d_%d" % (m, t))
+                    res = sbuf([P, S], F32, "w3_raw0" if (m, t) == (1, 3) else "res_%d_%d" % (m, t))
                     nc.scalar.copy(res[:], banks[(m, t)][:])
                     results.append(res)
+                    if then is not None:
+                        then(t)
             return results
 
         round_pass(0, 0)
@@ -139,58 +146,66 @@ def tile_picked_zpt_tanh_po_kernel(
         round_pass(1, 0)
         first_pass(1)
         round_pass(1, 1)
-        e = last_pass(1)
-        yc = [sbuf([P, V], F32, "yc%d" % t) for t in range(PACK)]
-        for t in range(PACK):
-            nc.vector.tensor_copy(yc[t][:], y[t][:].indirect(cen_t[:]))
         round_pass(2, 0)
+        e = last_pass(1)
+        yc_early = sbuf([P, V], F32, "w2_raw0")
+        yc_late = sbuf([P, 3, V], F32, "w2_raw1")
+        yc = [yc_early[:], yc_late[:, 0, :], yc_late[:, 1, :], yc_late[:, 2, :]]
+        for t in range(PACK):
+            nc.vector.tensor_copy(yc[t], y[t][:].indirect(cen_t[:]))
         first_pass(2)
         round_pass(2, 1)
-        diff = [sbuf([P, 2, V], F32, "diff%d" % t) for t in range(PACK)]
+        diffs = [sbuf([P, 2, 2, V], F32, "diff%d" % r) for r in range(2)]
+        diff = [diffs[t // 2][:, t % 2] for t in range(PACK)]
         for t in range(PACK):
             for d in range(2):
-                nc.vector.tensor_tensor(diff[t][:, d, :], e[t][:].indirect(pos_t[d][:]), yc[t][:], SUB)
+                nc.vector.tensor_tensor(diff[t][:, d, :], e[t][:].indirect(pos_t[d][:]), yc[t], SUB)
 
         def round_w4():
-            w4_bf16 = sbuf([P, N * PACK], BF16, "w4_bf16")
-            nc.scalar.copy(
-                w4_bf16[:].rearrange("p (t m j) -> p m j t", t=PACK, j=PACK),
-                w4_raw[:].rearrange("p j (m t) -> p m j t", t=PACK),
-            )
+            dst = w4_bf16[:].rearrange("p (t m j) -> p m j t", t=PACK, j=PACK)
+            src = w4_raw[:].rearrange("p j (m t) -> p m j t", t=PACK)
+            nc.vector.tensor_copy(dst[:, :48], src[:, :48])
+            nc.scalar.copy(dst[:, 48:], src[:, 48:])
             nc.vector.quantize_mx(out=w4_codes[:].bitcast(FP8X4), scales=w4_scales[:], in_=w4_bf16[:])
 
+        w4_bf16 = sbuf([P, N * PACK], BF16, "w4_bf16")
         w4_codes = sbuf([P, N], U32, "w4_codes")
         w4_scales = sbuf([P, N], U8, "w4_scales")
 
-        h = last_pass(2)
+        squashed = sbuf([P, PACK, 2, V], F32, "w3_raw1")
+        leads = [sbuf([P, 2, V], F32, "lead%d" % r) for r in range(2)]
+        for r in range(2):
+            pair = squashed[:, 2 * r : 2 * r + 2]
+            nc.scalar.activation(pair, diffs[r][:], SIGMOID, scale=-2.0)
+            nc.vector.tensor_tensor(leads[r][:], pair[:, :, 0, :], pair[:, :, 1, :], SUB)
+        lead = [leads[t // 2][:, t % 2, :] for t in range(PACK)]
+        share = [sbuf([P, 2, V], F32, "share%d" % t) for t in range(PACK)]
 
-        share = []
-        for t in range(PACK):
-            squashed = sbuf([P, 2, V], F32, "squashed%d" % t)
-            nc.scalar.activation(squashed[:], diff[t][:], SIGMOID, scale=-2.0)
-            lead = sbuf([P, V], F32, "lead%d" % t)
-            nc.vector.tensor_tensor(lead[:], squashed[:, 0, :], squashed[:, 1, :], SUB)
-            pair = sbuf([P, 2, V], F32, "share%d" % t)
-            nc.scalar.activation(pair[:, 0, :], lead[:], SIGMOID, scale=2.0)
-            nc.scalar.activation(pair[:, 1, :], lead[:], SIGMOID, scale=-2.0)
-            share.append(pair)
+        def make_share(t):
+            nc.scalar.activation(share[t][:, 0, :], lead[t], SIGMOID, scale=2.0)
+            nc.scalar.activation(share[t][:, 1, :], lead[t], SIGMOID, scale=-2.0)
+
+        h = last_pass(2, make_share)
         round_w4()
 
+        terms = [sbuf([P, PACK, V], F32, "term%d" % d) for d in range(2)]
+        for t in range(FULL):
+            for d in range(2):
+                nc.vector.tensor_tensor(terms[d][:, t, :], h[t][:].indirect(pos_t[d][:]), share[t][:, d, :], MULT)
         out_scales = sbuf([P, V], U8, "out_scales")
         for g in range(2):
             cols = slice(g * HALF, (g + 1) * HALF)
             lists = slice(g * HALF // 16, (g + 1) * HALF // 16)
-            terms = [sbuf([P, PACK, HALF], F32, "term%d" % d) for d in range(2)]
-            for t in range(PACK):
+            for t in range(FULL, PACK):
                 for d in range(2):
                     nc.vector.tensor_tensor(
-                        terms[d][:, t, :], h[t][:].indirect(pos_t[d][:, lists]), share[t][:, d, cols], MULT
+                        terms[d][:, t, cols], h[t][:].indirect(pos_t[d][:, lists]), share[t][:, d, cols], MULT
                     )
             z = sbuf([P, HALF * PACK], BF16, "z%d" % g)
             nc.vector.tensor_tensor(
                 z[:].rearrange("p (c i t) -> p c t i", i=4, t=PACK),
-                terms[0][:].rearrange("p t (c i) -> p c t i", i=4),
-                terms[1][:].rearrange("p t (c i) -> p c t i", i=4),
+                terms[0][:, :, cols].rearrange("p t (c i) -> p c t i", i=4),
+                terms[1][:, :, cols].rearrange("p t (c i) -> p c t i", i=4),
                 ADD,
             )
             z_codes = sbuf([P, HALF], U32, "z_codes%d" % g)

@@ -22,7 +22,7 @@ PACK = 4
 K_PASS = P * PACK
 PASSES = K // K_PASS
 HALF = V // 2
-ON_VECTOR = [0,2,4,1,0,1]
+ON_VECTOR = [0,2,4,2,0,1]
 FULL = 3
 
 
@@ -164,8 +164,8 @@ def tile_picked_zpt_tanh_po_kernel(
         def round_w4():
             dst = w4_bf16[:].rearrange("p (t m j) -> p m j t", t=PACK, j=PACK)
             src = w4_raw[:].rearrange("p j (m t) -> p m j t", t=PACK)
-            nc.vector.tensor_copy(dst[:, :48], src[:, :48])
-            nc.scalar.copy(dst[:, 48:], src[:, 48:])
+            nc.vector.tensor_copy(dst[:, :96], src[:, :96])
+            nc.scalar.copy(dst[:, 96:], src[:, 96:])
             nc.vector.quantize_mx(out=w4_codes[:].bitcast(FP8X4), scales=w4_scales[:], in_=w4_bf16[:])
 
         w4_bf16 = sbuf([P, N * PACK], BF16, "w4_bf16")
@@ -230,8 +230,13 @@ def tile_picked_zpt_tanh_po_kernel(
             else:
                 nc.vector.tensor_copy(dst, src)
             res = sbuf([P, PACK, HALF], F32, "out%d" % g)
-            nc.scalar.copy(res[:].rearrange("p t v -> p (t v)"), bank[:])
-            nc.scalar.dma_start(out_0.rearrange("(p t) v -> p t v", t=PACK)[:, :, cols], res[:])
+            rows = out_0.rearrange("(p t) v -> p t v", t=PACK)
+            step = PACK if g == 0 else 2
+            for t0 in range(0, PACK, step):
+                nc.scalar.copy(
+                    res[:, t0 : t0 + step].rearrange("p t v -> p (t v)"), bank[:, t0 * HALF : (t0 + step) * HALF]
+                )
+                nc.scalar.dma_start(rows[:, t0 : t0 + step, cols], res[:, t0 : t0 + step])
             out_codes = sbuf([P, HALF], U32, "out_codes%d" % g)
             nc.vector.quantize_mx(out=out_codes[:].bitcast(FP8X4), scales=out_scales[:, cols], in_=res_bf16[:])
             nc.sync.dma_start(

@@ -1,6 +1,7 @@
 from contextlib import ExitStack
 
 import concourse.mybir as mybir
+from concourse.masks import make_identity
 
 K, T, S, V, H, N = 1024, 1024, 512, 256, 512, 512
 FLOPS = 2 * (3 * K * N * S + H * N * V)
@@ -22,8 +23,6 @@ PACK = 4
 K_PASS = P * PACK
 PASSES = K // K_PASS
 HALF = V // 2
-ON_VECTOR = [0,2,4,2,0,1]
-FULL = 3
 
 
 def tile_picked_zpt_tanh_po_kernel(
@@ -32,7 +31,7 @@ def tile_picked_zpt_tanh_po_kernel(
     nc = tc.nc
     with ExitStack() as ctx:
         keep = ctx.enter_context(tc.tile_pool(name="keep", bufs=1))
-        psum = ctx.enter_context(tc.psum_pool(name="psum", bufs=8))
+        psum = ctx.enter_context(tc.psum_pool(name="psum", bufs=1))
 
         def sbuf(shape, dtype, name):
             return keep.tile(shape, dtype, name=name, align_bytes=64)
@@ -77,144 +76,154 @@ def tile_picked_zpt_tanh_po_kernel(
 
         warm = sbuf([P, 1], F32, "warm")
         nc.scalar.activation(warm[:], raw[(0, 0)][:, 0, 0:1], SIGMOID)
+
         xq = [sbuf([P, S], U32, "xq%d" % o) for o in range(PASSES)]
         xq_scales = sbuf([P, S], U8, "xq_scales")
-        nc.vector.tensor_copy(xq[0][:], xw[0][:].bitcast(U32).indirect(offs_t[:]))
-        nc.vector.tensor_copy(xq_scales[:], x_bytes[:].indirect(offs_t[:]))
-        nc.vector.tensor_copy(xq[1][:], xw[1][:].bitcast(U32).indirect(offs_t[:]))
 
-        codes, scales, rounded, banks = {}, {}, {}, {}
+        codes, scales, rounded, banks, res = {}, {}, {}, {}, {}
+        for m in range(3):
+            for o in range(PASSES):
+                for r in range(2):
+                    rounded[(m, o, r)] = sbuf([P, 2 * P * PACK], BF16, "bf_%d_%d_%d" % (m, o, r))
 
-        def round_pass(m, o):
-            split = ON_VECTOR[PASSES * m + o]
-            dst = sbuf([P, N * PACK], BF16, "w_bf16_%d_%d" % (m, o))
-            src = raw[(m, o)][:].rearrange("p j (u t i) -> p t u j i", t=PACK, i=4)
-            view = dst[:].rearrange("p (t u i j) -> p t u j i", t=PACK, i=4, j=PACK)
-            for t0 in range(0, split, 2):
-                t1 = min(split, t0 + 2)
-                nc.vector.tensor_copy(view[:, t0:t1], src[:, t0:t1])
-            for t in range(split, PACK):
-                nc.scalar.copy(view[:, t], src[:, t])
-            rounded[(m, o)] = dst
-            codes[(m, o)] = sbuf([P, N], U32, "codes_%d_%d" % (m, o))
-            scales[(m, o)] = sbuf([P, N], U8, "scales_%d_%d" % (m, o))
+        def views(m, o, r):
+            src = raw[(m, o)][:].rearrange("p j (u t i) -> p t u j i", t=PACK, i=4)[:, 2 * r : 2 * r + 2]
+            dst = rounded[(m, o, r)][:].rearrange("p (t u i j) -> p t u j i", t=2, i=4, j=PACK)
+            return dst, src
 
-        def quantise(m, o, t0, t1):
+        def round_v(m, o, r, ts=(0, 1)):
+            dst, src = views(m, o, r)
+            nc.vector.tensor_copy(dst[:, ts[0] : ts[-1] + 1], src[:, ts[0] : ts[-1] + 1])
+
+        def round_s(m, o, r, ts=(0, 1)):
+            dst, src = views(m, o, r)
+            for t in ts:
+                nc.scalar.copy(dst[:, t], src[:, t])
+
+        def quantise(m, o, r, ts=(0, 1), name=None):
+            a, b = ts[0], ts[-1] + 1
+            if a == 0:
+                codes[(m, o, r)] = sbuf([P, 2 * P], U32, name or "codes_%d_%d_%d" % (m, o, r))
+                scales[(m, o, r)] = sbuf([P, 2 * P], U8, "scales_%d_%d_%d" % (m, o, r))
             nc.vector.quantize_mx(
-                out=codes[(m, o)][:, t0 * P : t1 * P].bitcast(FP8X4),
-                scales=scales[(m, o)][:, t0 * P : t1 * P],
-                in_=rounded[(m, o)][:, t0 * P * PACK : t1 * P * PACK],
+                out=codes[(m, o, r)][:, a * P : b * P].bitcast(FP8X4),
+                scales=scales[(m, o, r)][:, a * P : b * P],
+                in_=rounded[(m, o, r)][:, a * P * PACK : b * P * PACK],
             )
+            for t in range(2 * r + a, 2 * r + b):
+                multiply(m, o, t)
+
+        def bank(n):
+            return psum.tile([P, S], F32, name="bank%d" % n)
 
         def multiply(m, o, t):
             if o == 0:
-                banks[(m, t)] = psum.tile([P, S], F32, name="bank")
+                banks[(m, t)] = bank(PACK * (m % 2) + t)
+            cols = slice(t % 2 * P, (t % 2 + 1) * P)
             nc.tensor.matmul_mx(
                 out=banks[(m, t)][:],
-                lhsT=codes[(m, o)][:, t * P : (t + 1) * P].bitcast(FP8X4),
-                lhsT_scale=scales[(m, o)][:, t * P : (t + 1) * P],
+                lhsT=codes[(m, o, t // 2)][:, cols].bitcast(FP8X4),
+                lhsT_scale=scales[(m, o, t // 2)][:, cols],
                 rhs=xq[o][:].bitcast(FP8X4),
                 rhs_scale=xq_scales[4 * o : P, :],
                 start=(o == 0),
                 stop=(o == PASSES - 1),
             )
 
-        def first_pass(m):
-            for t0 in (0, 2):
-                quantise(m, 0, t0, t0 + 2)
-                for t in (t0, t0 + 1):
-                    multiply(m, 0, t)
+        def drain(m, t, name=None):
+            res[(m, t)] = sbuf([P, S], F32, name or "res_%d_%d" % (m, t))
+            nc.scalar.copy(res[(m, t)][:], banks[(m, t)][:])
 
-        def last_pass(m, then=None):
-            results = []
-            step = 2 if m == 2 else 1
-            for t0 in range(0, PACK, step):
-                quantise(m, 1, t0, t0 + step)
-                for t in range(t0, t0 + step):
-                    multiply(m, 1, t)
-                    res = sbuf([P, S], F32, "w3_raw0" if (m, t) == (1, 3) else "res_%d_%d" % (m, t))
-                    nc.scalar.copy(res[:], banks[(m, t)][:])
-                    results.append(res)
-                    if then is not None:
-                        then(t)
-            return results
+        yc, diff, squashed, lead, share = {}, {}, {}, {}, {}
 
-        round_pass(0, 0)
-        first_pass(0)
-        round_pass(0, 1)
-        y = last_pass(0)
-        round_pass(1, 0)
-        first_pass(1)
-        round_pass(1, 1)
-        round_pass(2, 0)
-        e = last_pass(1)
-        yc_early = sbuf([P, V], F32, "w2_raw0")
-        yc_late = sbuf([P, 3, V], F32, "w2_raw1")
-        yc = [yc_early[:], yc_late[:, 0, :], yc_late[:, 1, :], yc_late[:, 2, :]]
-        for t in range(PACK):
-            nc.vector.tensor_copy(yc[t], y[t][:].indirect(cen_t[:]))
-        first_pass(2)
-        round_pass(2, 1)
-        diffs = [sbuf([P, 2, 2, V], F32, "diff%d" % r) for r in range(2)]
-        diff = [diffs[t // 2][:, t % 2] for t in range(PACK)]
-        for t in range(PACK):
+        def centres(ts, name):
+            picked = sbuf([P, len(ts), V], F32, name)
+            for n, t in enumerate(ts):
+                yc[t] = picked[:, n, :]
+                nc.vector.tensor_copy(yc[t], res[(0, t)][:].indirect(cen_t[:]))
+
+        def keys(t, name=None):
+            diff[t] = sbuf([P, 2, V], F32, name or "diff%d" % t)
             for d in range(2):
-                nc.vector.tensor_tensor(diff[t][:, d, :], e[t][:].indirect(pos_t[d][:]), yc[t], SUB)
+                nc.vector.tensor_tensor(diff[t][:, d, :], res[(1, t)][:].indirect(pos_t[d][:]), yc[t], SUB)
 
-        def round_w4():
-            dst = w4_bf16[:].rearrange("p (t m j) -> p m j t", t=PACK, j=PACK)
-            src = w4_raw[:].rearrange("p j (m t) -> p m j t", t=PACK)
-            nc.vector.tensor_copy(dst[:, :96], src[:, :96])
-            nc.scalar.copy(dst[:, 96:], src[:, 96:])
-            nc.vector.quantize_mx(out=w4_codes[:].bitcast(FP8X4), scales=w4_scales[:], in_=w4_bf16[:])
+        ident = sbuf([P, P], F32, "ident")
+        make_identity(nc, ident[:])
+        turned = {}
+
+        def turn(t, n):
+            turned[t] = bank(n)
+            for d in range(2):
+                for g in range(2):
+                    c = (2 * d + g) * P
+                    nc.tensor.transpose(turned[t][:, c : c + P], diff[t][:, d, g * P : (g + 1) * P], ident[:])
+
+        def squash(ts, name):
+            both = sbuf([P, len(ts), 2, V], F32, name)
+            for n, t in enumerate(ts):
+                squashed[t] = both[:, n]
+                for d in range(2):
+                    nc.scalar.activation(squashed[t][:, d, :], turned[t][:, d * V : (d + 1) * V], SIGMOID, scale=4.0 * d - 2.0)
+
+        def leading(t, n):
+            lead[t] = bank(n)
+            for g in range(2):
+                for d in range(2):
+                    nc.tensor.matmul(
+                        lead[t][:, g * P : (g + 1) * P],
+                        squashed[t][:, d, g * P : (g + 1) * P],
+                        ident[:],
+                        start=(d == 0),
+                        stop=(d == 1),
+                        is_transpose=True,
+                    )
+
+        def shares(t, name=None):
+            share[t] = sbuf([P, 2, V], F32, name or "share%d" % t)
+            for d in range(2):
+                nc.scalar.activation(share[t][:, d, :], lead[t][:, :V], SIGMOID, scale=2.0 - 4.0 * d, bias=4.0 * d - 2.0)
 
         w4_bf16 = sbuf([P, N * PACK], BF16, "w4_bf16")
         w4_codes = sbuf([P, N], U32, "w4_codes")
         w4_scales = sbuf([P, N], U8, "w4_scales")
-
-        squashed = sbuf([P, PACK, 2, V], F32, "w3_raw1")
-        leads = [sbuf([P, 2, V], F32, "lead%d" % r) for r in range(2)]
-        for r in range(2):
-            pair = squashed[:, 2 * r : 2 * r + 2]
-            nc.scalar.activation(pair, diffs[r][:], SIGMOID, scale=-2.0)
-            nc.vector.tensor_tensor(leads[r][:], pair[:, :, 0, :], pair[:, :, 1, :], SUB)
-        lead = [leads[t // 2][:, t % 2, :] for t in range(PACK)]
-        share = [sbuf([P, 2, V], F32, "share%d" % t) for t in range(PACK)]
-
-        def make_share(t):
-            nc.scalar.activation(share[t][:, 0, :], lead[t], SIGMOID, scale=2.0)
-            nc.scalar.activation(share[t][:, 1, :], lead[t], SIGMOID, scale=-2.0)
-
-        h = last_pass(2, make_share)
-        round_w4()
+        w4_dst = w4_bf16[:].rearrange("p (t m j) -> p m j t", t=PACK, j=PACK)
+        w4_src = w4_raw[:].rearrange("p j (m t) -> p m j t", t=PACK)
 
         terms = [sbuf([P, PACK, V], F32, "term%d" % d) for d in range(2)]
-        for t in range(FULL):
+
+        def values(t, c0, c1):
             for d in range(2):
-                nc.vector.tensor_tensor(terms[d][:, t, :], h[t][:].indirect(pos_t[d][:]), share[t][:, d, :], MULT)
+                nc.vector.tensor_tensor(
+                    terms[d][:, t, c0:c1],
+                    res[(2, t)][:].indirect(pos_t[d][:, c0 // 16 : c1 // 16]),
+                    share[t][:, d, c0:c1],
+                    MULT,
+                )
+
         out_scales = sbuf([P, V], U8, "out_scales")
-        for g in range(2):
-            cols = slice(g * HALF, (g + 1) * HALF)
-            lists = slice(g * HALF // 16, (g + 1) * HALF // 16)
-            for t in range(FULL, PACK):
-                for d in range(2):
-                    nc.vector.tensor_tensor(
-                        terms[d][:, t, cols], h[t][:].indirect(pos_t[d][:, lists]), share[t][:, d, cols], MULT
-                    )
-            z = sbuf([P, HALF * PACK], BF16, "z%d" % g)
+        rows = out_0.rearrange("(p t) v -> p t v", t=PACK)
+        zq, obank, obf = {}, {}, {}
+
+        def mix(c0, c1):
+            w = c1 - c0
+            z = sbuf([P, w * PACK], BF16, "z%d" % c0)
             nc.vector.tensor_tensor(
                 z[:].rearrange("p (c i t) -> p c t i", i=4, t=PACK),
-                terms[0][:, :, cols].rearrange("p t (c i) -> p c t i", i=4),
-                terms[1][:, :, cols].rearrange("p t (c i) -> p c t i", i=4),
+                terms[0][:, :, c0:c1].rearrange("p t (c i) -> p c t i", i=4),
+                terms[1][:, :, c0:c1].rearrange("p t (c i) -> p c t i", i=4),
                 ADD,
             )
-            z_codes = sbuf([P, HALF], U32, "z_codes%d" % g)
-            z_scales = sbuf([P, HALF], U8, "z_scales%d" % g)
-            nc.vector.quantize_mx(out=z_codes[:].bitcast(FP8X4), scales=z_scales[:], in_=z[:])
-            bank = psum.tile([P, S], F32, name="bank")
+            zq[c0] = z
+
+        def project(c0, c1, n):
+            w = c1 - c0
+            z_codes = sbuf([P, w], U32, "z_codes%d" % c0)
+            z_scales = sbuf([P, w], U8, "z_scales%d" % c0)
+            nc.vector.quantize_mx(out=z_codes[:].bitcast(FP8X4), scales=z_scales[:], in_=zq[c0][:])
+            obank[c0] = bank(n)
             for t in range(PACK):
                 nc.tensor.matmul_mx(
-                    out=bank[:, t * HALF : (t + 1) * HALF],
+                    out=obank[c0][:, t * w : (t + 1) * w],
                     lhsT=w4_codes[:, t * P : (t + 1) * P].bitcast(FP8X4),
                     lhsT_scale=w4_scales[:, t * P : (t + 1) * P],
                     rhs=z_codes[:].bitcast(FP8X4),
@@ -222,27 +231,100 @@ def tile_picked_zpt_tanh_po_kernel(
                     start=True,
                     stop=True,
                 )
-            res_bf16 = sbuf([P, HALF * PACK], BF16, "res_bf16_%d" % g)
-            src = bank[:].rearrange("p (t v) -> p v t", t=PACK)
-            dst = res_bf16[:].rearrange("p (v t) -> p v t", t=PACK)
-            if g == 0:
-                nc.scalar.copy(dst, src)
-            else:
-                nc.vector.tensor_copy(dst, src)
-            res = sbuf([P, PACK, HALF], F32, "out%d" % g)
-            rows = out_0.rearrange("(p t) v -> p t v", t=PACK)
-            step = PACK if g == 0 else 2
+
+        def round_out(c0, c1, copy):
+            w = c1 - c0
+            obf[c0] = sbuf([P, w * PACK], BF16, "out_bf16_%d" % c0)
+            copy(obf[c0][:].rearrange("p (v t) -> p v t", t=PACK), obank[c0][:, : PACK * w].rearrange("p (t v) -> p v t", t=PACK))
+
+        def store_values(c0, c1, step):
+            w = c1 - c0
+            vals = sbuf([P, PACK, w], F32, "out%d" % c0)
             for t0 in range(0, PACK, step):
-                nc.scalar.copy(
-                    res[:, t0 : t0 + step].rearrange("p t v -> p (t v)"), bank[:, t0 * HALF : (t0 + step) * HALF]
-                )
-                nc.scalar.dma_start(rows[:, t0 : t0 + step, cols], res[:, t0 : t0 + step])
-            out_codes = sbuf([P, HALF], U32, "out_codes%d" % g)
-            nc.vector.quantize_mx(out=out_codes[:].bitcast(FP8X4), scales=out_scales[:, cols], in_=res_bf16[:])
-            nc.sync.dma_start(
-                out_1[0].rearrange("p c r -> p (c r)").bitcast(I32)[:, cols], out_codes[:].bitcast(I32)
-            )
+                nc.scalar.copy(vals[:, t0 : t0 + step].rearrange("p t v -> p (t v)"), obank[c0][:, t0 * w : (t0 + step) * w])
+                nc.scalar.dma_start(rows[:, t0 : t0 + step, c0:c1], vals[:, t0 : t0 + step])
+
+        out_codes = sbuf([P, V], U32, "out_codes")
+
+        def quantise_out(c0, c1):
+            nc.vector.quantize_mx(out=out_codes[:, c0:c1].bitcast(FP8X4), scales=out_scales[:, c0:c1], in_=obf[c0][:])
+
+        nc.vector.tensor_copy(xq[0][:], xw[0][:].bitcast(U32).indirect(offs_t[:]))
+        round_s(0, 0, 0)
+        round_s(0, 0, 1)
+        nc.vector.tensor_copy(xq_scales[:], x_bytes[:].indirect(offs_t[:]))
+        quantise(0, 0, 0)
+        nc.vector.tensor_copy(xq[1][:], xw[1][:].bitcast(U32).indirect(offs_t[:]))
+        quantise(0, 0, 1)
+        round_v(0, 1, 0)
+        round_s(0, 1, 1)
+        quantise(0, 1, 0)
+        quantise(0, 1, 1)
+        for t in range(4):
+            drain(0, t)
+        round_v(1, 0, 0)
+        round_v(1, 0, 1)
+        quantise(1, 0, 0)
+        quantise(1, 0, 1)
+        centres((0,), "w2_raw0")
+        round_v(1, 1, 0)
+        round_s(1, 1, 1)
+        quantise(1, 1, 0, (0,))
+        quantise(1, 1, 0, (1,))
+        quantise(1, 1, 1)
+        centres((1, 2, 3), "bf_1_1_0")
+        for t in range(4):
+            drain(1, t)
+        round_s(2, 0, 0)
+        round_s(2, 0, 1)
+        keys(0)
+        turn(0, 4)
+        keys(1)
+        turn(1, 5)
+        squash((0, 1), "w3_raw0")
+        quantise(2, 0, 0)
+        round_v(2, 1, 0)
+        round_v(2, 1, 1)
+        leading(0, 6)
+        leading(1, 7)
+        quantise(2, 1, 0)
+        quantise(2, 0, 1, name="w3_raw1")
+        quantise(2, 1, 1)
+        keys(2, "bf_2_1_0")
+        turn(2, 4)
+        keys(3, "bf_2_0_1")
+        turn(3, 5)
+        shares(0)
+        shares(1)
+        drain(2, 0)
+        drain(2, 1)
+        squash((2,), "squashed2")
+        leading(2, 6)
+        drain(2, 2)
+        squash((3,), "squashed3")
+        leading(3, 7)
+        shares(2)
+        drain(2, 3)
+        shares(3)
+        values(0, 0, V)
+        values(1, 0, V)
+        values(2, 0, V)
+        nc.vector.tensor_copy(w4_dst[:, :32], w4_src[:, :32])
+        for m0 in range(32, P, 32):
+            nc.scalar.copy(w4_dst[:, m0 : m0 + 32], w4_src[:, m0 : m0 + 32])
+        values(3, 0, HALF)
+        values(3, HALF, V)
+        mix(0, HALF)
+        nc.vector.quantize_mx(out=w4_codes[:].bitcast(FP8X4), scales=w4_scales[:], in_=w4_bf16[:])
+        project(0, HALF, 4)
+        mix(HALF, V)
+        project(HALF, V, 5)
+        round_out(0, HALF, nc.scalar.copy)
+        store_values(0, HALF, 4)
+        quantise_out(0, HALF)
+        round_out(HALF, V, nc.vector.tensor_copy)
+        quantise_out(HALF, V)
+        store_values(HALF, V, 2)
+        nc.sync.dma_start(out_1[0].rearrange("p c r -> p (c r)").bitcast(I32), out_codes[:].bitcast(I32))
         for q in range(4):
-            nc.sync.dma_start(
-                out_2[0, 4 * q : 4 * q + 4, :].bitcast(I32), out_scales[32 * q : 32 * q + 4, :].bitcast(I32)
-            )
+            nc.sync.dma_start(out_2[0, 4 * q : 4 * q + 4, :].bitcast(I32), out_scales[32 * q : 32 * q + 4, :].bitcast(I32))

@@ -183,6 +183,19 @@ def tile_picked_zpt_tanh_po_kernel(
             for d in range(2):
                 nc.scalar.activation(share[t][:, d, :], lead[t][:, :V], SIGMOID, scale=2.0 - 4.0 * d, bias=4.0 * d - 2.0)
 
+        def squash_plain(t):
+            squashed[t] = sbuf([P, 2, V], F32, "squashed%d" % t)
+            nc.scalar.activation(squashed[t][:], diff[t][:], SIGMOID, scale=-2.0)
+
+        def leading_plain(t):
+            lead[t] = sbuf([P, V], F32, "lead%d" % t)
+            nc.vector.tensor_tensor(lead[t][:], squashed[t][:, 0, :], squashed[t][:, 1, :], SUB)
+
+        def shares_plain(t):
+            share[t] = sbuf([P, 2, V], F32, "share%d" % t)
+            for d in range(2):
+                nc.scalar.activation(share[t][:, d, :], lead[t][:], SIGMOID, scale=2.0 - 4.0 * d)
+
         w4_bf16 = sbuf([P, N * PACK], BF16, "w4_bf16")
         w4_codes = sbuf([P, N], U32, "w4_codes")
         w4_scales = sbuf([P, N], U8, "w4_scales")
@@ -291,25 +304,24 @@ def tile_picked_zpt_tanh_po_kernel(
         quantise(2, 0, 1, name="w3_raw1")
         quantise(2, 1, 1)
         keys(2, "bf_2_1_0")
-        turn(2, 4)
+
         keys(3, "bf_2_0_1")
-        turn(3, 5)
         shares(0)
         shares(1)
         drain(2, 0)
+        squash_plain(2)
         drain(2, 1)
-        squash((2,), "squashed2")
-        leading(2, 6)
-        drain(2, 2)
-        squash((3,), "squashed3")
-        leading(3, 7)
-        shares(2)
-        drain(2, 3)
-        shares(3)
+        squash_plain(3)
         values(0, 0, V)
+        leading_plain(2)
+        leading_plain(3)
+        drain(2, 2)
+        shares_plain(2)
+        drain(2, 3)
+        shares_plain(3)
         values(1, 0, V)
-        values(2, 0, V)
         nc.vector.tensor_copy(w4_dst[:, :32], w4_src[:, :32])
+        values(2, 0, V)
         for m0 in range(32, P, 32):
             nc.scalar.copy(w4_dst[:, m0 : m0 + 32], w4_src[:, m0 : m0 + 32])
         values(3, 0, HALF)

@@ -80,11 +80,13 @@ def tile_picked_zpt_tanh_po_kernel(
         xq = [sbuf([P, S], U32, "xq%d" % o) for o in range(PASSES)]
         xq_scales = sbuf([P, S], U8, "xq_scales")
 
+        LATE = ()
         codes, scales, rounded, banks, res = {}, {}, {}, {}, {}
         for m in range(3):
             for o in range(PASSES):
                 for r in range(2):
-                    rounded[(m, o, r)] = sbuf([P, 2 * P * PACK], BF16, "bf_%d_%d_%d" % (m, o, r))
+                    if (m, o, r) not in LATE:
+                        rounded[(m, o, r)] = sbuf([P, 2 * P * PACK], BF16, "bf_%d_%d_%d" % (m, o, r))
 
         def views(m, o, r):
             src = raw[(m, o)][:].rearrange("p j (u t i) -> p t u j i", t=PACK, i=4)[:, 2 * r : 2 * r + 2]
@@ -99,6 +101,17 @@ def tile_picked_zpt_tanh_po_kernel(
             dst, src = views(m, o, r)
             for t in ts:
                 nc.scalar.copy(dst[:, t], src[:, t])
+
+        def round_g(m, o, r):
+            dst, src = views(m, o, r)
+            for t in range(2):
+                nc.gpsimd.tensor_scalar(
+                    dst[:, t].rearrange("p u j i -> p u i j"), src[:, t].rearrange("p u j i -> p u i j"), 1.0, 0.0, MULT, ADD
+                )
+
+        def round_pair_s(m, o, r):
+            dst, src = views(m, o, r)
+            nc.scalar.copy(dst, src)
 
         def quantise(m, o, r, ts=(0, 1), name=None):
             a, b = ts[0], ts[-1] + 1
@@ -204,8 +217,8 @@ def tile_picked_zpt_tanh_po_kernel(
 
         terms = [sbuf([P, PACK, V], F32, "term%d" % d) for d in range(2)]
 
-        def values(t, c0, c1):
-            for d in range(2):
+        def values(t, c0, c1, ds=(0, 1)):
+            for d in ds:
                 nc.vector.tensor_tensor(
                     terms[d][:, t, c0:c1],
                     res[(2, t)][:].indirect(pos_t[d][:, c0 // 16 : c1 // 16]),
@@ -215,7 +228,7 @@ def tile_picked_zpt_tanh_po_kernel(
 
         out_scales = sbuf([P, V], U8, "out_scales")
         rows = out_0.rearrange("(p t) v -> p t v", t=PACK)
-        zq, obank, obf = {}, {}, {}
+        zq, obank, obf, ovals = {}, {}, {}, {}
 
         def mix(c0, c1):
             w = c1 - c0
@@ -228,34 +241,43 @@ def tile_picked_zpt_tanh_po_kernel(
             )
             zq[c0] = z
 
-        def project(c0, c1, n):
+        def project(c0, c1, n, again=None):
             w = c1 - c0
             z_codes = sbuf([P, w], U32, "z_codes%d" % c0)
             z_scales = sbuf([P, w], U8, "z_scales%d" % c0)
             nc.vector.quantize_mx(out=z_codes[:].bitcast(FP8X4), scales=z_scales[:], in_=zq[c0][:])
-            obank[c0] = bank(n)
-            for t in range(PACK):
-                nc.tensor.matmul_mx(
-                    out=obank[c0][:, t * w : (t + 1) * w],
-                    lhsT=w4_codes[:, t * P : (t + 1) * P].bitcast(FP8X4),
-                    lhsT_scale=w4_scales[:, t * P : (t + 1) * P],
-                    rhs=z_codes[:].bitcast(FP8X4),
-                    rhs_scale=z_scales[:],
-                    start=True,
-                    stop=True,
-                )
+            for key, spot in ((c0, n), (c0 + 1, again)):
+                if spot is None:
+                    obank[key] = obank[c0]
+                    continue
+                obank[key] = bank(spot)
+                for t in range(PACK):
+                    nc.tensor.matmul_mx(
+                        out=obank[key][:, t * w : (t + 1) * w],
+                        lhsT=w4_codes[:, t * P : (t + 1) * P].bitcast(FP8X4),
+                        lhsT_scale=w4_scales[:, t * P : (t + 1) * P],
+                        rhs=z_codes[:].bitcast(FP8X4),
+                        rhs_scale=z_scales[:],
+                        start=True,
+                        stop=True,
+                    )
 
         def round_out(c0, c1, copy):
             w = c1 - c0
             obf[c0] = sbuf([P, w * PACK], BF16, "out_bf16_%d" % c0)
             copy(obf[c0][:].rearrange("p (v t) -> p v t", t=PACK), obank[c0][:, : PACK * w].rearrange("p (t v) -> p v t", t=PACK))
 
-        def store_values(c0, c1, step):
+        def round_stored(c0, c1):
+            obf[c0] = sbuf([P, (c1 - c0) * PACK], BF16, "out_bf16_%d" % c0)
+            nc.vector.tensor_copy(obf[c0][:].rearrange("p (v t) -> p v t", t=PACK), ovals[c0][:].rearrange("p t v -> p v t"))
+
+        def store_values(c0, c1, step, queue):
             w = c1 - c0
             vals = sbuf([P, PACK, w], F32, "out%d" % c0)
+            ovals[c0] = vals
             for t0 in range(0, PACK, step):
-                nc.scalar.copy(vals[:, t0 : t0 + step].rearrange("p t v -> p (t v)"), obank[c0][:, t0 * w : (t0 + step) * w])
-                nc.scalar.dma_start(rows[:, t0 : t0 + step, c0:c1], vals[:, t0 : t0 + step])
+                nc.scalar.copy(vals[:, t0 : t0 + step].rearrange("p t v -> p (t v)"), obank[c0 + 1][:, t0 * w : (t0 + step) * w])
+                queue.dma_start(rows[:, t0 : t0 + step, c0:c1], vals[:, t0 : t0 + step])
 
         out_codes = sbuf([P, V], U32, "out_codes")
 
@@ -288,8 +310,8 @@ def tile_picked_zpt_tanh_po_kernel(
         centres((1, 2, 3), "bf_1_1_0")
         for t in range(4):
             drain(1, t)
-        round_s(2, 0, 0)
-        round_s(2, 0, 1)
+        round_pair_s(2, 0, 0)
+        round_pair_s(2, 0, 1)
         keys(0)
         turn(0, 4)
         keys(1)
@@ -320,23 +342,26 @@ def tile_picked_zpt_tanh_po_kernel(
         drain(2, 3)
         shares_plain(3)
         values(1, 0, V)
-        nc.vector.tensor_copy(w4_dst[:, :32], w4_src[:, :32])
+        nc.vector.tensor_copy(
+            w4_dst[:, :32].rearrange("p m j (a b) -> p a m j b", a=2), w4_src[:, :32].rearrange("p m j (a b) -> p a m j b", a=2)
+        )
         values(2, 0, V)
-        for m0 in range(32, P, 32):
-            nc.scalar.copy(w4_dst[:, m0 : m0 + 32], w4_src[:, m0 : m0 + 32])
-        values(3, 0, HALF)
-        values(3, HALF, V)
+        nc.scalar.copy(w4_dst[:, 32:], w4_src[:, 32:])
+        values(3, 0, V, (0,))
+        values(3, 0, HALF, (1,))
+        values(3, HALF, V, (1,))
         mix(0, HALF)
         nc.vector.quantize_mx(out=w4_codes[:].bitcast(FP8X4), scales=w4_scales[:], in_=w4_bf16[:])
         project(0, HALF, 4)
         mix(HALF, V)
-        project(HALF, V, 5)
-        round_out(0, HALF, nc.scalar.copy)
-        store_values(0, HALF, 4)
-        quantise_out(0, HALF)
+        project(HALF, V, 5, 6)
+        store_values(0, HALF, 4, nc.sync)
         round_out(HALF, V, nc.vector.tensor_copy)
+        round_stored(0, HALF)
         quantise_out(HALF, V)
-        store_values(HALF, V, 2)
+        quantise_out(0, HALF)
+        store_values(HALF, V, 2, nc.scalar)
         nc.sync.dma_start(out_1[0].rearrange("p c r -> p (c r)").bitcast(I32), out_codes[:].bitcast(I32))
         for q in range(4):
-            nc.sync.dma_start(out_2[0, 4 * q : 4 * q + 4, :].bitcast(I32), out_scales[32 * q : 32 * q + 4, :].bitcast(I32))
+            queue = nc.sync if q < 2 else nc.scalar
+            queue.dma_start(out_2[0, 4 * q : 4 * q + 4, :].bitcast(I32), out_scales[32 * q : 32 * q + 4, :].bitcast(I32))

@@ -212,8 +212,8 @@ def tile_picked_zpt_tanh_po_kernel(
         w4_bf16 = sbuf([P, N * PACK], BF16, "w4_bf16")
         w4_codes = sbuf([P, N], U32, "w4_codes")
         w4_scales = sbuf([P, N], U8, "w4_scales")
-        w4_dst = w4_bf16[:].rearrange("p (t m j) -> p m j t", t=PACK, j=PACK)
-        w4_src = w4_raw[:].rearrange("p j (m t) -> p m j t", t=PACK)
+        w4_dst = w4_bf16[:].rearrange("p (a b m j) -> p a m j b", a=2, b=2, j=PACK)
+        w4_src = w4_raw[:].rearrange("p j (m a b) -> p a m j b", a=2, b=2)
 
         terms = [sbuf([P, PACK, V], F32, "term%d" % d) for d in range(2)]
 
@@ -269,7 +269,9 @@ def tile_picked_zpt_tanh_po_kernel(
 
         def round_stored(c0, c1):
             obf[c0] = sbuf([P, (c1 - c0) * PACK], BF16, "out_bf16_%d" % c0)
-            nc.vector.tensor_copy(obf[c0][:].rearrange("p (v t) -> p v t", t=PACK), ovals[c0][:].rearrange("p t v -> p v t"))
+            nc.vector.tensor_copy(
+                obf[c0][:].rearrange("p (c i t) -> p c t i", i=4, t=PACK), ovals[c0][:].rearrange("p t (c i) -> p c t i", i=4)
+            )
 
         def store_values(c0, c1, step, queue):
             w = c1 - c0
@@ -342,11 +344,9 @@ def tile_picked_zpt_tanh_po_kernel(
         drain(2, 3)
         shares_plain(3)
         values(1, 0, V)
-        nc.vector.tensor_copy(
-            w4_dst[:, :32].rearrange("p m j (a b) -> p a m j b", a=2), w4_src[:, :32].rearrange("p m j (a b) -> p a m j b", a=2)
-        )
+        nc.vector.tensor_copy(w4_dst[:, :, :32], w4_src[:, :, :32])
         values(2, 0, V)
-        nc.scalar.copy(w4_dst[:, 32:], w4_src[:, 32:])
+        nc.scalar.copy(w4_dst[:, :, 32:], w4_src[:, :, 32:])
         values(3, 0, V, (0,))
         values(3, 0, HALF, (1,))
         values(3, HALF, V, (1,))

@@ -20,9 +20,14 @@ MULT = mybir.AluOpType.mult
 
 P = 128
 PACK = 4
+RUN = 4
 K_PASS = P * PACK
 PASSES = K // K_PASS
 HALF = V // 2
+Y, E, HID = 0, 1, 2
+FIRST, LAST = 0, 1
+LOW, HIGH = 0, 1
+W4_ON_VECTOR = 16
 
 
 def tile_picked_zpt_tanh_po_kernel(
@@ -36,6 +41,15 @@ def tile_picked_zpt_tanh_po_kernel(
         def sbuf(shape, dtype, name):
             return keep.tile(shape, dtype, name=name, align_bytes=64)
 
+        def bank(n):
+            return psum.tile([P, S], F32, name="bank%d" % n)
+
+        def raw_name(m, o):
+            return "w%d_raw%d" % (m + 1, o)
+
+        def rounded_name(m, o, pair):
+            return "bf_%d_%d_%d" % (m, o, pair)
+
         def load_list(src, name):
             lst = sbuf(list(src.shape), U16, name)
             nc.sync.dma_start(lst[:], src)
@@ -46,91 +60,64 @@ def tile_picked_zpt_tanh_po_kernel(
             nc.sync.dma_start(words[:], x_words[o].rearrange("p c r -> p (c r)").bitcast(I32))
             return words
 
-        def load_pass(w, o, name):
-            raw = sbuf([P, PACK, N], F32, name)
-            nc.sync.dma_start(raw[:], w[o * K_PASS : (o + 1) * K_PASS, :].rearrange("(p j) n -> p j n", j=PACK))
-            return raw
+        raw = {}
+
+        def load_pass(w, m, o):
+            raw[(m, o)] = sbuf([P, PACK, N], F32, raw_name(m, o))
+            rows = w[o * K_PASS : (o + 1) * K_PASS, :]
+            nc.sync.dma_start(raw[(m, o)][:], rows.rearrange("(p j) n -> p j n", j=PACK))
 
         x_bytes = sbuf([P, T], U8, "x_bytes")
         nc.vector.memset(x_bytes[:].bitcast(I32), 0)
         offs_t = load_list(offs, "offs")
-        xw = [load_words(0)]
-        raw = {(0, 0): load_pass(w1, 0, "w1_raw0")}
+        words = [load_words(FIRST)]
+        load_pass(w1, Y, FIRST)
         for q in range(4):
             nc.sync.dma_start(
                 x_bytes[32 * q : 32 * q + 4 * PASSES, :].bitcast(I32),
                 x_scales[:, 4 * q : 4 * q + 4, :].bitcast(I32),
             )
-        xw.append(load_words(1))
-        raw[(0, 1)] = load_pass(w1, 1, "w1_raw1")
+        words.append(load_words(LAST))
+        load_pass(w1, Y, LAST)
         cen_t = load_list(cen, "cen")
-        raw[(1, 0)] = load_pass(w2, 0, "w2_raw0")
-        raw[(1, 1)] = load_pass(w2, 1, "w2_raw1")
+        load_pass(w2, E, FIRST)
+        load_pass(w2, E, LAST)
         pos_t = [load_list(pos1, "pos1"), load_list(pos2, "pos2")]
-        raw[(2, 0)] = load_pass(w3, 0, "w3_raw0")
-        raw[(2, 1)] = load_pass(w3, 1, "w3_raw1")
+        load_pass(w3, HID, FIRST)
+        load_pass(w3, HID, LAST)
         w4_raw = sbuf([P, PACK, N], F32, "w4_raw")
-        w4_rows = w4.rearrange("(u t i) n -> t u i n", t=PACK, i=4)
+        w4_rows = w4.rearrange("(u t r) n -> t u r n", t=PACK, r=RUN)
         for t in range(PACK):
             nc.sync.dma_start(w4_raw[:, t, :], w4_rows[t])
 
         warm = sbuf([P, 1], F32, "warm")
-        nc.scalar.activation(warm[:], raw[(0, 0)][:, 0, 0:1], SIGMOID)
+        nc.scalar.activation(warm[:], raw[(Y, FIRST)][:, 0, 0:1], SIGMOID)
 
         xq = [sbuf([P, S], U32, "xq%d" % o) for o in range(PASSES)]
         xq_scales = sbuf([P, S], U8, "xq_scales")
+        rounded = {
+            (m, o, pair): sbuf([P, 2 * P * PACK], BF16, rounded_name(m, o, pair))
+            for m in (Y, E, HID)
+            for o in (FIRST, LAST)
+            for pair in (LOW, HIGH)
+        }
+        codes, scales, banks, result = {}, {}, {}, {}
 
-        LATE = ()
-        codes, scales, rounded, banks, res = {}, {}, {}, {}, {}
-        for m in range(3):
-            for o in range(PASSES):
-                for r in range(2):
-                    if (m, o, r) not in LATE:
-                        rounded[(m, o, r)] = sbuf([P, 2 * P * PACK], BF16, "bf_%d_%d_%d" % (m, o, r))
-
-        def views(m, o, r):
-            src = raw[(m, o)][:].rearrange("p j (u t i) -> p t u j i", t=PACK, i=4)[:, 2 * r : 2 * r + 2]
-            dst = rounded[(m, o, r)][:].rearrange("p (t u i j) -> p t u j i", t=2, i=4, j=PACK)
+        def rounding_views(m, o, pair):
+            src = raw[(m, o)][:].rearrange("p j (u t r) -> p t u j r", t=PACK, r=RUN)[:, 2 * pair : 2 * pair + 2]
+            dst = rounded[(m, o, pair)][:].rearrange("p (t u r j) -> p t u j r", t=2, r=RUN, j=PACK)
             return dst, src
 
-        def round_v(m, o, r, ts=(0, 1)):
-            dst, src = views(m, o, r)
-            nc.vector.tensor_copy(dst[:, ts[0] : ts[-1] + 1], src[:, ts[0] : ts[-1] + 1])
+        def round_pair(copy, m, o, pair):
+            copy(*rounding_views(m, o, pair))
 
-        def round_s(m, o, r, ts=(0, 1)):
-            dst, src = views(m, o, r)
-            for t in ts:
+        def round_tiles_on_scalar(m, o, pair):
+            dst, src = rounding_views(m, o, pair)
+            for t in range(2):
                 nc.scalar.copy(dst[:, t], src[:, t])
 
-        def round_g(m, o, r):
-            dst, src = views(m, o, r)
-            for t in range(2):
-                nc.gpsimd.tensor_scalar(
-                    dst[:, t].rearrange("p u j i -> p u i j"), src[:, t].rearrange("p u j i -> p u i j"), 1.0, 0.0, MULT, ADD
-                )
-
-        def round_pair_s(m, o, r):
-            dst, src = views(m, o, r)
-            nc.scalar.copy(dst, src)
-
-        def quantise(m, o, r, ts=(0, 1), name=None):
-            a, b = ts[0], ts[-1] + 1
-            if a == 0:
-                codes[(m, o, r)] = sbuf([P, 2 * P], U32, name or "codes_%d_%d_%d" % (m, o, r))
-                scales[(m, o, r)] = sbuf([P, 2 * P], U8, "scales_%d_%d_%d" % (m, o, r))
-            nc.vector.quantize_mx(
-                out=codes[(m, o, r)][:, a * P : b * P].bitcast(FP8X4),
-                scales=scales[(m, o, r)][:, a * P : b * P],
-                in_=rounded[(m, o, r)][:, a * P * PACK : b * P * PACK],
-            )
-            for t in range(2 * r + a, 2 * r + b):
-                multiply(m, o, t)
-
-        def bank(n):
-            return psum.tile([P, S], F32, name="bank%d" % n)
-
         def multiply(m, o, t):
-            if o == 0:
+            if o == FIRST:
                 banks[(m, t)] = bank(PACK * (m % 2) + t)
             cols = slice(t % 2 * P, (t % 2 + 1) * P)
             nc.tensor.matmul_mx(
@@ -139,75 +126,87 @@ def tile_picked_zpt_tanh_po_kernel(
                 lhsT_scale=scales[(m, o, t // 2)][:, cols],
                 rhs=xq[o][:].bitcast(FP8X4),
                 rhs_scale=xq_scales[4 * o : P, :],
-                start=(o == 0),
-                stop=(o == PASSES - 1),
+                start=(o == FIRST),
+                stop=(o == LAST),
             )
 
-        def drain(m, t, name=None):
-            res[(m, t)] = sbuf([P, S], F32, name or "res_%d_%d" % (m, t))
-            nc.scalar.copy(res[(m, t)][:], banks[(m, t)][:])
+        def quantise_and_multiply(m, o, pair, tiles_a_call=2, behind=None):
+            key = (m, o, pair)
+            codes[key] = sbuf([P, 2 * P], U32, behind or "codes_%d_%d_%d" % key)
+            scales[key] = sbuf([P, 2 * P], U8, "scales_%d_%d_%d" % key)
+            for a in range(0, 2, tiles_a_call):
+                b = a + tiles_a_call
+                nc.vector.quantize_mx(
+                    out=codes[key][:, a * P : b * P].bitcast(FP8X4),
+                    scales=scales[key][:, a * P : b * P],
+                    in_=rounded[key][:, a * P * PACK : b * P * PACK],
+                )
+                for t in range(2 * pair + a, 2 * pair + b):
+                    multiply(m, o, t)
 
-        yc, diff, squashed, lead, share = {}, {}, {}, {}, {}
+        def drain(m, t):
+            result[(m, t)] = sbuf([P, S], F32, "res_%d_%d" % (m, t))
+            nc.scalar.copy(result[(m, t)][:], banks[(m, t)][:])
 
-        def centres(ts, name):
-            picked = sbuf([P, len(ts), V], F32, name)
-            for n, t in enumerate(ts):
-                yc[t] = picked[:, n, :]
-                nc.vector.tensor_copy(yc[t], res[(0, t)][:].indirect(cen_t[:]))
+        centre, diff, turned, squashed, summed, lead, share = {}, {}, {}, {}, {}, {}, {}
 
-        def keys(t, name=None):
-            diff[t] = sbuf([P, 2, V], F32, name or "diff%d" % t)
+        def gather_centres(tiles, behind):
+            picked = sbuf([P, len(tiles), V], F32, behind)
+            for n, t in enumerate(tiles):
+                centre[t] = picked[:, n, :]
+                nc.vector.tensor_copy(centre[t], result[(Y, t)][:].indirect(cen_t[:]))
+
+        def gather_keys(t, behind=None):
+            diff[t] = sbuf([P, 2, V], F32, behind or "diff%d" % t)
             for d in range(2):
-                nc.vector.tensor_tensor(diff[t][:, d, :], res[(1, t)][:].indirect(pos_t[d][:]), yc[t], SUB)
+                nc.vector.tensor_tensor(diff[t][:, d, :], result[(E, t)][:].indirect(pos_t[d][:]), centre[t], SUB)
 
         ident = sbuf([P, P], F32, "ident")
         make_identity(nc, ident[:])
-        turned = {}
 
         def turn(t, n):
             turned[t] = bank(n)
             for d in range(2):
-                for g in range(2):
-                    c = (2 * d + g) * P
-                    nc.tensor.transpose(turned[t][:, c : c + P], diff[t][:, d, g * P : (g + 1) * P], ident[:])
+                for c in range(0, V, P):
+                    nc.tensor.transpose(turned[t][:, d * V + c : d * V + c + P], diff[t][:, d, c : c + P], ident[:])
 
-        def squash(ts, name):
-            both = sbuf([P, len(ts), 2, V], F32, name)
-            for n, t in enumerate(ts):
+        def squash_turned(tiles, behind):
+            both = sbuf([P, len(tiles), 2, V], F32, behind)
+            for n, t in enumerate(tiles):
                 squashed[t] = both[:, n]
-                for d in range(2):
-                    nc.scalar.activation(squashed[t][:, d, :], turned[t][:, d * V : (d + 1) * V], SIGMOID, scale=4.0 * d - 2.0)
+                for d, sign in enumerate((-1.0, 1.0)):
+                    nc.scalar.activation(squashed[t][:, d, :], turned[t][:, d * V : (d + 1) * V], SIGMOID, scale=2.0 * sign)
 
-        def leading(t, n):
-            lead[t] = bank(n)
-            for g in range(2):
+        def add_and_turn_back(t, n):
+            summed[t] = bank(n)
+            for c in range(0, V, P):
                 for d in range(2):
                     nc.tensor.matmul(
-                        lead[t][:, g * P : (g + 1) * P],
-                        squashed[t][:, d, g * P : (g + 1) * P],
+                        summed[t][:, c : c + P],
+                        squashed[t][:, d, c : c + P],
                         ident[:],
                         start=(d == 0),
                         stop=(d == 1),
                         is_transpose=True,
                     )
 
-        def shares(t, name=None):
-            share[t] = sbuf([P, 2, V], F32, name or "share%d" % t)
-            for d in range(2):
-                nc.scalar.activation(share[t][:, d, :], lead[t][:, :V], SIGMOID, scale=2.0 - 4.0 * d, bias=4.0 * d - 2.0)
+        def shares_from_sum(t):
+            share[t] = sbuf([P, 2, V], F32, "share%d" % t)
+            for d, sign in enumerate((1.0, -1.0)):
+                nc.scalar.activation(share[t][:, d, :], summed[t][:, :V], SIGMOID, scale=2.0 * sign, bias=-2.0 * sign)
 
-        def squash_plain(t):
+        def squash(t):
             squashed[t] = sbuf([P, 2, V], F32, "squashed%d" % t)
             nc.scalar.activation(squashed[t][:], diff[t][:], SIGMOID, scale=-2.0)
 
-        def leading_plain(t):
+        def subtract(t):
             lead[t] = sbuf([P, V], F32, "lead%d" % t)
             nc.vector.tensor_tensor(lead[t][:], squashed[t][:, 0, :], squashed[t][:, 1, :], SUB)
 
-        def shares_plain(t):
+        def shares_from_difference(t):
             share[t] = sbuf([P, 2, V], F32, "share%d" % t)
-            for d in range(2):
-                nc.scalar.activation(share[t][:, d, :], lead[t][:], SIGMOID, scale=2.0 - 4.0 * d)
+            for d, sign in enumerate((1.0, -1.0)):
+                nc.scalar.activation(share[t][:, d, :], lead[t][:], SIGMOID, scale=2.0 * sign)
 
         w4_bf16 = sbuf([P, N * PACK], BF16, "w4_bf16")
         w4_codes = sbuf([P, N], U32, "w4_codes")
@@ -217,150 +216,150 @@ def tile_picked_zpt_tanh_po_kernel(
 
         terms = [sbuf([P, PACK, V], F32, "term%d" % d) for d in range(2)]
 
-        def values(t, c0, c1, ds=(0, 1)):
-            for d in ds:
-                nc.vector.tensor_tensor(
-                    terms[d][:, t, c0:c1],
-                    res[(2, t)][:].indirect(pos_t[d][:, c0 // 16 : c1 // 16]),
-                    share[t][:, d, c0:c1],
-                    MULT,
-                )
+        def gather_values(t, d, c0=0, c1=V):
+            nc.vector.tensor_tensor(
+                terms[d][:, t, c0:c1],
+                result[(HID, t)][:].indirect(pos_t[d][:, c0 // 16 : c1 // 16]),
+                share[t][:, d, c0:c1],
+                MULT,
+            )
 
         out_scales = sbuf([P, V], U8, "out_scales")
-        rows = out_0.rearrange("(p t) v -> p t v", t=PACK)
-        zq, obank, obf, ovals = {}, {}, {}, {}
-
-        def mix(c0, c1):
-            w = c1 - c0
-            z = sbuf([P, w * PACK], BF16, "z%d" % c0)
-            nc.vector.tensor_tensor(
-                z[:].rearrange("p (c i t) -> p c t i", i=4, t=PACK),
-                terms[0][:, :, c0:c1].rearrange("p t (c i) -> p c t i", i=4),
-                terms[1][:, :, c0:c1].rearrange("p t (c i) -> p c t i", i=4),
-                ADD,
-            )
-            zq[c0] = z
-
-        def project(c0, c1, n, again=None):
-            w = c1 - c0
-            z_codes = sbuf([P, w], U32, "z_codes%d" % c0)
-            z_scales = sbuf([P, w], U8, "z_scales%d" % c0)
-            nc.vector.quantize_mx(out=z_codes[:].bitcast(FP8X4), scales=z_scales[:], in_=zq[c0][:])
-            for key, spot in ((c0, n), (c0 + 1, again)):
-                if spot is None:
-                    obank[key] = obank[c0]
-                    continue
-                obank[key] = bank(spot)
-                for t in range(PACK):
-                    nc.tensor.matmul_mx(
-                        out=obank[key][:, t * w : (t + 1) * w],
-                        lhsT=w4_codes[:, t * P : (t + 1) * P].bitcast(FP8X4),
-                        lhsT_scale=w4_scales[:, t * P : (t + 1) * P],
-                        rhs=z_codes[:].bitcast(FP8X4),
-                        rhs_scale=z_scales[:],
-                        start=True,
-                        stop=True,
-                    )
-
-        def round_out(c0, c1, copy):
-            w = c1 - c0
-            obf[c0] = sbuf([P, w * PACK], BF16, "out_bf16_%d" % c0)
-            copy(obf[c0][:].rearrange("p (v t) -> p v t", t=PACK), obank[c0][:, : PACK * w].rearrange("p (t v) -> p v t", t=PACK))
-
-        def round_stored(c0, c1):
-            obf[c0] = sbuf([P, (c1 - c0) * PACK], BF16, "out_bf16_%d" % c0)
-            nc.vector.tensor_copy(
-                obf[c0][:].rearrange("p (c i t) -> p c t i", i=4, t=PACK), ovals[c0][:].rearrange("p t (c i) -> p c t i", i=4)
-            )
-
-        def store_values(c0, c1, step, queue):
-            w = c1 - c0
-            vals = sbuf([P, PACK, w], F32, "out%d" % c0)
-            ovals[c0] = vals
-            for t0 in range(0, PACK, step):
-                nc.scalar.copy(vals[:, t0 : t0 + step].rearrange("p t v -> p (t v)"), obank[c0 + 1][:, t0 * w : (t0 + step) * w])
-                queue.dma_start(rows[:, t0 : t0 + step, c0:c1], vals[:, t0 : t0 + step])
-
         out_codes = sbuf([P, V], U32, "out_codes")
 
-        def quantise_out(c0, c1):
-            nc.vector.quantize_mx(out=out_codes[:, c0:c1].bitcast(FP8X4), scales=out_scales[:, c0:c1], in_=obf[c0][:])
-
-        nc.vector.tensor_copy(xq[0][:], xw[0][:].bitcast(U32).indirect(offs_t[:]))
-        round_s(0, 0, 0)
-        round_s(0, 0, 1)
+        nc.vector.tensor_copy(xq[FIRST][:], words[FIRST][:].bitcast(U32).indirect(offs_t[:]))
+        round_tiles_on_scalar(Y, FIRST, LOW)
+        round_tiles_on_scalar(Y, FIRST, HIGH)
         nc.vector.tensor_copy(xq_scales[:], x_bytes[:].indirect(offs_t[:]))
-        quantise(0, 0, 0)
-        nc.vector.tensor_copy(xq[1][:], xw[1][:].bitcast(U32).indirect(offs_t[:]))
-        quantise(0, 0, 1)
-        round_v(0, 1, 0)
-        round_s(0, 1, 1)
-        quantise(0, 1, 0)
-        quantise(0, 1, 1)
-        for t in range(4):
-            drain(0, t)
-        round_v(1, 0, 0)
-        round_v(1, 0, 1)
-        quantise(1, 0, 0)
-        quantise(1, 0, 1)
-        centres((0,), "w2_raw0")
-        round_v(1, 1, 0)
-        round_s(1, 1, 1)
-        quantise(1, 1, 0, (0,))
-        quantise(1, 1, 0, (1,))
-        quantise(1, 1, 1)
-        centres((1, 2, 3), "bf_1_1_0")
-        for t in range(4):
-            drain(1, t)
-        round_pair_s(2, 0, 0)
-        round_pair_s(2, 0, 1)
-        keys(0)
-        turn(0, 4)
-        keys(1)
-        turn(1, 5)
-        squash((0, 1), "w3_raw0")
-        quantise(2, 0, 0)
-        round_v(2, 1, 0)
-        round_v(2, 1, 1)
-        leading(0, 6)
-        leading(1, 7)
-        quantise(2, 1, 0)
-        quantise(2, 0, 1, name="w3_raw1")
-        quantise(2, 1, 1)
-        keys(2, "bf_2_1_0")
+        quantise_and_multiply(Y, FIRST, LOW)
+        nc.vector.tensor_copy(xq[LAST][:], words[LAST][:].bitcast(U32).indirect(offs_t[:]))
+        quantise_and_multiply(Y, FIRST, HIGH)
+        round_pair(nc.vector.tensor_copy, Y, LAST, LOW)
+        round_tiles_on_scalar(Y, LAST, HIGH)
+        for pair in (LOW, HIGH):
+            quantise_and_multiply(Y, LAST, pair)
+        for t in range(PACK):
+            drain(Y, t)
 
-        keys(3, "bf_2_0_1")
-        shares(0)
-        shares(1)
-        drain(2, 0)
-        squash_plain(2)
-        drain(2, 1)
-        squash_plain(3)
-        values(0, 0, V)
-        leading_plain(2)
-        leading_plain(3)
-        drain(2, 2)
-        shares_plain(2)
-        drain(2, 3)
-        shares_plain(3)
-        values(1, 0, V)
-        nc.vector.tensor_copy(w4_dst[:, :, :32], w4_src[:, :, :32])
-        values(2, 0, V)
-        nc.scalar.copy(w4_dst[:, :, 32:], w4_src[:, :, 32:])
-        values(3, 0, V, (0,))
-        values(3, 0, HALF, (1,))
-        values(3, HALF, V, (1,))
-        mix(0, HALF)
-        nc.vector.quantize_mx(out=w4_codes[:].bitcast(FP8X4), scales=w4_scales[:], in_=w4_bf16[:])
-        project(0, HALF, 4)
-        mix(HALF, V)
-        project(HALF, V, 5, 6)
-        store_values(0, HALF, 4, nc.sync)
-        round_out(HALF, V, nc.vector.tensor_copy)
-        round_stored(0, HALF)
-        quantise_out(HALF, V)
-        quantise_out(0, HALF)
-        store_values(HALF, V, 2, nc.scalar)
+        for pair in (LOW, HIGH):
+            round_pair(nc.vector.tensor_copy, E, FIRST, pair)
+        for pair in (LOW, HIGH):
+            quantise_and_multiply(E, FIRST, pair)
+        gather_centres((0,), behind=raw_name(E, FIRST))
+        round_pair(nc.vector.tensor_copy, E, LAST, LOW)
+        round_tiles_on_scalar(E, LAST, HIGH)
+        quantise_and_multiply(E, LAST, LOW, tiles_a_call=1)
+        quantise_and_multiply(E, LAST, HIGH)
+        gather_centres((1, 2, 3), behind=rounded_name(E, LAST, LOW))
+        for t in range(PACK):
+            drain(E, t)
+
+        for pair in (LOW, HIGH):
+            round_pair(nc.scalar.copy, HID, FIRST, pair)
+        for t in (0, 1):
+            gather_keys(t)
+            turn(t, 4 + t)
+        squash_turned((0, 1), behind=raw_name(HID, FIRST))
+        quantise_and_multiply(HID, FIRST, LOW)
+        for pair in (LOW, HIGH):
+            round_pair(nc.vector.tensor_copy, HID, LAST, pair)
+        for t in (0, 1):
+            add_and_turn_back(t, 6 + t)
+        quantise_and_multiply(HID, LAST, LOW)
+        quantise_and_multiply(HID, FIRST, HIGH, behind=raw_name(HID, LAST))
+        quantise_and_multiply(HID, LAST, HIGH)
+        gather_keys(2, behind=rounded_name(HID, LAST, LOW))
+        gather_keys(3, behind=rounded_name(HID, FIRST, HIGH))
+
+        for t in (0, 1):
+            shares_from_sum(t)
+        for t in (0, 1):
+            drain(HID, t)
+            squash(t + 2)
+        for d in range(2):
+            gather_values(0, d)
+        for t in (2, 3):
+            subtract(t)
+        for t in (2, 3):
+            drain(HID, t)
+            shares_from_difference(t)
+        for d in range(2):
+            gather_values(1, d)
+        nc.vector.tensor_copy(w4_dst[:, :, :W4_ON_VECTOR], w4_src[:, :, :W4_ON_VECTOR])
+        for d in range(2):
+            gather_values(2, d)
+        for a in range(2):
+            nc.scalar.copy(w4_dst[:, a, W4_ON_VECTOR:], w4_src[:, a, W4_ON_VECTOR:])
+        gather_values(3, 0)
+        for c0 in (0, HALF):
+            gather_values(3, 1, c0, c0 + HALF)
+
+        z_bf16 = []
+        for c0 in (0, HALF):
+            z = sbuf([P, HALF * PACK], BF16, "z%d" % c0)
+            nc.vector.tensor_tensor(
+                z[:].rearrange("p (c r t) -> p c t r", r=RUN, t=PACK),
+                terms[0][:, :, c0 : c0 + HALF].rearrange("p t (c r) -> p c t r", r=RUN),
+                terms[1][:, :, c0 : c0 + HALF].rearrange("p t (c r) -> p c t r", r=RUN),
+                ADD,
+            )
+            z_bf16.append(z)
+        z_codes, z_scales = [], []
+        for g in range(2):
+            z_codes.append(sbuf([P, HALF], U32, "z_codes%d" % (g * HALF)))
+            z_scales.append(sbuf([P, HALF], U8, "z_scales%d" % (g * HALF)))
+            nc.vector.quantize_mx(out=z_codes[g][:].bitcast(FP8X4), scales=z_scales[g][:], in_=z_bf16[g][:])
+
+        first_half, second_for_codes, second_for_values = bank(4), bank(5), bank(6)
+
+        def project(target, g, t):
+            nc.tensor.matmul_mx(
+                out=target[:, t * HALF : (t + 1) * HALF],
+                lhsT=w4_codes[:, t * P : (t + 1) * P].bitcast(FP8X4),
+                lhsT_scale=w4_scales[:, t * P : (t + 1) * P],
+                rhs=z_codes[g][:].bitcast(FP8X4),
+                rhs_scale=z_scales[g][:],
+                start=True,
+                stop=True,
+            )
+
+        for t in range(PACK):
+            nc.vector.quantize_mx(
+                out=w4_codes[:, t * P : (t + 1) * P].bitcast(FP8X4),
+                scales=w4_scales[:, t * P : (t + 1) * P],
+                in_=w4_bf16[:, t * P * PACK : (t + 1) * P * PACK],
+            )
+            project(first_half, 0, t)
+        for target in (second_for_codes, second_for_values):
+            for t in range(PACK):
+                project(target, 1, t)
+
+        out_rows = out_0.rearrange("(p t) v -> p t v", t=PACK)
+
+        def store_values(source, c0, tiles_a_store, queue):
+            values = sbuf([P, PACK, HALF], F32, "out%d" % c0)
+            for t0 in range(0, PACK, tiles_a_store):
+                t1 = t0 + tiles_a_store
+                nc.scalar.copy(values[:, t0:t1].rearrange("p t v -> p (t v)"), source[:, t0 * HALF : t1 * HALF])
+                queue.dma_start(out_rows[:, t0:t1, c0 : c0 + HALF], values[:, t0:t1])
+            return values
+
+        first_values = store_values(first_half, 0, PACK, nc.sync)
+        second_bf16 = sbuf([P, HALF * PACK], BF16, "out_bf16_%d" % HALF)
+        nc.vector.tensor_copy(
+            second_bf16[:].rearrange("p (v t) -> p v t", t=PACK),
+            second_for_codes[:].rearrange("p (t v) -> p v t", t=PACK),
+        )
+        first_bf16 = sbuf([P, HALF * PACK], BF16, "out_bf16_0")
+        nc.vector.tensor_copy(
+            first_bf16[:].rearrange("p (c r t) -> p c t r", r=RUN, t=PACK),
+            first_values[:].rearrange("p t (c r) -> p c t r", r=RUN),
+        )
+        for c0, source in ((HALF, second_bf16), (0, first_bf16)):
+            nc.vector.quantize_mx(
+                out=out_codes[:, c0 : c0 + HALF].bitcast(FP8X4), scales=out_scales[:, c0 : c0 + HALF], in_=source[:]
+            )
+        store_values(second_for_values, HALF, 2, nc.scalar)
         nc.sync.dma_start(out_1[0].rearrange("p c r -> p (c r)").bitcast(I32), out_codes[:].bitcast(I32))
         for q in range(4):
             queue = nc.sync if q < 2 else nc.scalar

@@ -26,8 +26,9 @@ PASSES = K // K_PASS
 HALF = V // 2
 Y, E, HID = 0, 1, 2
 FIRST, LAST = 0, 1
-LOW, HIGH = 0, 1
+LOW, HIGH = (0, 2), (2, 4)
 W4_ON_VECTOR = 16
+T0, T1, T2, T3 = (0, 1), (1, 2), (2, 3), (3, 4)
 
 
 def tile_picked_zpt_tanh_po_kernel(
@@ -47,8 +48,11 @@ def tile_picked_zpt_tanh_po_kernel(
         def raw_name(m, o):
             return "w%d_raw%d" % (m + 1, o)
 
-        def rounded_name(m, o, pair):
-            return "bf_%d_%d_%d" % (m, o, pair)
+        def rounded_name(m, o, group):
+            return "bf_%d_%d_%d" % (m, o, group[0])
+
+        def codes_name(m, o, group):
+            return "codes_%d_%d_%d" % (m, o, group[0])
 
         def load_list(src, name):
             lst = sbuf(list(src.shape), U16, name)
@@ -85,67 +89,53 @@ def tile_picked_zpt_tanh_po_kernel(
         pos_t = [load_list(pos1, "pos1"), load_list(pos2, "pos2")]
         load_pass(w3, HID, FIRST)
         load_pass(w3, HID, LAST)
-        w4_raw = sbuf([P, PACK, N], F32, "w4_raw")
         w4_rows = w4.rearrange("(u t r) n -> t u r n", t=PACK, r=RUN)
-        for t in range(PACK):
-            nc.sync.dma_start(w4_raw[:, t, :], w4_rows[t])
+        w4_raw = []
+        for side in range(2):
+            w4_raw.append(sbuf([P, PACK, N // 2], F32, "w4_raw%d" % side))
+            for t in range(PACK):
+                nc.sync.dma_start(w4_raw[side][:, t, :], w4_rows[t][:, :, side * N // 2 : (side + 1) * N // 2])
 
         warm = sbuf([P, 1], F32, "warm")
         nc.scalar.activation(warm[:], raw[(Y, FIRST)][:, 0, 0:1], SIGMOID)
 
         xq = [sbuf([P, S], U32, "xq%d" % o) for o in range(PASSES)]
         xq_scales = sbuf([P, S], U8, "xq_scales")
-        rounded = {
-            (m, o, pair): sbuf([P, 2 * P * PACK], BF16, rounded_name(m, o, pair))
-            for m in (Y, E, HID)
-            for o in (FIRST, LAST)
-            for pair in (LOW, HIGH)
-        }
-        codes, scales, banks, result = {}, {}, {}, {}
+        rounded, codes, scales, banks, result = {}, {}, {}, {}, {}
 
-        def rounding_views(m, o, pair):
-            src = raw[(m, o)][:].rearrange("p j (u t r) -> p t u j r", t=PACK, r=RUN)[:, 2 * pair : 2 * pair + 2]
-            dst = rounded[(m, o, pair)][:].rearrange("p (t u r j) -> p t u j r", t=2, r=RUN, j=PACK)
-            return dst, src
+        def round_tiles(copy, m, o, group, tiles=None):
+            key = (m, o, group)
+            if key not in rounded:
+                rounded[key] = sbuf([P, (group[1] - group[0]) * P * PACK], BF16, rounded_name(m, o, group))
+            a, b = tiles or group
+            src = raw[(m, o)][:].rearrange("p j (u t r) -> p t u j r", t=PACK, r=RUN)
+            dst = rounded[key][:].rearrange("p (t u r j) -> p t u j r", u=P // RUN, r=RUN, j=PACK)
+            if b - a == 1:
+                copy(dst[:, a - group[0]], src[:, a])
+            else:
+                copy(dst[:, a - group[0] : b - group[0]], src[:, a:b])
 
-        def round_pair(copy, m, o, pair):
-            copy(*rounding_views(m, o, pair))
-
-        def round_tiles_on_scalar(m, o, pair):
-            dst, src = rounding_views(m, o, pair)
-            for t in range(2):
-                nc.scalar.copy(dst[:, t], src[:, t])
-
-        def multiply(m, o, t):
-            if o == FIRST:
-                banks[(m, t)] = bank(PACK * (m % 2) + t)
-            cols = slice(t % 2 * P, (t % 2 + 1) * P)
-            nc.tensor.matmul_mx(
-                out=banks[(m, t)][:],
-                lhsT=codes[(m, o, t // 2)][:, cols].bitcast(FP8X4),
-                lhsT_scale=scales[(m, o, t // 2)][:, cols],
-                rhs=xq[o][:].bitcast(FP8X4),
-                rhs_scale=xq_scales[4 * o : P, :],
-                start=(o == FIRST),
-                stop=(o == LAST),
-            )
-
-        def quantise_and_multiply(m, o, pair, tiles_a_call=2, behind=None):
-            key = (m, o, pair)
-            codes[key] = sbuf([P, 2 * P], U32, behind or "codes_%d_%d_%d" % key)
-            scales[key] = sbuf([P, 2 * P], U8, "scales_%d_%d_%d" % key)
-            for a in range(0, 2, tiles_a_call):
-                b = a + tiles_a_call
-                nc.vector.quantize_mx(
-                    out=codes[key][:, a * P : b * P].bitcast(FP8X4),
-                    scales=scales[key][:, a * P : b * P],
-                    in_=rounded[key][:, a * P * PACK : b * P * PACK],
+        def quantise_and_multiply(m, o, group, behind=None):
+            width = (group[1] - group[0]) * P
+            words_q = sbuf([P, width], U32, behind or codes_name(m, o, group))
+            bytes_q = sbuf([P, width], U8, "scales_%d_%d_%d" % (m, o, group[0]))
+            nc.vector.quantize_mx(out=words_q[:].bitcast(FP8X4), scales=bytes_q[:], in_=rounded[(m, o, group)][:])
+            for t in range(*group):
+                if o == FIRST:
+                    banks[(m, t)] = bank(PACK * (m % 2) + t)
+                cols = slice((t - group[0]) * P, (t - group[0] + 1) * P)
+                nc.tensor.matmul_mx(
+                    out=banks[(m, t)][:],
+                    lhsT=words_q[:, cols].bitcast(FP8X4),
+                    lhsT_scale=bytes_q[:, cols],
+                    rhs=xq[o][:].bitcast(FP8X4),
+                    rhs_scale=xq_scales[4 * o : P, :],
+                    start=(o == FIRST),
+                    stop=(o == LAST),
                 )
-                for t in range(2 * pair + a, 2 * pair + b):
-                    multiply(m, o, t)
 
-        def drain(m, t):
-            result[(m, t)] = sbuf([P, S], F32, "res_%d_%d" % (m, t))
+        def drain(m, t, behind=None):
+            result[(m, t)] = sbuf([P, S], F32, behind or "res_%d_%d" % (m, t))
             nc.scalar.copy(result[(m, t)][:], banks[(m, t)][:])
 
         centre, diff, turned, squashed, summed, lead, share = {}, {}, {}, {}, {}, {}, {}
@@ -156,10 +146,13 @@ def tile_picked_zpt_tanh_po_kernel(
                 centre[t] = picked[:, n, :]
                 nc.vector.tensor_copy(centre[t], result[(Y, t)][:].indirect(cen_t[:]))
 
-        def gather_keys(t, behind=None):
-            diff[t] = sbuf([P, 2, V], F32, behind or "diff%d" % t)
-            for d in range(2):
-                nc.vector.tensor_tensor(diff[t][:, d, :], result[(E, t)][:].indirect(pos_t[d][:]), centre[t], SUB)
+        def new_diffs(tiles, behind):
+            both = sbuf([P, len(tiles), 2, V], F32, behind)
+            for n, t in enumerate(tiles):
+                diff[t] = both[:, n]
+
+        def gather_key(t, d):
+            nc.vector.tensor_tensor(diff[t][:, d, :], result[(E, t)][:].indirect(pos_t[d][:]), centre[t], SUB)
 
         ident = sbuf([P, P], F32, "ident")
         make_identity(nc, ident[:])
@@ -208,11 +201,14 @@ def tile_picked_zpt_tanh_po_kernel(
             for d, sign in enumerate((1.0, -1.0)):
                 nc.scalar.activation(share[t][:, d, :], lead[t][:], SIGMOID, scale=2.0 * sign)
 
-        w4_bf16 = sbuf([P, N * PACK], BF16, "w4_bf16")
+        w4_bf16 = [sbuf([P, 2 * P * PACK], BF16, "w4_bf16_%d" % a) for a in range(2)]
         w4_codes = sbuf([P, N], U32, "w4_codes")
         w4_scales = sbuf([P, N], U8, "w4_scales")
-        w4_dst = w4_bf16[:].rearrange("p (a b m j) -> p a m j b", a=2, b=2, j=PACK)
-        w4_src = w4_raw[:].rearrange("p j (m a b) -> p a m j b", a=2, b=2)
+
+        def round_w4(copy, side, a, m0=0, m1=P // 2):
+            dst = w4_bf16[a][:].rearrange("p (b h m j) -> p h m j b", b=2, h=2, j=PACK)
+            src = w4_raw[side][:].rearrange("p j (m a b) -> p a m j b", a=2, b=2)
+            copy(dst[:, side, m0:m1], src[:, a, m0:m1])
 
         terms = [sbuf([P, PACK, V], F32, "term%d" % d) for d in range(2)]
 
@@ -227,112 +223,142 @@ def tile_picked_zpt_tanh_po_kernel(
         out_scales = sbuf([P, V], U8, "out_scales")
         out_codes = sbuf([P, V], U32, "out_codes")
 
-        nc.vector.tensor_copy(xq[FIRST][:], words[FIRST][:].bitcast(U32).indirect(offs_t[:]))
-        round_tiles_on_scalar(Y, FIRST, LOW)
-        round_tiles_on_scalar(Y, FIRST, HIGH)
-        nc.vector.tensor_copy(xq_scales[:], x_bytes[:].indirect(offs_t[:]))
-        quantise_and_multiply(Y, FIRST, LOW)
-        nc.vector.tensor_copy(xq[LAST][:], words[LAST][:].bitcast(U32).indirect(offs_t[:]))
-        quantise_and_multiply(Y, FIRST, HIGH)
-        round_pair(nc.vector.tensor_copy, Y, LAST, LOW)
-        round_tiles_on_scalar(Y, LAST, HIGH)
-        for pair in (LOW, HIGH):
-            quantise_and_multiply(Y, LAST, pair)
-        for t in range(PACK):
-            drain(Y, t)
+        def quantise_w4(a):
+            nc.vector.quantize_mx(
+                out=w4_codes[:, a * 2 * P : (a + 1) * 2 * P].bitcast(FP8X4),
+                scales=w4_scales[:, a * 2 * P : (a + 1) * 2 * P],
+                in_=w4_bf16[a][:],
+            )
 
-        for pair in (LOW, HIGH):
-            round_pair(nc.vector.tensor_copy, E, FIRST, pair)
-        for pair in (LOW, HIGH):
-            quantise_and_multiply(E, FIRST, pair)
-        gather_centres((0,), behind=raw_name(E, FIRST))
-        round_pair(nc.vector.tensor_copy, E, LAST, LOW)
-        round_tiles_on_scalar(E, LAST, HIGH)
-        quantise_and_multiply(E, LAST, LOW, tiles_a_call=1)
-        quantise_and_multiply(E, LAST, HIGH)
-        gather_centres((1, 2, 3), behind=rounded_name(E, LAST, LOW))
-        for t in range(PACK):
-            drain(E, t)
+        z_bf16, z_codes, z_scales = {}, {}, {}
 
-        for pair in (LOW, HIGH):
-            round_pair(nc.scalar.copy, HID, FIRST, pair)
-        for t in (0, 1):
-            gather_keys(t)
-            turn(t, 4 + t)
-        squash_turned((0, 1), behind=raw_name(HID, FIRST))
-        quantise_and_multiply(HID, FIRST, LOW)
-        for pair in (LOW, HIGH):
-            round_pair(nc.vector.tensor_copy, HID, LAST, pair)
-        for t in (0, 1):
-            add_and_turn_back(t, 6 + t)
-        quantise_and_multiply(HID, LAST, LOW)
-        quantise_and_multiply(HID, FIRST, HIGH, behind=raw_name(HID, LAST))
-        quantise_and_multiply(HID, LAST, HIGH)
-        gather_keys(2, behind=rounded_name(HID, LAST, LOW))
-        gather_keys(3, behind=rounded_name(HID, FIRST, HIGH))
-
-        for t in (0, 1):
-            shares_from_sum(t)
-        for t in (0, 1):
-            drain(HID, t)
-            squash(t + 2)
-        for d in range(2):
-            gather_values(0, d)
-        for t in (2, 3):
-            subtract(t)
-        for t in (2, 3):
-            drain(HID, t)
-            shares_from_difference(t)
-        for d in range(2):
-            gather_values(1, d)
-        nc.vector.tensor_copy(w4_dst[:, :, :W4_ON_VECTOR], w4_src[:, :, :W4_ON_VECTOR])
-        for d in range(2):
-            gather_values(2, d)
-        for a in range(2):
-            nc.scalar.copy(w4_dst[:, a, W4_ON_VECTOR:], w4_src[:, a, W4_ON_VECTOR:])
-        gather_values(3, 0)
-        for c0 in (0, HALF):
-            gather_values(3, 1, c0, c0 + HALF)
-
-        z_bf16 = []
-        for c0 in (0, HALF):
-            z = sbuf([P, HALF * PACK], BF16, "z%d" % c0)
+        def sum_terms(g, behind):
+            c0 = g * HALF
+            z_bf16[g] = sbuf([P, HALF * PACK], BF16, behind)
             nc.vector.tensor_tensor(
-                z[:].rearrange("p (c r t) -> p c t r", r=RUN, t=PACK),
+                z_bf16[g][:].rearrange("p (c r t) -> p c t r", r=RUN, t=PACK),
                 terms[0][:, :, c0 : c0 + HALF].rearrange("p t (c r) -> p c t r", r=RUN),
                 terms[1][:, :, c0 : c0 + HALF].rearrange("p t (c r) -> p c t r", r=RUN),
                 ADD,
             )
-            z_bf16.append(z)
-        z_codes, z_scales = [], []
-        for g in range(2):
-            z_codes.append(sbuf([P, HALF], U32, "z_codes%d" % (g * HALF)))
-            z_scales.append(sbuf([P, HALF], U8, "z_scales%d" % (g * HALF)))
+
+        def quantise_z(g):
+            z_codes[g] = sbuf([P, HALF], U32, "z_codes%d" % (g * HALF))
+            z_scales[g] = sbuf([P, HALF], U8, "z_scales%d" % (g * HALF))
             nc.vector.quantize_mx(out=z_codes[g][:].bitcast(FP8X4), scales=z_scales[g][:], in_=z_bf16[g][:])
 
-        first_half, second_for_codes, second_for_values = bank(4), bank(5), bank(6)
+        def project(target, g, tiles=(0, PACK)):
+            for t in range(*tiles):
+                nc.tensor.matmul_mx(
+                    out=target[:, (t - tiles[0]) * HALF : (t - tiles[0] + 1) * HALF],
+                    lhsT=w4_codes[:, t * P : (t + 1) * P].bitcast(FP8X4),
+                    lhsT_scale=w4_scales[:, t * P : (t + 1) * P],
+                    rhs=z_codes[g][:].bitcast(FP8X4),
+                    rhs_scale=z_scales[g][:],
+                    start=True,
+                    stop=True,
+                )
 
-        def project(target, g, t):
-            nc.tensor.matmul_mx(
-                out=target[:, t * HALF : (t + 1) * HALF],
-                lhsT=w4_codes[:, t * P : (t + 1) * P].bitcast(FP8X4),
-                lhsT_scale=w4_scales[:, t * P : (t + 1) * P],
-                rhs=z_codes[g][:].bitcast(FP8X4),
-                rhs_scale=z_scales[g][:],
-                start=True,
-                stop=True,
-            )
+        on_vector, on_scalar = nc.vector.tensor_copy, nc.scalar.copy
 
+        nc.vector.tensor_copy(xq[FIRST][:], words[FIRST][:].bitcast(U32).indirect(offs_t[:]))
+        for group in (LOW, HIGH):
+            for t in range(*group):
+                round_tiles(on_scalar, Y, FIRST, group, (t, t + 1))
+        nc.vector.tensor_copy(xq_scales[:], x_bytes[:].indirect(offs_t[:]))
+        quantise_and_multiply(Y, FIRST, LOW)
+        nc.vector.tensor_copy(xq[LAST][:], words[LAST][:].bitcast(U32).indirect(offs_t[:]))
+        quantise_and_multiply(Y, FIRST, HIGH)
+        round_tiles(on_vector, Y, LAST, LOW)
+        for t in range(*HIGH):
+            round_tiles(on_scalar, Y, LAST, HIGH, (t, t + 1))
+        for group in (LOW, HIGH):
+            quantise_and_multiply(Y, LAST, group)
         for t in range(PACK):
-            nc.vector.quantize_mx(
-                out=w4_codes[:, t * P : (t + 1) * P].bitcast(FP8X4),
-                scales=w4_scales[:, t * P : (t + 1) * P],
-                in_=w4_bf16[:, t * P * PACK : (t + 1) * P * PACK],
-            )
-            project(first_half, 0, t)
-        for target in (second_for_codes, second_for_values):
-            for t in range(PACK):
-                project(target, 1, t)
+            drain(Y, t)
+
+        for group in (LOW, HIGH):
+            round_tiles(on_vector, E, FIRST, group)
+        for group in (LOW, HIGH):
+            quantise_and_multiply(E, FIRST, group)
+        gather_centres((0, 1, 2, 3), behind=raw_name(E, FIRST))
+        for group in (LOW, HIGH):
+            round_tiles(on_scalar, E, LAST, group)
+        quantise_and_multiply(E, LAST, LOW)
+        for t in (0, 1):
+            drain(E, t)
+
+        for group in (T0, T1):
+            round_tiles(on_vector, HID, FIRST, group)
+        quantise_and_multiply(HID, FIRST, T0)
+        round_tiles(on_vector, HID, FIRST, HIGH, T2)
+        round_tiles(on_scalar, HID, FIRST, HIGH, T3)
+        quantise_and_multiply(HID, FIRST, T1)
+        quantise_and_multiply(E, LAST, HIGH, behind=rounded_name(HID, FIRST, T0))
+        for t in (2, 3):
+            drain(E, t)
+        new_diffs((0,), behind=rounded_name(HID, FIRST, T1))
+        for d in range(2):
+            gather_key(0, d)
+        turn(0, 4)
+
+        for group in (T0, T1):
+            round_tiles(on_vector, HID, LAST, group)
+        round_tiles(on_scalar, HID, LAST, HIGH)
+        for group in (T0, T1):
+            quantise_and_multiply(HID, LAST, group)
+        quantise_and_multiply(HID, FIRST, HIGH, behind=rounded_name(HID, LAST, T0))
+        new_diffs((1,), behind=rounded_name(HID, LAST, T1))
+        for d in range(2):
+            gather_key(1, d)
+        squash_turned((0,), behind=codes_name(HID, LAST, T0))
+        add_and_turn_back(0, 6)
+        turn(1, 5)
+        new_diffs((2, 3), behind=raw_name(HID, LAST))
+        gather_key(2, 0)
+        quantise_and_multiply(HID, LAST, HIGH, behind="res_1_1")
+        gather_key(2, 1)
+        for d in range(2):
+            gather_key(3, d)
+        drain(HID, 0)
+        shares_from_sum(0)
+        squash_turned((1,), behind="sq1")
+        add_and_turn_back(1, 7)
+        drain(HID, 1)
+        squash(2)
+        shares_from_sum(1)
+        squash(3)
+        for d in range(2):
+            gather_values(0, d)
+        subtract(2)
+        for d in range(2):
+            gather_values(1, d)
+        subtract(3)
+        for t in (2, 3):
+            drain(HID, t)
+            shares_from_difference(t)
+        for a in range(2):
+            round_w4(on_vector, 0, a, 0, W4_ON_VECTOR)
+        for a in range(2):
+            round_w4(on_scalar, 0, a, W4_ON_VECTOR)
+        for a in range(2):
+            round_w4(on_scalar, 1, a)
+        for d in range(2):
+            gather_values(2, d)
+        gather_values(3, 0)
+        for c0 in (0, HALF):
+            gather_values(3, 1, c0, c0 + HALF)
+        sum_terms(0, behind="w4_raw0")
+        quantise_w4(0)
+        quantise_z(0)
+        sum_terms(1, behind="w4_bf16_0")
+        quantise_w4(1)
+        quantise_z(1)
+        first_half, second_for_codes, second_for_values = bank(4), bank(5), (bank(6), bank(7))
+        project(first_half, 0)
+        project(second_for_codes, 1)
+        for a, pair in enumerate((LOW, HIGH)):
+            project(second_for_values[a], 1, pair)
 
         out_rows = out_0.rearrange("(p t) v -> p t v", t=PACK)
 
@@ -342,24 +368,27 @@ def tile_picked_zpt_tanh_po_kernel(
                 t1 = t0 + tiles_a_store
                 nc.scalar.copy(values[:, t0:t1].rearrange("p t v -> p (t v)"), source[:, t0 * HALF : t1 * HALF])
                 queue.dma_start(out_rows[:, t0:t1, c0 : c0 + HALF], values[:, t0:t1])
-            return values
 
-        first_values = store_values(first_half, 0, PACK, nc.sync)
-        second_bf16 = sbuf([P, HALF * PACK], BF16, "out_bf16_%d" % HALF)
-        nc.vector.tensor_copy(
-            second_bf16[:].rearrange("p (v t) -> p v t", t=PACK),
-            second_for_codes[:].rearrange("p (t v) -> p v t", t=PACK),
-        )
-        first_bf16 = sbuf([P, HALF * PACK], BF16, "out_bf16_0")
-        nc.vector.tensor_copy(
-            first_bf16[:].rearrange("p (c r t) -> p c t r", r=RUN, t=PACK),
-            first_values[:].rearrange("p t (c r) -> p c t r", r=RUN),
-        )
-        for c0, source in ((HALF, second_bf16), (0, first_bf16)):
-            nc.vector.quantize_mx(
-                out=out_codes[:, c0 : c0 + HALF].bitcast(FP8X4), scales=out_scales[:, c0 : c0 + HALF], in_=source[:]
+        def round_out(copy, source, c0):
+            rounded_out = sbuf([P, HALF * PACK], BF16, "out_bf16_%d" % c0)
+            copy(
+                rounded_out[:].rearrange("p (v t) -> p v t", t=PACK),
+                source[:].rearrange("p (t v) -> p v t", t=PACK),
             )
-        store_values(second_for_values, HALF, 2, nc.scalar)
+            return rounded_out
+
+        store_values(first_half, 0, PACK, nc.sync)
+        halves = ((0, round_out(on_scalar, first_half, 0)), (HALF, round_out(on_vector, second_for_codes, HALF)))
+        for c0, rounded_out in halves:
+            nc.vector.quantize_mx(
+                out=out_codes[:, c0 : c0 + HALF].bitcast(FP8X4),
+                scales=out_scales[:, c0 : c0 + HALF],
+                in_=rounded_out[:],
+            )
+        values = sbuf([P, PACK, HALF], F32, "out%d" % HALF)
+        for a in range(2):
+            nc.scalar.copy(values[:, 2 * a : 2 * a + 2].rearrange("p t v -> p (t v)"), second_for_values[a][:, : 2 * HALF])
+            nc.sync.dma_start(out_rows[:, 2 * a : 2 * a + 2, HALF:V], values[:, 2 * a : 2 * a + 2])
         nc.sync.dma_start(out_1[0].rearrange("p c r -> p (c r)").bitcast(I32), out_codes[:].bitcast(I32))
         for q in range(4):
             queue = nc.sync if q < 2 else nc.scalar

@@ -73,8 +73,8 @@ def tile_picked_zpt_tanh_po_kernel(
 
         x_bytes = sbuf([P, T], U8, "x_bytes")
         nc.vector.memset(x_bytes[:].bitcast(I32), 0)
-        offs_t = load_list(offs, "offs")
         words = [load_words(FIRST)]
+        offs_t = load_list(offs, "offs")
         load_pass(w1, Y, FIRST)
         for q in range(4):
             nc.sync.dma_start(
@@ -83,11 +83,11 @@ def tile_picked_zpt_tanh_po_kernel(
             )
         words.append(load_words(LAST))
         load_pass(w1, Y, LAST)
-        cen_t = load_list(cen, "cen")
         load_pass(w2, E, FIRST)
+        cen_t = load_list(cen, "cen")
         load_pass(w2, E, LAST)
-        pos_t = [load_list(pos1, "pos1"), load_list(pos2, "pos2")]
         load_pass(w3, HID, FIRST)
+        pos_t = [load_list(pos1, "pos1"), load_list(pos2, "pos2")]
         load_pass(w3, HID, LAST)
         w4_rows = w4.rearrange("(u t r) n -> t u r n", t=PACK, r=RUN)
         w4_raw = []
@@ -103,7 +103,7 @@ def tile_picked_zpt_tanh_po_kernel(
         xq_scales = sbuf([P, S], U8, "xq_scales")
         rounded, codes, scales, banks, result = {}, {}, {}, {}, {}
 
-        def round_tiles(copy, m, o, group, tiles=None):
+        def round_tiles(copy, m, o, group, tiles=None, part=slice(0, P // RUN)):
             key = (m, o, group)
             if key not in rounded:
                 rounded[key] = sbuf([P, (group[1] - group[0]) * P * PACK], BF16, rounded_name(m, o, group))
@@ -111,7 +111,7 @@ def tile_picked_zpt_tanh_po_kernel(
             src = raw[(m, o)][:].rearrange("p j (u t r) -> p t u j r", t=PACK, r=RUN)
             dst = rounded[key][:].rearrange("p (t u r j) -> p t u j r", u=P // RUN, r=RUN, j=PACK)
             if b - a == 1:
-                copy(dst[:, a - group[0]], src[:, a])
+                copy(dst[:, a - group[0], part], src[:, a, part])
             else:
                 copy(dst[:, a - group[0] : b - group[0]], src[:, a:b])
 
@@ -281,10 +281,14 @@ def tile_picked_zpt_tanh_po_kernel(
             round_tiles(on_vector, E, FIRST, group)
         for group in (LOW, HIGH):
             quantise_and_multiply(E, FIRST, group)
-        gather_centres((0, 1, 2, 3), behind=raw_name(E, FIRST))
-        for group in (LOW, HIGH):
-            round_tiles(on_scalar, E, LAST, group)
-        quantise_and_multiply(E, LAST, LOW)
+        gather_centres((0, 1, 2), behind=raw_name(E, FIRST))
+        for part in (slice(0, 16), slice(16, 32)):
+            for group in (T0, T1):
+                round_tiles(on_scalar, E, LAST, group, part=part)
+        round_tiles(on_scalar, E, LAST, HIGH)
+        for group in (T0, T1):
+            quantise_and_multiply(E, LAST, group)
+        gather_centres((3,), behind=rounded_name(E, LAST, T0))
         for t in (0, 1):
             drain(E, t)
 
@@ -325,18 +329,21 @@ def tile_picked_zpt_tanh_po_kernel(
         squash_turned((1,), behind="sq1")
         add_and_turn_back(1, 7)
         drain(HID, 1)
-        squash(2)
+        turn(2, 4)
         shares_from_sum(1)
-        squash(3)
+        squash_turned((2,), behind="sq2")
+        add_and_turn_back(2, 6)
+        turn(3, 5)
+        drain(HID, 2)
+        squash_turned((3,), behind="sq3")
+        add_and_turn_back(3, 7)
+        shares_from_sum(2)
+        drain(HID, 3)
+        shares_from_sum(3)
         for d in range(2):
             gather_values(0, d)
-        subtract(2)
         for d in range(2):
             gather_values(1, d)
-        subtract(3)
-        for t in (2, 3):
-            drain(HID, t)
-            shares_from_difference(t)
         for a in range(2):
             round_w4(on_vector, 0, a, 0, W4_ON_VECTOR)
         for a in range(2):

@@ -295,8 +295,7 @@ def tile_picked_zpt_tanh_po_kernel(
         for group in (T0, T1):
             round_tiles(on_vector, HID, FIRST, group)
         quantise_and_multiply(HID, FIRST, T0)
-        round_tiles(on_vector, HID, FIRST, HIGH, T2)
-        round_tiles(on_scalar, HID, FIRST, HIGH, T3)
+        round_tiles(on_scalar, HID, FIRST, HIGH)
         quantise_and_multiply(HID, FIRST, T1)
         quantise_and_multiply(E, LAST, HIGH, behind=rounded_name(HID, FIRST, T0))
         for t in (2, 3):

@@ -21,20 +21,23 @@ MULT = mybir.AluOpType.mult
 P = 128
 PACK = 4
 RUN = 4
+RUNS = P // RUN
 K_PASS = P * PACK
 PASSES = K // K_PASS
 HALF = V // 2
+SIDE = N // 2
 Y, E, HID = 0, 1, 2
 FIRST, LAST = 0, 1
 LOW, HIGH = (0, 2), (2, 4)
+T0, T1 = (0, 1), (1, 2)
 W4_ON_VECTOR = 16
-T0, T1, T2, T3 = (0, 1), (1, 2), (2, 3), (3, 4)
 
 
 def tile_picked_zpt_tanh_po_kernel(
     tc, x_words, x_scales, w1, w2, w3, w4, offs, cen, pos1, pos2, out_0, out_1, out_2
 ):
     nc = tc.nc
+    on_vector, on_scalar = nc.vector.tensor_copy, nc.scalar.copy
     with ExitStack() as ctx:
         keep = ctx.enter_context(tc.tile_pool(name="keep", bufs=1))
         psum = ctx.enter_context(tc.psum_pool(name="psum", bufs=1))
@@ -54,15 +57,24 @@ def tile_picked_zpt_tanh_po_kernel(
         def codes_name(m, o, group):
             return "codes_%d_%d_%d" % (m, o, group[0])
 
+        def result_name(m, t):
+            return "res_%d_%d" % (m, t)
+
+        def w4_raw_name(side):
+            return "w4_raw%d" % side
+
+        def w4_rounded_name(a):
+            return "w4_bf16_%d" % a
+
         def load_list(src, name):
             lst = sbuf(list(src.shape), U16, name)
             nc.sync.dma_start(lst[:], src)
             return lst
 
         def load_words(o):
-            words = sbuf([P, T], I32, "x_words%d" % o)
-            nc.sync.dma_start(words[:], x_words[o].rearrange("p c r -> p (c r)").bitcast(I32))
-            return words
+            loaded = sbuf([P, T], I32, "x_words%d" % o)
+            nc.sync.dma_start(loaded[:], x_words[o].rearrange("p c r -> p (c r)").bitcast(I32))
+            return loaded
 
         raw = {}
 
@@ -92,53 +104,56 @@ def tile_picked_zpt_tanh_po_kernel(
         w4_rows = w4.rearrange("(u t r) n -> t u r n", t=PACK, r=RUN)
         w4_raw = []
         for side in range(2):
-            w4_raw.append(sbuf([P, PACK, N // 2], F32, "w4_raw%d" % side))
+            w4_raw.append(sbuf([P, PACK, SIDE], F32, w4_raw_name(side)))
             for t in range(PACK):
-                nc.sync.dma_start(w4_raw[side][:, t, :], w4_rows[t][:, :, side * N // 2 : (side + 1) * N // 2])
+                nc.sync.dma_start(w4_raw[side][:, t, :], w4_rows[t][:, :, side * SIDE : (side + 1) * SIDE])
 
         warm = sbuf([P, 1], F32, "warm")
         nc.scalar.activation(warm[:], raw[(Y, FIRST)][:, 0, 0:1], SIGMOID)
 
         xq = [sbuf([P, S], U32, "xq%d" % o) for o in range(PASSES)]
         xq_scales = sbuf([P, S], U8, "xq_scales")
-        rounded, codes, scales, banks, result = {}, {}, {}, {}, {}
+        rounded, banks, result = {}, {}, {}
 
-        def round_tiles(copy, m, o, group, tiles=None, part=slice(0, P // RUN)):
+        def rounding_views(m, o, group):
             key = (m, o, group)
             if key not in rounded:
                 rounded[key] = sbuf([P, (group[1] - group[0]) * P * PACK], BF16, rounded_name(m, o, group))
-            a, b = tiles or group
+            dst = rounded[key][:].rearrange("p (t u r j) -> p t u j r", u=RUNS, r=RUN, j=PACK)
             src = raw[(m, o)][:].rearrange("p j (u t r) -> p t u j r", t=PACK, r=RUN)
-            dst = rounded[key][:].rearrange("p (t u r j) -> p t u j r", u=P // RUN, r=RUN, j=PACK)
-            if b - a == 1:
-                copy(dst[:, a - group[0], part], src[:, a, part])
-            else:
-                copy(dst[:, a - group[0] : b - group[0]], src[:, a:b])
+            return dst, src[:, group[0] : group[1]]
+
+        def round_pair(copy, m, o, pair):
+            copy(*rounding_views(m, o, pair))
+
+        def round_tile(copy, m, o, group, n=0, runs=slice(0, RUNS)):
+            dst, src = rounding_views(m, o, group)
+            copy(dst[:, n, runs], src[:, n, runs])
 
         def quantise_and_multiply(m, o, group, behind=None):
             width = (group[1] - group[0]) * P
-            words_q = sbuf([P, width], U32, behind or codes_name(m, o, group))
-            bytes_q = sbuf([P, width], U8, "scales_%d_%d_%d" % (m, o, group[0]))
-            nc.vector.quantize_mx(out=words_q[:].bitcast(FP8X4), scales=bytes_q[:], in_=rounded[(m, o, group)][:])
+            codes = sbuf([P, width], U32, behind or codes_name(m, o, group))
+            scales = sbuf([P, width], U8, "scales_%d_%d_%d" % (m, o, group[0]))
+            nc.vector.quantize_mx(out=codes[:].bitcast(FP8X4), scales=scales[:], in_=rounded[(m, o, group)][:])
             for t in range(*group):
                 if o == FIRST:
                     banks[(m, t)] = bank(PACK * (m % 2) + t)
                 cols = slice((t - group[0]) * P, (t - group[0] + 1) * P)
                 nc.tensor.matmul_mx(
                     out=banks[(m, t)][:],
-                    lhsT=words_q[:, cols].bitcast(FP8X4),
-                    lhsT_scale=bytes_q[:, cols],
+                    lhsT=codes[:, cols].bitcast(FP8X4),
+                    lhsT_scale=scales[:, cols],
                     rhs=xq[o][:].bitcast(FP8X4),
                     rhs_scale=xq_scales[4 * o : P, :],
                     start=(o == FIRST),
                     stop=(o == LAST),
                 )
 
-        def drain(m, t, behind=None):
-            result[(m, t)] = sbuf([P, S], F32, behind or "res_%d_%d" % (m, t))
+        def drain(m, t):
+            result[(m, t)] = sbuf([P, S], F32, result_name(m, t))
             nc.scalar.copy(result[(m, t)][:], banks[(m, t)][:])
 
-        centre, diff, turned, squashed, summed, lead, share = {}, {}, {}, {}, {}, {}, {}
+        centre, diff, turned, squashed, summed, share = {}, {}, {}, {}, {}, {}
 
         def gather_centres(tiles, behind):
             picked = sbuf([P, len(tiles), V], F32, behind)
@@ -146,10 +161,10 @@ def tile_picked_zpt_tanh_po_kernel(
                 centre[t] = picked[:, n, :]
                 nc.vector.tensor_copy(centre[t], result[(Y, t)][:].indirect(cen_t[:]))
 
-        def new_diffs(tiles, behind):
-            both = sbuf([P, len(tiles), 2, V], F32, behind)
+        def room_for_diffs(tiles, behind):
+            room = sbuf([P, len(tiles), 2, V], F32, behind)
             for n, t in enumerate(tiles):
-                diff[t] = both[:, n]
+                diff[t] = room[:, n]
 
         def gather_key(t, d):
             nc.vector.tensor_tensor(diff[t][:, d, :], result[(E, t)][:].indirect(pos_t[d][:]), centre[t], SUB)
@@ -157,21 +172,19 @@ def tile_picked_zpt_tanh_po_kernel(
         ident = sbuf([P, P], F32, "ident")
         make_identity(nc, ident[:])
 
-        def turn(t, n):
-            turned[t] = bank(n)
+        def turn(t):
+            turned[t] = bank(4 + t % 2)
             for d in range(2):
                 for c in range(0, V, P):
                     nc.tensor.transpose(turned[t][:, d * V + c : d * V + c + P], diff[t][:, d, c : c + P], ident[:])
 
-        def squash_turned(tiles, behind):
-            both = sbuf([P, len(tiles), 2, V], F32, behind)
-            for n, t in enumerate(tiles):
-                squashed[t] = both[:, n]
-                for d, sign in enumerate((-1.0, 1.0)):
-                    nc.scalar.activation(squashed[t][:, d, :], turned[t][:, d * V : (d + 1) * V], SIGMOID, scale=2.0 * sign)
+        def squash(t, behind=None):
+            squashed[t] = sbuf([P, 2, V], F32, behind or "squashed%d" % t)
+            for d, sign in enumerate((-1.0, 1.0)):
+                nc.scalar.activation(squashed[t][:, d, :], turned[t][:, d * V : (d + 1) * V], SIGMOID, scale=2.0 * sign)
 
-        def add_and_turn_back(t, n):
-            summed[t] = bank(n)
+        def add_and_turn_back(t):
+            summed[t] = bank(6 + t % 2)
             for c in range(0, V, P):
                 for d in range(2):
                     nc.tensor.matmul(
@@ -183,25 +196,12 @@ def tile_picked_zpt_tanh_po_kernel(
                         is_transpose=True,
                     )
 
-        def shares_from_sum(t):
+        def shares(t):
             share[t] = sbuf([P, 2, V], F32, "share%d" % t)
             for d, sign in enumerate((1.0, -1.0)):
                 nc.scalar.activation(share[t][:, d, :], summed[t][:, :V], SIGMOID, scale=2.0 * sign, bias=-2.0 * sign)
 
-        def squash(t):
-            squashed[t] = sbuf([P, 2, V], F32, "squashed%d" % t)
-            nc.scalar.activation(squashed[t][:], diff[t][:], SIGMOID, scale=-2.0)
-
-        def subtract(t):
-            lead[t] = sbuf([P, V], F32, "lead%d" % t)
-            nc.vector.tensor_tensor(lead[t][:], squashed[t][:, 0, :], squashed[t][:, 1, :], SUB)
-
-        def shares_from_difference(t):
-            share[t] = sbuf([P, 2, V], F32, "share%d" % t)
-            for d, sign in enumerate((1.0, -1.0)):
-                nc.scalar.activation(share[t][:, d, :], lead[t][:], SIGMOID, scale=2.0 * sign)
-
-        w4_bf16 = [sbuf([P, 2 * P * PACK], BF16, "w4_bf16_%d" % a) for a in range(2)]
+        w4_bf16 = [sbuf([P, 2 * P * PACK], BF16, w4_rounded_name(a)) for a in range(2)]
         w4_codes = sbuf([P, N], U32, "w4_codes")
         w4_scales = sbuf([P, N], U8, "w4_scales")
 
@@ -243,8 +243,8 @@ def tile_picked_zpt_tanh_po_kernel(
             )
 
         def quantise_z(g):
-            z_codes[g] = sbuf([P, HALF], U32, "z_codes%d" % (g * HALF))
-            z_scales[g] = sbuf([P, HALF], U8, "z_scales%d" % (g * HALF))
+            z_codes[g] = sbuf([P, HALF], U32, "z_codes%d" % g)
+            z_scales[g] = sbuf([P, HALF], U8, "z_scales%d" % g)
             nc.vector.quantize_mx(out=z_codes[g][:].bitcast(FP8X4), scales=z_scales[g][:], in_=z_bf16[g][:])
 
         def project(target, g, tiles=(0, PACK)):
@@ -259,90 +259,89 @@ def tile_picked_zpt_tanh_po_kernel(
                     stop=True,
                 )
 
-        on_vector, on_scalar = nc.vector.tensor_copy, nc.scalar.copy
 
         nc.vector.tensor_copy(xq[FIRST][:], words[FIRST][:].bitcast(U32).indirect(offs_t[:]))
-        for group in (LOW, HIGH):
-            for t in range(*group):
-                round_tiles(on_scalar, Y, FIRST, group, (t, t + 1))
+        for pair in (LOW, HIGH):
+            for n in range(2):
+                round_tile(on_scalar, Y, FIRST, pair, n)
         nc.vector.tensor_copy(xq_scales[:], x_bytes[:].indirect(offs_t[:]))
         quantise_and_multiply(Y, FIRST, LOW)
         nc.vector.tensor_copy(xq[LAST][:], words[LAST][:].bitcast(U32).indirect(offs_t[:]))
         quantise_and_multiply(Y, FIRST, HIGH)
-        round_tiles(on_vector, Y, LAST, LOW)
-        for t in range(*HIGH):
-            round_tiles(on_scalar, Y, LAST, HIGH, (t, t + 1))
-        for group in (LOW, HIGH):
-            quantise_and_multiply(Y, LAST, group)
+        round_pair(on_vector, Y, LAST, LOW)
+        for n in range(2):
+            round_tile(on_scalar, Y, LAST, HIGH, n)
+        for pair in (LOW, HIGH):
+            quantise_and_multiply(Y, LAST, pair)
         for t in range(PACK):
             drain(Y, t)
 
-        for group in (LOW, HIGH):
-            round_tiles(on_vector, E, FIRST, group)
-        for group in (LOW, HIGH):
-            quantise_and_multiply(E, FIRST, group)
+        for pair in (LOW, HIGH):
+            round_pair(on_vector, E, FIRST, pair)
+        for pair in (LOW, HIGH):
+            quantise_and_multiply(E, FIRST, pair)
         gather_centres((0, 1, 2), behind=raw_name(E, FIRST))
-        for part in (slice(0, 16), slice(16, 32)):
+        for runs in (slice(0, RUNS // 2), slice(RUNS // 2, RUNS)):
             for group in (T0, T1):
-                round_tiles(on_scalar, E, LAST, group, part=part)
-        round_tiles(on_scalar, E, LAST, HIGH)
+                round_tile(on_scalar, E, LAST, group, runs=runs)
+        round_pair(on_scalar, E, LAST, HIGH)
         for group in (T0, T1):
             quantise_and_multiply(E, LAST, group)
         gather_centres((3,), behind=rounded_name(E, LAST, T0))
-        for t in (0, 1):
+        for t in range(*LOW):
             drain(E, t)
 
         for group in (T0, T1):
-            round_tiles(on_vector, HID, FIRST, group)
+            round_tile(on_vector, HID, FIRST, group)
         quantise_and_multiply(HID, FIRST, T0)
-        round_tiles(on_scalar, HID, FIRST, HIGH)
+        round_pair(on_scalar, HID, FIRST, HIGH)
         quantise_and_multiply(HID, FIRST, T1)
         quantise_and_multiply(E, LAST, HIGH, behind=rounded_name(HID, FIRST, T0))
-        for t in (2, 3):
+        for t in range(*HIGH):
             drain(E, t)
-        new_diffs((0,), behind=rounded_name(HID, FIRST, T1))
+        room_for_diffs((0,), behind=rounded_name(HID, FIRST, T1))
         for d in range(2):
             gather_key(0, d)
-        turn(0, 4)
+        turn(0)
 
         for group in (T0, T1):
-            round_tiles(on_vector, HID, LAST, group)
-        round_tiles(on_scalar, HID, LAST, HIGH)
+            round_tile(on_vector, HID, LAST, group)
+        round_pair(on_scalar, HID, LAST, HIGH)
         for group in (T0, T1):
             quantise_and_multiply(HID, LAST, group)
         quantise_and_multiply(HID, FIRST, HIGH, behind=rounded_name(HID, LAST, T0))
-        new_diffs((1,), behind=rounded_name(HID, LAST, T1))
+        room_for_diffs((1,), behind=rounded_name(HID, LAST, T1))
         for d in range(2):
             gather_key(1, d)
-        squash_turned((0,), behind=codes_name(HID, LAST, T0))
-        add_and_turn_back(0, 6)
-        turn(1, 5)
-        new_diffs((2, 3), behind=raw_name(HID, LAST))
+        squash(0, behind=codes_name(HID, LAST, T0))
+        add_and_turn_back(0)
+        turn(1)
+        room_for_diffs((2, 3), behind=raw_name(HID, LAST))
         gather_key(2, 0)
-        quantise_and_multiply(HID, LAST, HIGH, behind="res_1_1")
+        quantise_and_multiply(HID, LAST, HIGH, behind=result_name(E, 1))
         gather_key(2, 1)
         for d in range(2):
             gather_key(3, d)
+
         drain(HID, 0)
-        shares_from_sum(0)
-        squash_turned((1,), behind="sq1")
-        add_and_turn_back(1, 7)
+        shares(0)
+        squash(1)
+        add_and_turn_back(1)
         drain(HID, 1)
-        turn(2, 4)
-        shares_from_sum(1)
-        squash_turned((2,), behind="sq2")
-        add_and_turn_back(2, 6)
-        turn(3, 5)
+        turn(2)
+        shares(1)
+        squash(2)
+        add_and_turn_back(2)
+        turn(3)
         drain(HID, 2)
-        squash_turned((3,), behind="sq3")
-        add_and_turn_back(3, 7)
-        shares_from_sum(2)
+        squash(3)
+        add_and_turn_back(3)
+        shares(2)
         drain(HID, 3)
-        shares_from_sum(3)
-        for d in range(2):
-            gather_values(0, d)
-        for d in range(2):
-            gather_values(1, d)
+        shares(3)
+        for t in range(*LOW):
+            for d in range(2):
+                gather_values(t, d)
         for a in range(2):
             round_w4(on_vector, 0, a, 0, W4_ON_VECTOR)
         for a in range(2):
@@ -354,10 +353,11 @@ def tile_picked_zpt_tanh_po_kernel(
         gather_values(3, 0)
         for c0 in (0, HALF):
             gather_values(3, 1, c0, c0 + HALF)
-        sum_terms(0, behind="w4_raw0")
+
+        sum_terms(0, behind=w4_raw_name(0))
         quantise_w4(0)
         quantise_z(0)
-        sum_terms(1, behind="w4_bf16_0")
+        sum_terms(1, behind=w4_rounded_name(0))
         quantise_w4(1)
         quantise_z(1)
         first_half, second_for_codes, second_for_values = bank(4), bank(5), (bank(6), bank(7))
@@ -367,35 +367,28 @@ def tile_picked_zpt_tanh_po_kernel(
             project(second_for_values[a], 1, pair)
 
         out_rows = out_0.rearrange("(p t) v -> p t v", t=PACK)
-
-        def store_values(source, c0, tiles_a_store, queue):
-            values = sbuf([P, PACK, HALF], F32, "out%d" % c0)
-            for t0 in range(0, PACK, tiles_a_store):
-                t1 = t0 + tiles_a_store
-                nc.scalar.copy(values[:, t0:t1].rearrange("p t v -> p (t v)"), source[:, t0 * HALF : t1 * HALF])
-                queue.dma_start(out_rows[:, t0:t1, c0 : c0 + HALF], values[:, t0:t1])
-
-        def round_out(copy, source, c0):
-            rounded_out = sbuf([P, HALF * PACK], BF16, "out_bf16_%d" % c0)
-            copy(
-                rounded_out[:].rearrange("p (v t) -> p v t", t=PACK),
-                source[:].rearrange("p (t v) -> p v t", t=PACK),
-            )
-            return rounded_out
-
-        store_values(first_half, 0, PACK, nc.sync)
-        halves = ((0, round_out(on_scalar, first_half, 0)), (HALF, round_out(on_vector, second_for_codes, HALF)))
-        for c0, rounded_out in halves:
+        first_values = sbuf([P, PACK, HALF], F32, "first_values")
+        nc.scalar.copy(first_values[:].rearrange("p t v -> p (t v)"), first_half[:])
+        nc.sync.dma_start(out_rows[:, :, :HALF], first_values[:])
+        first_bf16 = sbuf([P, HALF * PACK], BF16, "first_bf16")
+        nc.vector.tensor_copy(
+            first_bf16[:].rearrange("p (c r t) -> p c t r", r=RUN, t=PACK),
+            first_values[:].rearrange("p t (c r) -> p c t r", r=RUN),
+        )
+        second_bf16 = sbuf([P, HALF * PACK], BF16, "second_bf16")
+        nc.vector.tensor_copy(
+            second_bf16[:].rearrange("p (v t) -> p v t", t=PACK),
+            second_for_codes[:].rearrange("p (t v) -> p v t", t=PACK),
+        )
+        for c0, source in ((0, first_bf16), (HALF, second_bf16)):
             nc.vector.quantize_mx(
-                out=out_codes[:, c0 : c0 + HALF].bitcast(FP8X4),
-                scales=out_scales[:, c0 : c0 + HALF],
-                in_=rounded_out[:],
+                out=out_codes[:, c0 : c0 + HALF].bitcast(FP8X4), scales=out_scales[:, c0 : c0 + HALF], in_=source[:]
             )
-        values = sbuf([P, PACK, HALF], F32, "out%d" % HALF)
-        for a in range(2):
-            nc.scalar.copy(values[:, 2 * a : 2 * a + 2].rearrange("p t v -> p (t v)"), second_for_values[a][:, : 2 * HALF])
-            nc.sync.dma_start(out_rows[:, 2 * a : 2 * a + 2, HALF:V], values[:, 2 * a : 2 * a + 2])
+        second_values = sbuf([P, PACK, HALF], F32, "second_values")
+        for a, queue in enumerate((nc.sync, nc.scalar)):
+            piece = second_values[:, 2 * a : 2 * a + 2]
+            nc.scalar.copy(piece.rearrange("p t v -> p (t v)"), second_for_values[a][:, : 2 * HALF])
+            queue.dma_start(out_rows[:, 2 * a : 2 * a + 2, HALF:], piece)
         nc.sync.dma_start(out_1[0].rearrange("p c r -> p (c r)").bitcast(I32), out_codes[:].bitcast(I32))
-        for q in range(4):
-            queue = nc.sync if q < 2 else nc.scalar
+        for q, queue in enumerate((nc.sync, nc.sync, nc.scalar, nc.scalar)):
             queue.dma_start(out_2[0, 4 * q : 4 * q + 4, :].bitcast(I32), out_scales[32 * q : 32 * q + 4, :].bitcast(I32))

@@ -385,10 +385,10 @@ def tile_picked_zpt_tanh_po_kernel(
                 out=out_codes[:, c0 : c0 + HALF].bitcast(FP8X4), scales=out_scales[:, c0 : c0 + HALF], in_=source[:]
             )
         second_values = sbuf([P, PACK, HALF], F32, "second_values")
-        for a, queue in enumerate((nc.sync, nc.scalar)):
+        for a in range(2):
             piece = second_values[:, 2 * a : 2 * a + 2]
             nc.scalar.copy(piece.rearrange("p t v -> p (t v)"), second_for_values[a][:, : 2 * HALF])
-            queue.dma_start(out_rows[:, 2 * a : 2 * a + 2, HALF:], piece)
+            nc.sync.dma_start(out_rows[:, 2 * a : 2 * a + 2, HALF:], piece)
         nc.sync.dma_start(out_1[0].rearrange("p c r -> p (c r)").bitcast(I32), out_codes[:].bitcast(I32))
         for q, queue in enumerate((nc.sync, nc.sync, nc.scalar, nc.scalar)):
             queue.dma_start(out_2[0, 4 * q : 4 * q + 4, :].bitcast(I32), out_scales[32 * q : 32 * q + 4, :].bitcast(I32))

@@ -357,38 +357,36 @@ def tile_picked_zpt_tanh_po_kernel(
         sum_terms(0, behind=w4_raw_name(0))
         quantise_w4(0)
         quantise_z(0)
-        sum_terms(1, behind=w4_rounded_name(0))
         quantise_w4(1)
+        sum_terms(1, behind=w4_raw_name(0))
         quantise_z(1)
-        first_half, second_for_codes, second_for_values = bank(4), bank(5), (bank(6), bank(7))
+        first_half, second_half = bank(4), (bank(6), bank(7))
         project(first_half, 0)
-        project(second_for_codes, 1)
         for a, pair in enumerate((LOW, HIGH)):
-            project(second_for_values[a], 1, pair)
+            project(second_half[a], 1, pair)
 
         out_rows = out_0.rearrange("(p t) v -> p t v", t=PACK)
+
+        def round_and_quantise(values, c0):
+            as_bf16 = sbuf([P, HALF * PACK], BF16, "out_bf16_%d" % c0)
+            nc.vector.tensor_copy(
+                as_bf16[:].rearrange("p (c r t) -> p c t r", r=RUN, t=PACK),
+                values[:].rearrange("p t (c r) -> p c t r", r=RUN),
+            )
+            nc.vector.quantize_mx(
+                out=out_codes[:, c0 : c0 + HALF].bitcast(FP8X4), scales=out_scales[:, c0 : c0 + HALF], in_=as_bf16[:]
+            )
+
         first_values = sbuf([P, PACK, HALF], F32, "first_values")
         nc.scalar.copy(first_values[:].rearrange("p t v -> p (t v)"), first_half[:])
         nc.sync.dma_start(out_rows[:, :, :HALF], first_values[:])
-        first_bf16 = sbuf([P, HALF * PACK], BF16, "first_bf16")
-        nc.vector.tensor_copy(
-            first_bf16[:].rearrange("p (c r t) -> p c t r", r=RUN, t=PACK),
-            first_values[:].rearrange("p t (c r) -> p c t r", r=RUN),
-        )
-        second_bf16 = sbuf([P, HALF * PACK], BF16, "second_bf16")
-        nc.vector.tensor_copy(
-            second_bf16[:].rearrange("p (v t) -> p v t", t=PACK),
-            second_for_codes[:].rearrange("p (t v) -> p v t", t=PACK),
-        )
-        for c0, source in ((0, first_bf16), (HALF, second_bf16)):
-            nc.vector.quantize_mx(
-                out=out_codes[:, c0 : c0 + HALF].bitcast(FP8X4), scales=out_scales[:, c0 : c0 + HALF], in_=source[:]
-            )
+        round_and_quantise(first_values, 0)
         second_values = sbuf([P, PACK, HALF], F32, "second_values")
         for a in range(2):
             piece = second_values[:, 2 * a : 2 * a + 2]
-            nc.scalar.copy(piece.rearrange("p t v -> p (t v)"), second_for_values[a][:, : 2 * HALF])
+            nc.scalar.copy(piece.rearrange("p t v -> p (t v)"), second_half[a][:, : 2 * HALF])
             nc.sync.dma_start(out_rows[:, 2 * a : 2 * a + 2, HALF:], piece)
+        round_and_quantise(second_values, HALF)
         nc.sync.dma_start(out_1[0].rearrange("p c r -> p (c r)").bitcast(I32), out_codes[:].bitcast(I32))
         for q, queue in enumerate((nc.sync, nc.sync, nc.scalar, nc.scalar)):
             queue.dma_start(out_2[0, 4 * q : 4 * q + 4, :].bitcast(I32), out_scales[32 * q : 32 * q + 4, :].bitcast(I32))

@@ -232,20 +232,28 @@ def tile_picked_zpt_tanh_po_kernel(
 
         z_bf16, z_codes, z_scales = {}, {}, {}
 
-        def sum_terms(g, behind):
-            c0 = g * HALF
+        def sum_terms(g, behind, pieces=1):
             z_bf16[g] = sbuf([P, HALF * PACK], BF16, behind)
-            nc.vector.tensor_tensor(
-                z_bf16[g][:].rearrange("p (c r t) -> p c t r", r=RUN, t=PACK),
-                terms[0][:, :, c0 : c0 + HALF].rearrange("p t (c r) -> p c t r", r=RUN),
-                terms[1][:, :, c0 : c0 + HALF].rearrange("p t (c r) -> p c t r", r=RUN),
-                ADD,
-            )
+            width = HALF // pieces
+            for c in range(0, HALF, width):
+                c0 = g * HALF + c
+                nc.vector.tensor_tensor(
+                    z_bf16[g][:, c * PACK : (c + width) * PACK].rearrange("p (c r t) -> p c t r", r=RUN, t=PACK),
+                    terms[0][:, :, c0 : c0 + width].rearrange("p t (c r) -> p c t r", r=RUN),
+                    terms[1][:, :, c0 : c0 + width].rearrange("p t (c r) -> p c t r", r=RUN),
+                    ADD,
+                )
 
-        def quantise_z(g):
+        def quantise_z(g, pieces=1):
             z_codes[g] = sbuf([P, HALF], U32, "z_codes%d" % g)
             z_scales[g] = sbuf([P, HALF], U8, "z_scales%d" % g)
-            nc.vector.quantize_mx(out=z_codes[g][:].bitcast(FP8X4), scales=z_scales[g][:], in_=z_bf16[g][:])
+            width = HALF // pieces
+            for c in range(0, HALF, width):
+                nc.vector.quantize_mx(
+                    out=z_codes[g][:, c : c + width].bitcast(FP8X4),
+                    scales=z_scales[g][:, c : c + width],
+                    in_=z_bf16[g][:, c * PACK : (c + width) * PACK],
+                )
 
         def project(target, g, tiles=(0, PACK)):
             for t in range(*tiles):
@@ -358,35 +366,44 @@ def tile_picked_zpt_tanh_po_kernel(
         quantise_w4(0)
         quantise_z(0)
         quantise_w4(1)
-        sum_terms(1, behind=w4_raw_name(0))
-        quantise_z(1)
-        first_half, second_half = bank(4), (bank(6), bank(7))
-        project(first_half, 0)
-        for a, pair in enumerate((LOW, HIGH)):
-            project(second_half[a], 1, pair)
+        sum_terms(1, behind=w4_raw_name(1), pieces=2)
+        quantise_z(1, pieces=2)
+        first_half, second_half = (bank(4), bank(5)), (bank(6), bank(7))
+        for g, half in enumerate((first_half, second_half)):
+            for a, pair in enumerate((LOW, HIGH)):
+                project(half[a], g, pair)
 
         out_rows = out_0.rearrange("(p t) v -> p t v", t=PACK)
 
-        def round_and_quantise(values, c0):
+        def round_and_quantise(values, c0, groups):
             as_bf16 = sbuf([P, HALF * PACK], BF16, "out_bf16_%d" % c0)
-            nc.vector.tensor_copy(
-                as_bf16[:].rearrange("p (c r t) -> p c t r", r=RUN, t=PACK),
-                values[:].rearrange("p t (c r) -> p c t r", r=RUN),
-            )
-            nc.vector.quantize_mx(
-                out=out_codes[:, c0 : c0 + HALF].bitcast(FP8X4), scales=out_scales[:, c0 : c0 + HALF], in_=as_bf16[:]
-            )
+            dst = as_bf16[:].rearrange("p (c r t) -> p c t r", r=RUN, t=PACK)
+            src = values[:].rearrange("p t (c r) -> p c t r", r=RUN)
+            for lo, hi in groups[:-1]:
+                nc.vector.tensor_copy(dst[:, :, lo:hi], src[:, :, lo:hi])
+            lo, hi = groups[-1]
+            for runs in (slice(0, RUNS // 2), slice(RUNS // 2, RUNS)):
+                nc.vector.tensor_copy(dst[:, runs, lo:hi], src[:, runs, lo:hi])
+            for c in (0, HALF // 2):
+                cols = slice(c0 + c, c0 + c + HALF // 2)
+                nc.vector.quantize_mx(
+                    out=out_codes[:, cols].bitcast(FP8X4),
+                    scales=out_scales[:, cols],
+                    in_=as_bf16[:, c * PACK : (c + HALF // 2) * PACK],
+                )
 
         first_values = sbuf([P, PACK, HALF], F32, "first_values")
-        nc.scalar.copy(first_values[:].rearrange("p t v -> p (t v)"), first_half[:])
+        for a in range(2):
+            piece = first_values[:, 2 * a : 2 * a + 2]
+            nc.scalar.copy(piece.rearrange("p t v -> p (t v)"), first_half[a][:, : 2 * HALF])
         nc.sync.dma_start(out_rows[:, :, :HALF], first_values[:])
-        round_and_quantise(first_values, 0)
+        round_and_quantise(first_values, 0, [(0, PACK)])
         second_values = sbuf([P, PACK, HALF], F32, "second_values")
         for a in range(2):
             piece = second_values[:, 2 * a : 2 * a + 2]
             nc.scalar.copy(piece.rearrange("p t v -> p (t v)"), second_half[a][:, : 2 * HALF])
             nc.sync.dma_start(out_rows[:, 2 * a : 2 * a + 2, HALF:], piece)
-        round_and_quantise(second_values, HALF)
+        round_and_quantise(second_values, HALF, [LOW, HIGH])
         nc.sync.dma_start(out_1[0].rearrange("p c r -> p (c r)").bitcast(I32), out_codes[:].bitcast(I32))
         for q, queue in enumerate((nc.sync, nc.sync, nc.scalar, nc.scalar)):
             queue.dma_start(out_2[0, 4 * q : 4 * q + 4, :].bitcast(I32), out_scales[32 * q : 32 * q + 4, :].bitcast(I32))

@@ -113,7 +113,7 @@ def tile_picked_zpt_tanh_po_kernel(
 
         xq = [sbuf([P, S], U32, "xq%d" % o) for o in range(PASSES)]
         xq_scales = sbuf([P, S], U8, "xq_scales")
-        rounded, banks, result = {}, {}, {}
+        rounded, quantised, banks, result = {}, {}, {}, {}
 
         def rounding_views(m, o, group):
             key = (m, o, group)
@@ -135,6 +135,7 @@ def tile_picked_zpt_tanh_po_kernel(
             codes = sbuf([P, width], U32, behind or codes_name(m, o, group))
             scales = sbuf([P, width], U8, "scales_%d_%d_%d" % (m, o, group[0]))
             nc.vector.quantize_mx(out=codes[:].bitcast(FP8X4), scales=scales[:], in_=rounded[(m, o, group)][:])
+            quantised[(m, o, group)] = (codes, scales)
             for t in range(*group):
                 if o == FIRST:
                     banks[(m, t)] = bank(PACK * (m % 2) + t)
@@ -358,10 +359,24 @@ def tile_picked_zpt_tanh_po_kernel(
             round_w4(on_scalar, 1, a)
         for d in range(2):
             gather_values(2, d)
+        kept_codes, kept_scales = quantised[(Y, FIRST, LOW)]
         gather_values(3, 0)
         for c0 in (0, HALF):
             gather_values(3, 1, c0, c0 + HALF)
 
+        for n, t in enumerate(range(*HIGH)):
+            idle = bank(n)
+            nc.tensor.transpose(idle[:, :P], terms[0][:, t, :P], ident[:])
+            for again in range(2):
+                nc.tensor.matmul_mx(
+                    out=idle[:],
+                    lhsT=kept_codes[:, :P].bitcast(FP8X4),
+                    lhsT_scale=kept_scales[:, :P],
+                    rhs=xq[FIRST][:].bitcast(FP8X4),
+                    rhs_scale=xq_scales[:],
+                    start=True,
+                    stop=True,
+                )
         sum_terms(0, behind=w4_raw_name(0))
         quantise_w4(0)
         quantise_z(0)

@@ -85,14 +85,17 @@ def tile_picked_zpt_tanh_po_kernel(
 
         x_bytes = sbuf([P, T], U8, "x_bytes")
         nc.vector.memset(x_bytes[:].bitcast(I32), 0)
+
+        def load_scale_rows(o):
+            rows = x_scales[o].rearrange("(q r) c -> r q c", r=4)
+            for r in range(4):
+                nc.sync.dma_start(x_bytes[4 * o + r : P : 32, :].bitcast(I32), rows[r].bitcast(I32))
+
         words = [load_words(FIRST)]
+        load_scale_rows(FIRST)
         offs_t = load_list(offs, "offs")
         load_pass(w1, Y, FIRST)
-        for q in range(4):
-            nc.sync.dma_start(
-                x_bytes[32 * q : 32 * q + 4 * PASSES, :].bitcast(I32),
-                x_scales[:, 4 * q : 4 * q + 4, :].bitcast(I32),
-            )
+        load_scale_rows(LAST)
         words.append(load_words(LAST))
         load_pass(w1, Y, LAST)
         load_pass(w2, E, FIRST)

@@ -28,7 +28,7 @@ HALF = V // 2
 SIDE = N // 2
 Y, E, HID = 0, 1, 2
 FIRST, LAST = 0, 1
-LOW, HIGH = (0, 2), (2, 4)
+LOW, HIGH, ALL = (0, 2), (2, 4), (0, 4)
 T0, T1 = (0, 1), (1, 2)
 W4_ON_VECTOR = 16
 
@@ -62,9 +62,6 @@ def tile_picked_zpt_tanh_po_kernel(
 
         def w4_raw_name(side):
             return "w4_raw%d" % side
-
-        def w4_rounded_name(a):
-            return "w4_bf16_%d" % a
 
         def load_list(src, name):
             lst = sbuf(list(src.shape), U16, name)
@@ -205,7 +202,7 @@ def tile_picked_zpt_tanh_po_kernel(
             for d, sign in enumerate((1.0, -1.0)):
                 nc.scalar.activation(share[t][:, d, :], summed[t][:, :V], SIGMOID, scale=2.0 * sign, bias=-2.0 * sign)
 
-        w4_bf16 = [sbuf([P, 2 * P * PACK], BF16, w4_rounded_name(a)) for a in range(2)]
+        w4_bf16 = [sbuf([P, 2 * P * PACK], BF16, "w4_bf16_%d" % a) for a in range(2)]
         w4_codes = sbuf([P, N], U32, "w4_codes")
         w4_scales = sbuf([P, N], U8, "w4_scales")
 
@@ -259,10 +256,10 @@ def tile_picked_zpt_tanh_po_kernel(
                     in_=z_bf16[g][:, c * PACK : (c + width) * PACK],
                 )
 
-        def project(target, g, tiles=(0, PACK)):
-            for t in range(*tiles):
+        def project(target, g, pair):
+            for t in range(*pair):
                 nc.tensor.matmul_mx(
-                    out=target[:, (t - tiles[0]) * HALF : (t - tiles[0] + 1) * HALF],
+                    out=target[:, (t - pair[0]) * HALF : (t - pair[0] + 1) * HALF],
                     lhsT=w4_codes[:, t * P : (t + 1) * P].bitcast(FP8X4),
                     lhsT_scale=w4_scales[:, t * P : (t + 1) * P],
                     rhs=z_codes[g][:].bitcast(FP8X4),
@@ -362,34 +359,38 @@ def tile_picked_zpt_tanh_po_kernel(
             round_w4(on_scalar, 1, a)
         for d in range(2):
             gather_values(2, d)
-        kept_codes, kept_scales = quantised[(Y, FIRST, LOW)]
         gather_values(3, 0)
         for c0 in (0, HALF):
             gather_values(3, 1, c0, c0 + HALF)
 
-        for n, t in enumerate(range(*HIGH)):
+        def warm_up(n, passes, codes, scales):
             idle = bank(n)
-            nc.tensor.transpose(idle[:, :P], terms[0][:, t, :P], ident[:])
-            for again in range(2):
+            for repeat in range(passes):
                 nc.tensor.matmul_mx(
                     out=idle[:],
-                    lhsT=kept_codes[:, :P].bitcast(FP8X4),
-                    lhsT_scale=kept_scales[:, :P],
+                    lhsT=codes[:, :P].bitcast(FP8X4),
+                    lhsT_scale=scales[:, :P],
                     rhs=xq[FIRST][:].bitcast(FP8X4),
                     rhs_scale=xq_scales[:],
                     start=True,
                     stop=True,
                 )
+
+        warm_up(3, 2, *quantised[(Y, FIRST, LOW)])
+        warm_up(7, 3, *quantised[(Y, FIRST, LOW)])
+
         sum_terms(0, behind=w4_raw_name(0))
         quantise_w4(0)
+        warm_up(0, 1, w4_codes, w4_scales)
         quantise_z(0)
         quantise_w4(1)
         sum_terms(1, behind=w4_raw_name(1), pieces=2)
         quantise_z(1, pieces=2)
-        first_half, second_half = (bank(4), bank(5)), (bank(6), bank(7))
-        for g, half in enumerate((first_half, second_half)):
+        projected = {}
+        for g in range(2):
             for a, pair in enumerate((LOW, HIGH)):
-                project(half[a], g, pair)
+                projected[(g, a)] = bank(4 + 2 * g + a)
+                project(projected[(g, a)], g, pair)
 
         out_rows = out_0.rearrange("(p t) v -> p t v", t=PACK)
 
@@ -410,17 +411,19 @@ def tile_picked_zpt_tanh_po_kernel(
                     in_=as_bf16[:, c * PACK : (c + HALF // 2) * PACK],
                 )
 
+        def copy_out(values, g, a):
+            piece = values[:, 2 * a : 2 * a + 2]
+            nc.scalar.copy(piece.rearrange("p t v -> p (t v)"), projected[(g, a)][:, : 2 * HALF])
+            return piece
+
         first_values = sbuf([P, PACK, HALF], F32, "first_values")
         for a in range(2):
-            piece = first_values[:, 2 * a : 2 * a + 2]
-            nc.scalar.copy(piece.rearrange("p t v -> p (t v)"), first_half[a][:, : 2 * HALF])
+            copy_out(first_values, 0, a)
         nc.sync.dma_start(out_rows[:, :, :HALF], first_values[:])
-        round_and_quantise(first_values, 0, [(0, PACK)])
+        round_and_quantise(first_values, 0, [ALL])
         second_values = sbuf([P, PACK, HALF], F32, "second_values")
         for a in range(2):
-            piece = second_values[:, 2 * a : 2 * a + 2]
-            nc.scalar.copy(piece.rearrange("p t v -> p (t v)"), second_half[a][:, : 2 * HALF])
-            nc.sync.dma_start(out_rows[:, 2 * a : 2 * a + 2, HALF:], piece)
+            nc.sync.dma_start(out_rows[:, 2 * a : 2 * a + 2, HALF:], copy_out(second_values, 1, a))
         round_and_quantise(second_values, HALF, [LOW, HIGH])
         nc.sync.dma_start(out_1[0].rearrange("p c r -> p (c r)").bitcast(I32), out_codes[:].bitcast(I32))
         for q, queue in enumerate((nc.sync, nc.sync, nc.scalar, nc.scalar)):

@@ -14,6 +14,7 @@ U16 = mybir.dt.uint16
 U8 = mybir.dt.uint8
 FP8X4 = mybir.dt.float8_e4m3fn_x4
 SIGMOID = mybir.ActivationFunctionType.Sigmoid
+COPY = mybir.ActivationFunctionType.Copy
 ADD = mybir.AluOpType.add
 SUB = mybir.AluOpType.subtract
 MULT = mybir.AluOpType.mult
@@ -30,7 +31,6 @@ Y, E, HID = 0, 1, 2
 FIRST, LAST = 0, 1
 LOW, HIGH, ALL = (0, 2), (2, 4), (0, 4)
 T0, T1 = (0, 1), (1, 2)
-W4_ON_VECTOR = 16
 
 
 def tile_picked_zpt_tanh_po_kernel(
@@ -91,15 +91,15 @@ def tile_picked_zpt_tanh_po_kernel(
         words = [load_words(FIRST)]
         load_scale_rows(FIRST)
         offs_t = load_list(offs, "offs")
-        load_pass(w1, Y, FIRST)
+        load_pass(w2, E, FIRST)
         load_scale_rows(LAST)
         words.append(load_words(LAST))
-        load_pass(w1, Y, LAST)
-        load_pass(w2, E, FIRST)
-        cen_t = load_list(cen, "cen")
         load_pass(w2, E, LAST)
-        load_pass(w3, HID, FIRST)
         pos_t = [load_list(pos1, "pos1"), load_list(pos2, "pos2")]
+        load_pass(w1, Y, FIRST)
+        load_pass(w1, Y, LAST)
+        cen_t = load_list(cen, "cen")
+        load_pass(w3, HID, FIRST)
         load_pass(w3, HID, LAST)
         w4_rows = w4.rearrange("(u t r) n -> t u r n", t=PACK, r=RUN)
         w4_raw = []
@@ -109,7 +109,7 @@ def tile_picked_zpt_tanh_po_kernel(
                 nc.sync.dma_start(w4_raw[side][:, t, :], w4_rows[t][:, :, side * SIDE : (side + 1) * SIDE])
 
         warm = sbuf([P, 1], F32, "warm")
-        nc.scalar.activation(warm[:], raw[(Y, FIRST)][:, 0, 0:1], SIGMOID)
+        nc.scalar.activation(warm[:], raw[(E, FIRST)][:, 0, 0:1], SIGMOID)
 
         xq = [sbuf([P, S], U32, "xq%d" % o) for o in range(PASSES)]
         xq_scales = sbuf([P, S], U8, "xq_scales")
@@ -138,7 +138,7 @@ def tile_picked_zpt_tanh_po_kernel(
             quantised[(m, o, group)] = (codes, scales)
             for t in range(*group):
                 if o == FIRST:
-                    banks[(m, t)] = bank(PACK * (m % 2) + t)
+                    banks[(m, t)] = bank((PACK if m == Y else 0) + t)
                 cols = slice((t - group[0]) * P, (t - group[0] + 1) * P)
                 nc.tensor.matmul_mx(
                     out=banks[(m, t)][:],
@@ -150,34 +150,52 @@ def tile_picked_zpt_tanh_po_kernel(
                     stop=(o == LAST),
                 )
 
-        def drain(m, t):
-            result[(m, t)] = sbuf([P, S], F32, result_name(m, t))
-            nc.scalar.copy(result[(m, t)][:], banks[(m, t)][:])
+        def drain(m, t, copy=on_scalar, behind=None):
+            result[(m, t)] = sbuf([P, S], F32, behind or result_name(m, t))
+            copy(result[(m, t)][:], banks[(m, t)][:])
 
-        centre, diff, turned, squashed, summed, share = {}, {}, {}, {}, {}, {}
+        centre, key, turned, squashed, summed = {}, {}, {}, {}, {}
 
-        def gather_centres(tiles, behind):
-            picked = sbuf([P, len(tiles), V], F32, behind)
-            for n, t in enumerate(tiles):
-                centre[t] = picked[:, n, :]
-                nc.vector.tensor_copy(centre[t], result[(Y, t)][:].indirect(cen_t[:]))
+        terms = [sbuf([P, PACK, V], F32, "term%d" % d) for d in range(2)]
 
-        def room_for_diffs(tiles, behind):
-            room = sbuf([P, len(tiles), 2, V], F32, behind)
-            for n, t in enumerate(tiles):
-                diff[t] = room[:, n]
+        share = sbuf([P, PACK, V], F32, "share")
 
-        def gather_key(t, d):
-            nc.vector.tensor_tensor(diff[t][:, d, :], result[(E, t)][:].indirect(pos_t[d][:]), centre[t], SUB)
+        def gather_centre(t, behind=None, into=None):
+            centre[t] = into if into is not None else sbuf([P, V], F32, behind or "centre%d" % t)[:]
+            nc.scalar.activation(centre[t], result[(Y, t)][:].indirect(cen_t[:]), COPY, scale=-1.0)
+
+        def gather_key(t, d, vector=False, behind=None, into=None):
+            picked = into if into is not None else sbuf([P, V], F32, behind or "key%d_%d" % (t, d))[:]
+            window = result[(E, t)][:].indirect(pos_t[d][:])
+            if vector:
+                nc.vector.tensor_copy(picked, window)
+            else:
+                nc.scalar.activation(picked, window, COPY)
+            key[(t, d)] = (picked, False)
+
+        def gather_difference(t, d, behind):
+            into = sbuf([P, V], F32, behind)[:]
+            nc.vector.tensor_tensor(into, result[(E, t)][:].indirect(pos_t[d][:]), centre[t], ADD)
+            key[(t, d)] = (into, True)
 
         ident = sbuf([P, P], F32, "ident")
         make_identity(nc, ident[:])
 
         def turn(t):
-            turned[t] = bank(4 + t % 2)
-            for d in range(2):
+            turned[t] = bank(4 + t)
+            for d in (1, 0):
+                picked, whole = key[(t, d)]
+                parts = (picked,) if whole else (centre[t], picked)
                 for c in range(0, V, P):
-                    nc.tensor.transpose(turned[t][:, d * V + c : d * V + c + P], diff[t][:, d, c : c + P], ident[:])
+                    for n, part in enumerate(parts):
+                        nc.tensor.matmul(
+                            turned[t][:, d * V + c : d * V + c + P],
+                            part[:, c : c + P],
+                            ident[:],
+                            start=(n == 0),
+                            stop=(n == len(parts) - 1),
+                            is_transpose=True,
+                        )
 
         def squash(t, behind=None):
             squashed[t] = sbuf([P, 2, V], F32, behind or "squashed%d" % t)
@@ -185,7 +203,7 @@ def tile_picked_zpt_tanh_po_kernel(
                 nc.scalar.activation(squashed[t][:, d, :], turned[t][:, d * V : (d + 1) * V], SIGMOID, scale=2.0 * sign)
 
         def add_and_turn_back(t):
-            summed[t] = bank(6 + t % 2)
+            summed[t] = bank(4 + t)
             for c in range(0, V, P):
                 for d in range(2):
                     nc.tensor.matmul(
@@ -198,38 +216,45 @@ def tile_picked_zpt_tanh_po_kernel(
                     )
 
         def shares(t):
-            share[t] = sbuf([P, 2, V], F32, "share%d" % t)
-            for d, sign in enumerate((1.0, -1.0)):
-                nc.scalar.activation(share[t][:, d, :], summed[t][:, :V], SIGMOID, scale=2.0 * sign, bias=-2.0 * sign)
+            nc.scalar.activation(share[:, t, :], summed[t][:, :V], SIGMOID, scale=2.0, bias=-2.0)
 
-        w4_bf16 = [sbuf([P, 2 * P * PACK], BF16, "w4_bf16_%d" % a) for a in range(2)]
+        w4_bf16 = {}
         w4_codes = sbuf([P, N], U32, "w4_codes")
         w4_scales = sbuf([P, N], U8, "w4_scales")
 
-        def round_w4(copy, side, a, m0=0, m1=P // 2):
-            dst = w4_bf16[a][:].rearrange("p (b h m j) -> p h m j b", b=2, h=2, j=PACK)
+        def round_w4(copy, side, behind=None):
+            w4_bf16[side] = sbuf([P, PACK, SIDE], BF16, behind or "w4_bf16_%d" % side)
+            dst = w4_bf16[side][:].rearrange("p (a b) (m j) -> p a m j b", b=2, j=PACK)
             src = w4_raw[side][:].rearrange("p j (m a b) -> p a m j b", a=2, b=2)
-            copy(dst[:, side, m0:m1], src[:, a, m0:m1])
+            for a in range(2):
+                copy(dst[:, a], src[:, a])
 
-        terms = [sbuf([P, PACK, V], F32, "term%d" % d) for d in range(2)]
+        spread = sbuf([P, PACK, V], F32, "spread")
 
-        def gather_values(t, d, c0=0, c1=V):
-            nc.vector.tensor_tensor(
-                terms[d][:, t, c0:c1],
-                result[(HID, t)][:].indirect(pos_t[d][:, c0 // 16 : c1 // 16]),
-                share[t][:, d, c0:c1],
-                MULT,
-            )
+        def gather_second(t, vector=False):
+            window = result[(HID, t)][:].indirect(pos_t[1][:])
+            if vector:
+                nc.vector.tensor_copy(terms[1][:, t, :], window)
+            else:
+                nc.scalar.activation(terms[1][:, t, :], window, COPY)
+
+        def gather_spread(t, c0=0, c1=V):
+            window = result[(HID, t)][:].indirect(pos_t[0][:, c0 // 16 : c1 // 16])
+            nc.vector.tensor_tensor(spread[:, t, c0:c1], window, terms[1][:, t, c0:c1], SUB)
+
+        def weigh(group, c0=0, c1=V):
+            part = (slice(0, P), slice(*group), slice(c0, c1))
+            nc.vector.tensor_tensor(terms[0][part], spread[part], share[part], MULT)
 
         out_scales = sbuf([P, V], U8, "out_scales")
         out_codes = sbuf([P, V], U32, "out_codes")
 
-        def quantise_w4(a):
-            nc.vector.quantize_mx(
-                out=w4_codes[:, a * 2 * P : (a + 1) * 2 * P].bitcast(FP8X4),
-                scales=w4_scales[:, a * 2 * P : (a + 1) * 2 * P],
-                in_=w4_bf16[a][:],
-            )
+        def quantise_w4(side):
+            for t in range(PACK):
+                cols = slice(t * P + side * P // 2, t * P + (side + 1) * P // 2)
+                nc.vector.quantize_mx(
+                    out=w4_codes[:, cols].bitcast(FP8X4), scales=w4_scales[:, cols], in_=w4_bf16[side][:, t, :]
+                )
 
         z_bf16, z_codes, z_scales = {}, {}, {}
 
@@ -268,122 +293,88 @@ def tile_picked_zpt_tanh_po_kernel(
                     stop=True,
                 )
 
-
         nc.vector.tensor_copy(xq[FIRST][:], words[FIRST][:].bitcast(U32).indirect(offs_t[:]))
         for pair in (LOW, HIGH):
             for n in range(2):
-                round_tile(on_scalar, Y, FIRST, pair, n)
+                round_tile(on_scalar, E, FIRST, pair, n)
         nc.vector.tensor_copy(xq_scales[:], x_bytes[:].indirect(offs_t[:]))
-        quantise_and_multiply(Y, FIRST, LOW)
+        quantise_and_multiply(E, FIRST, LOW)
         nc.vector.tensor_copy(xq[LAST][:], words[LAST][:].bitcast(U32).indirect(offs_t[:]))
-        quantise_and_multiply(Y, FIRST, HIGH)
-        round_pair(on_vector, Y, LAST, LOW)
+        quantise_and_multiply(E, FIRST, HIGH)
+        round_pair(on_vector, E, LAST, LOW)
         for n in range(2):
-            round_tile(on_scalar, Y, LAST, HIGH, n)
+            round_tile(on_scalar, E, LAST, HIGH, n)
         for pair in (LOW, HIGH):
-            quantise_and_multiply(Y, LAST, pair)
-        for t in range(PACK):
-            drain(Y, t)
+            quantise_and_multiply(E, LAST, pair)
 
-        for pair in (LOW, HIGH):
-            round_pair(on_vector, E, FIRST, pair)
-        for pair in (LOW, HIGH):
-            quantise_and_multiply(E, FIRST, pair)
-        gather_centres((0, 1, 2), behind=raw_name(E, FIRST))
-        for runs in (slice(0, RUNS // 2), slice(RUNS // 2, RUNS)):
-            for group in (T0, T1):
-                round_tile(on_scalar, E, LAST, group, runs=runs)
-        round_pair(on_scalar, E, LAST, HIGH)
-        for group in (T0, T1):
-            quantise_and_multiply(E, LAST, group)
-        gather_centres((3,), behind=rounded_name(E, LAST, T0))
-        for t in range(*LOW):
-            drain(E, t)
+        def whole_pass_on_vector(m, o):
+            for pair in (LOW, HIGH):
+                round_pair(on_vector, m, o, pair)
+            for pair in (LOW, HIGH):
+                quantise_and_multiply(m, o, pair)
 
-        for group in (T0, T1):
-            round_tile(on_vector, HID, FIRST, group)
-        quantise_and_multiply(HID, FIRST, T0)
-        round_pair(on_scalar, HID, FIRST, HIGH)
-        quantise_and_multiply(HID, FIRST, T1)
-        quantise_and_multiply(E, LAST, HIGH, behind=rounded_name(HID, FIRST, T0))
-        for t in range(*HIGH):
-            drain(E, t)
-        room_for_diffs((0,), behind=rounded_name(HID, FIRST, T1))
+        drain(E, 0, on_vector)
+        drain(E, 1)
+        drain(E, 2)
+        whole_pass_on_vector(Y, FIRST)
         for d in range(2):
             gather_key(0, d)
-        turn(0)
-
-        for group in (T0, T1):
-            round_tile(on_vector, HID, LAST, group)
-        round_pair(on_scalar, HID, LAST, HIGH)
-        for group in (T0, T1):
-            quantise_and_multiply(HID, LAST, group)
-        quantise_and_multiply(HID, FIRST, HIGH, behind=rounded_name(HID, LAST, T0))
-        room_for_diffs((1,), behind=rounded_name(HID, LAST, T1))
+        drain(E, 3)
+        whole_pass_on_vector(Y, LAST)
         for d in range(2):
             gather_key(1, d)
-        squash(0, behind=codes_name(HID, LAST, T0))
-        add_and_turn_back(0)
-        turn(1)
-        room_for_diffs((2, 3), behind=raw_name(HID, LAST))
-        gather_key(2, 0)
-        quantise_and_multiply(HID, LAST, HIGH, behind=result_name(E, 1))
         gather_key(2, 1)
-        for d in range(2):
-            gather_key(3, d)
-
-        drain(HID, 0)
-        shares(0)
-        squash(1)
+        gather_key(2, 0, into=terms[1][:, 2, :])
+        gather_key(3, 0, vector=True, behind=rounded_name(Y, LAST, LOW))
+        for t in range(3):
+            drain(Y, t)
+        whole_pass_on_vector(HID, FIRST)
+        drain(Y, 3, on_vector, behind=raw_name(HID, FIRST))
+        gather_centre(0, behind=rounded_name(HID, FIRST, LOW))
+        turn(0)
+        gather_centre(1, behind=rounded_name(HID, FIRST, HIGH))
+        turn(1)
+        gather_centre(3, into=share[:, 1, :])
+        whole_pass_on_vector(HID, LAST)
+        squash(0, behind=raw_name(HID, LAST))
+        add_and_turn_back(0)
+        round_w4(on_vector, 0)
+        gather_difference(3, 1, behind=rounded_name(HID, LAST, LOW))
+        drain(HID, 0, on_vector, behind=w4_raw_name(0))
+        for t in (2, 3):
+            drain(HID, t, on_vector)
+        squash(1, behind=rounded_name(HID, LAST, HIGH))
         add_and_turn_back(1)
-        drain(HID, 1)
-        turn(2)
-        shares(1)
-        squash(2)
-        add_and_turn_back(2)
+        gather_centre(2, behind=codes_name(HID, LAST, LOW))
         turn(3)
-        drain(HID, 2)
+        turn(2)
+        drain(HID, 1)
+        gather_second(0)
+        gather_second(1)
+        quantise_w4(0)
+        gather_spread(0)
+        gather_spread(1)
+        shares(0)
         squash(3)
         add_and_turn_back(3)
-        shares(2)
-        drain(HID, 3)
+        squash(2)
+        add_and_turn_back(2)
+        gather_second(3, vector=True)
+        gather_second(2)
+        weigh(T0)
+        gather_spread(3)
+        gather_spread(2)
+        shares(1)
         shares(3)
-        for t in range(*LOW):
-            for d in range(2):
-                gather_values(t, d)
-        for a in range(2):
-            round_w4(on_vector, 0, a, 0, W4_ON_VECTOR)
-        for a in range(2):
-            round_w4(on_scalar, 0, a, W4_ON_VECTOR)
-        for a in range(2):
-            round_w4(on_scalar, 1, a)
-        for d in range(2):
-            gather_values(2, d)
-        gather_values(3, 0)
+        shares(2)
+        weigh(T1)
+        round_w4(on_scalar, 1, behind="squashed2")
         for c0 in (0, HALF):
-            gather_values(3, 1, c0, c0 + HALF)
+            weigh(HIGH, c0, c0 + HALF)
 
-        def warm_up(n, passes, codes, scales):
-            idle = bank(n)
-            for repeat in range(passes):
-                nc.tensor.matmul_mx(
-                    out=idle[:],
-                    lhsT=codes[:, :P].bitcast(FP8X4),
-                    lhsT_scale=scales[:, :P],
-                    rhs=xq[FIRST][:].bitcast(FP8X4),
-                    rhs_scale=xq_scales[:],
-                    start=True,
-                    stop=True,
-                )
-
-        warm_up(3, 2, *quantised[(Y, FIRST, LOW)])
-        warm_up(7, 3, *quantised[(Y, FIRST, LOW)])
-
-        sum_terms(0, behind=w4_raw_name(0))
-        quantise_w4(0)
-        warm_up(0, 1, w4_codes, w4_scales)
-        quantise_z(0)
+        sum_terms(0, behind="z_bf16_0")
         quantise_w4(1)
+        quantise_z(0)
         sum_terms(1, behind=w4_raw_name(1), pieces=2)
         quantise_z(1, pieces=2)
         projected = {}

@@ -26,11 +26,10 @@ RUNS = P // RUN
 K_PASS = P * PACK
 PASSES = K // K_PASS
 HALF = V // 2
-SIDE = N // 2
 Y, E, HID = 0, 1, 2
 FIRST, LAST = 0, 1
 LOW, HIGH, ALL = (0, 2), (2, 4), (0, 4)
-T0, T1 = (0, 1), (1, 2)
+T0, T1, T2, T3 = (0, 1), (1, 2), (2, 3), (3, 4)
 
 
 def tile_picked_zpt_tanh_po_kernel(
@@ -59,9 +58,6 @@ def tile_picked_zpt_tanh_po_kernel(
 
         def result_name(m, t):
             return "res_%d_%d" % (m, t)
-
-        def w4_raw_name(side):
-            return "w4_raw%d" % side
 
         def load_list(src, name):
             lst = sbuf(list(src.shape), U16, name)
@@ -102,11 +98,9 @@ def tile_picked_zpt_tanh_po_kernel(
         load_pass(w3, HID, FIRST)
         load_pass(w3, HID, LAST)
         w4_rows = w4.rearrange("(u t r) n -> t u r n", t=PACK, r=RUN)
-        w4_raw = []
-        for side in range(2):
-            w4_raw.append(sbuf([P, PACK, SIDE], F32, w4_raw_name(side)))
-            for t in range(PACK):
-                nc.sync.dma_start(w4_raw[side][:, t, :], w4_rows[t][:, :, side * SIDE : (side + 1) * SIDE])
+        w4_raw = sbuf([P, PACK, N], F32, "w4_raw")
+        for t in range(PACK):
+            nc.sync.dma_start(w4_raw[:, t, :], w4_rows[t])
 
         warm = sbuf([P, 1], F32, "warm")
         nc.scalar.activation(warm[:], raw[(E, FIRST)][:, 0, 0:1], SIGMOID)
@@ -171,72 +165,68 @@ def tile_picked_zpt_tanh_po_kernel(
                 nc.vector.tensor_copy(picked, window)
             else:
                 nc.scalar.activation(picked, window, COPY)
-            key[(t, d)] = (picked, False)
-
-        def gather_difference(t, d, behind):
-            into = sbuf([P, V], F32, behind)[:]
-            nc.vector.tensor_tensor(into, result[(E, t)][:].indirect(pos_t[d][:]), centre[t], ADD)
-            key[(t, d)] = (into, True)
+            key[(t, d)] = picked
 
         ident = sbuf([P, P], F32, "ident")
         make_identity(nc, ident[:])
 
-        def turn(t):
-            turned[t] = bank(4 + t)
-            for d in (1, 0):
-                picked, whole = key[(t, d)]
-                parts = (picked,) if whole else (centre[t], picked)
-                for c in range(0, V, P):
-                    for n, part in enumerate(parts):
+        units = {0: ((0, 0), (0, HALF)), 1: ((1, 0), (1, HALF)), 2: ((2, 0), (3, 0)), 3: ((2, HALF), (3, HALF))}
+
+        def turn(n):
+            turned[n] = bank(4 + n)
+            for d in range(2):
+                for b, (t, c) in reversed(list(enumerate(units[n]))):
+                    for first, part in ((True, centre[t]), (False, key[(t, d)])):
                         nc.tensor.matmul(
-                            turned[t][:, d * V + c : d * V + c + P],
+                            turned[n][:, d * V + b * P : d * V + (b + 1) * P],
                             part[:, c : c + P],
                             ident[:],
-                            start=(n == 0),
-                            stop=(n == len(parts) - 1),
+                            start=first,
+                            stop=not first,
                             is_transpose=True,
                         )
 
-        def squash(t, behind=None):
-            squashed[t] = sbuf([P, 2, V], F32, behind or "squashed%d" % t)
+        def squash(n, into=None):
+            squashed[n] = into if into is not None else sbuf([P, 2, V], F32, "squashed%d" % n)[:]
             for d, sign in enumerate((-1.0, 1.0)):
-                nc.scalar.activation(squashed[t][:, d, :], turned[t][:, d * V : (d + 1) * V], SIGMOID, scale=2.0 * sign)
+                nc.scalar.activation(squashed[n][:, d, :], turned[n][:, d * V : (d + 1) * V], SIGMOID, scale=2.0 * sign)
 
-        def add_and_turn_back(t):
-            summed[t] = bank(4 + t)
+        def add_and_turn_back(n):
+            summed[n] = bank(4 + n)
             for c in range(0, V, P):
                 for d in range(2):
                     nc.tensor.matmul(
-                        summed[t][:, c : c + P],
-                        squashed[t][:, d, c : c + P],
+                        summed[n][:, c : c + P],
+                        squashed[n][:, d, c : c + P],
                         ident[:],
                         start=(d == 0),
                         stop=(d == 1),
                         is_transpose=True,
                     )
 
-        def shares(t):
-            nc.scalar.activation(share[:, t, :], summed[t][:, :V], SIGMOID, scale=2.0, bias=-2.0)
+        def shares(n):
+            (t0, c0), (t1, c1) = units[n]
+            into = share[:, t0 : t1 + 1, c0 : c1 + P]
+            src = summed[n][:, :V].rearrange("p (t c) -> p t c", t=t1 + 1 - t0)
+            nc.scalar.activation(into, src, SIGMOID, scale=2.0, bias=-2.0)
 
-        w4_bf16 = {}
+        w4_bf16 = [sbuf([P, 2 * P * PACK], BF16, "w4_bf16_%d" % a) for a in range(2)]
         w4_codes = sbuf([P, N], U32, "w4_codes")
         w4_scales = sbuf([P, N], U8, "w4_scales")
 
-        def round_w4(copy, side, behind=None):
-            w4_bf16[side] = sbuf([P, PACK, SIDE], BF16, behind or "w4_bf16_%d" % side)
-            dst = w4_bf16[side][:].rearrange("p (a b) (m j) -> p a m j b", b=2, j=PACK)
-            src = w4_raw[side][:].rearrange("p j (m a b) -> p a m j b", a=2, b=2)
-            for a in range(2):
-                copy(dst[:, a], src[:, a])
+        def round_w4(a):
+            dst = w4_bf16[a][:].rearrange("p (b m j) -> p m j b", b=2, j=PACK)
+            src = w4_raw[:].rearrange("p j (m a b) -> p a m j b", a=2, b=2)
+            nc.vector.tensor_copy(dst, src[:, a])
 
         spread = sbuf([P, PACK, V], F32, "spread")
 
-        def gather_second(t, vector=False):
-            window = result[(HID, t)][:].indirect(pos_t[1][:])
+        def gather_second(t, c0=0, c1=V, vector=False):
+            window = result[(HID, t)][:].indirect(pos_t[1][:, c0 // 16 : c1 // 16])
             if vector:
-                nc.vector.tensor_copy(terms[1][:, t, :], window)
+                nc.vector.tensor_copy(terms[1][:, t, c0:c1], window)
             else:
-                nc.scalar.activation(terms[1][:, t, :], window, COPY)
+                nc.scalar.activation(terms[1][:, t, c0:c1], window, COPY)
 
         def gather_spread(t, c0=0, c1=V):
             window = result[(HID, t)][:].indirect(pos_t[0][:, c0 // 16 : c1 // 16])
@@ -249,12 +239,12 @@ def tile_picked_zpt_tanh_po_kernel(
         out_scales = sbuf([P, V], U8, "out_scales")
         out_codes = sbuf([P, V], U32, "out_codes")
 
-        def quantise_w4(side):
-            for t in range(PACK):
-                cols = slice(t * P + side * P // 2, t * P + (side + 1) * P // 2)
-                nc.vector.quantize_mx(
-                    out=w4_codes[:, cols].bitcast(FP8X4), scales=w4_scales[:, cols], in_=w4_bf16[side][:, t, :]
-                )
+        def quantise_w4(a):
+            nc.vector.quantize_mx(
+                out=w4_codes[:, a * 2 * P : (a + 1) * 2 * P].bitcast(FP8X4),
+                scales=w4_scales[:, a * 2 * P : (a + 1) * 2 * P],
+                in_=w4_bf16[a][:],
+            )
 
         z_bf16, z_codes, z_scales = {}, {}, {}
 
@@ -301,11 +291,12 @@ def tile_picked_zpt_tanh_po_kernel(
         quantise_and_multiply(E, FIRST, LOW)
         nc.vector.tensor_copy(xq[LAST][:], words[LAST][:].bitcast(U32).indirect(offs_t[:]))
         quantise_and_multiply(E, FIRST, HIGH)
-        round_pair(on_vector, E, LAST, LOW)
-        for n in range(2):
-            round_tile(on_scalar, E, LAST, HIGH, n)
-        for pair in (LOW, HIGH):
-            quantise_and_multiply(E, LAST, pair)
+        for group in (T0, T1):
+            round_tile(on_vector, E, LAST, group)
+        for group in (T2, T3):
+            round_tile(on_scalar, E, LAST, group)
+        for group in (T0, T1, T2, T3):
+            quantise_and_multiply(E, LAST, group)
 
         def whole_pass_on_vector(m, o):
             for pair in (LOW, HIGH):
@@ -317,15 +308,13 @@ def tile_picked_zpt_tanh_po_kernel(
         drain(E, 1)
         drain(E, 2)
         whole_pass_on_vector(Y, FIRST)
-        for d in range(2):
-            gather_key(0, d)
-        drain(E, 3)
+        drain(E, 3, on_vector, behind=raw_name(Y, FIRST))
+        for t in range(2):
+            for d in range(2):
+                gather_key(t, d)
         whole_pass_on_vector(Y, LAST)
-        for d in range(2):
-            gather_key(1, d)
-        gather_key(2, 1)
         gather_key(2, 0, into=terms[1][:, 2, :])
-        gather_key(3, 0, vector=True, behind=rounded_name(Y, LAST, LOW))
+        gather_key(2, 1)
         for t in range(3):
             drain(Y, t)
         whole_pass_on_vector(HID, FIRST)
@@ -334,48 +323,53 @@ def tile_picked_zpt_tanh_po_kernel(
         turn(0)
         gather_centre(1, behind=rounded_name(HID, FIRST, HIGH))
         turn(1)
-        gather_centre(3, into=share[:, 1, :])
+        gather_centre(2, behind=codes_name(HID, FIRST, LOW))
         whole_pass_on_vector(HID, LAST)
-        squash(0, behind=raw_name(HID, LAST))
-        add_and_turn_back(0)
-        round_w4(on_vector, 0)
-        gather_difference(3, 1, behind=rounded_name(HID, LAST, LOW))
-        drain(HID, 0, on_vector, behind=w4_raw_name(0))
-        for t in (2, 3):
-            drain(HID, t, on_vector)
-        squash(1, behind=rounded_name(HID, LAST, HIGH))
-        add_and_turn_back(1)
-        gather_centre(2, behind=codes_name(HID, LAST, LOW))
-        turn(3)
+        gather_centre(3, behind=raw_name(HID, LAST))
+        late_keys = sbuf([P, 2, V], F32, rounded_name(HID, LAST, LOW))
+        for d in range(2):
+            gather_key(3, d, vector=True, into=late_keys[:, d, :])
+        first_squashed = sbuf([P, 2, 2, V], F32, rounded_name(HID, LAST, HIGH))
+        for n in range(2):
+            squash(n, into=first_squashed[:, n])
         turn(2)
-        drain(HID, 1)
+        add_and_turn_back(0)
+        add_and_turn_back(1)
+        turn(3)
+        for t in (0, 3):
+            drain(HID, t, on_vector)
+        for t in (1, 2):
+            drain(HID, t)
+        for a in range(2):
+            round_w4(a)
         gather_second(0)
         gather_second(1)
-        quantise_w4(0)
+        for a in range(2):
+            quantise_w4(a)
         gather_spread(0)
         gather_spread(1)
-        shares(0)
-        squash(3)
-        add_and_turn_back(3)
         squash(2)
         add_and_turn_back(2)
-        gather_second(3, vector=True)
-        gather_second(2)
-        weigh(T0)
-        gather_spread(3)
-        gather_spread(2)
+        for t in range(*HIGH):
+            gather_second(t, 0, HALF)
+        squash(3)
+        add_and_turn_back(3)
+        shares(0)
         shares(1)
-        shares(3)
+        weigh(LOW)
         shares(2)
-        weigh(T1)
-        round_w4(on_scalar, 1, behind="squashed2")
-        for c0 in (0, HALF):
-            weigh(HIGH, c0, c0 + HALF)
-
-        sum_terms(0, behind="z_bf16_0")
-        quantise_w4(1)
+        for t in range(*HIGH):
+            gather_second(t, HALF, V)
+        shares(3)
+        for t in range(*HIGH):
+            gather_spread(t, 0, HALF)
+        weigh(HIGH, 0, HALF)
+        gather_spread(2, HALF, V)
+        sum_terms(0, behind="w4_raw")
+        gather_spread(3, HALF, V)
         quantise_z(0)
-        sum_terms(1, behind=w4_raw_name(1), pieces=2)
+        weigh(HIGH, HALF, V)
+        sum_terms(1, behind="w4_bf16_1", pieces=2)
         quantise_z(1, pieces=2)
         projected = {}
         for g in range(2):

@@ -29,7 +29,7 @@ HALF = V // 2
 Y, E, HID = 0, 1, 2
 FIRST, LAST = 0, 1
 LOW, HIGH, ALL = (0, 2), (2, 4), (0, 4)
-T0, T1, T2, T3 = (0, 1), (1, 2), (2, 3), (3, 4)
+SINGLES = [(t, t + 1) for t in range(PACK)]
 
 
 def tile_picked_zpt_tanh_po_kernel(
@@ -85,14 +85,14 @@ def tile_picked_zpt_tanh_po_kernel(
                 nc.sync.dma_start(x_bytes[4 * o + r : P : 32, :].bitcast(I32), rows[r].bitcast(I32))
 
         words = [load_words(FIRST)]
-        load_scale_rows(FIRST)
         offs_t = load_list(offs, "offs")
+        load_scale_rows(FIRST)
         load_pass(w2, E, FIRST)
         load_scale_rows(LAST)
         words.append(load_words(LAST))
         load_pass(w2, E, LAST)
-        pos_t = [load_list(pos1, "pos1"), load_list(pos2, "pos2")]
         load_pass(w1, Y, FIRST)
+        pos_t = [load_list(pos1, "pos1"), load_list(pos2, "pos2")]
         load_pass(w1, Y, LAST)
         cen_t = load_list(cen, "cen")
         load_pass(w3, HID, FIRST)
@@ -107,29 +107,27 @@ def tile_picked_zpt_tanh_po_kernel(
 
         xq = [sbuf([P, S], U32, "xq%d" % o) for o in range(PASSES)]
         xq_scales = sbuf([P, S], U8, "xq_scales")
-        rounded, quantised, banks, result = {}, {}, {}, {}
+        rounded, banks, result = {}, {}, {}
 
         def rounding_views(m, o, group):
-            key = (m, o, group)
-            if key not in rounded:
-                rounded[key] = sbuf([P, (group[1] - group[0]) * P * PACK], BF16, rounded_name(m, o, group))
-            dst = rounded[key][:].rearrange("p (t u r j) -> p t u j r", u=RUNS, r=RUN, j=PACK)
+            if (m, o, group) not in rounded:
+                rounded[(m, o, group)] = sbuf([P, (group[1] - group[0]) * P * PACK], BF16, rounded_name(m, o, group))
+            dst = rounded[(m, o, group)][:].rearrange("p (t u r j) -> p t u j r", u=RUNS, r=RUN, j=PACK)
             src = raw[(m, o)][:].rearrange("p j (u t r) -> p t u j r", t=PACK, r=RUN)
             return dst, src[:, group[0] : group[1]]
 
-        def round_pair(copy, m, o, pair):
-            copy(*rounding_views(m, o, pair))
+        def round_pair(m, o, pair):
+            nc.vector.tensor_copy(*rounding_views(m, o, pair))
 
-        def round_tile(copy, m, o, group, n=0, runs=slice(0, RUNS)):
+        def round_tile(copy, m, o, group, n=0):
             dst, src = rounding_views(m, o, group)
-            copy(dst[:, n, runs], src[:, n, runs])
+            copy(dst[:, n], src[:, n])
 
-        def quantise_and_multiply(m, o, group, behind=None):
+        def quantise_and_multiply(m, o, group):
             width = (group[1] - group[0]) * P
-            codes = sbuf([P, width], U32, behind or codes_name(m, o, group))
+            codes = sbuf([P, width], U32, codes_name(m, o, group))
             scales = sbuf([P, width], U8, "scales_%d_%d_%d" % (m, o, group[0]))
             nc.vector.quantize_mx(out=codes[:].bitcast(FP8X4), scales=scales[:], in_=rounded[(m, o, group)][:])
-            quantised[(m, o, group)] = (codes, scales)
             for t in range(*group):
                 if o == FIRST:
                     banks[(m, t)] = bank((PACK if m == Y else 0) + t)
@@ -149,23 +147,20 @@ def tile_picked_zpt_tanh_po_kernel(
             copy(result[(m, t)][:], banks[(m, t)][:])
 
         centre, key, turned, squashed, summed = {}, {}, {}, {}, {}
-
-        terms = [sbuf([P, PACK, V], F32, "term%d" % d) for d in range(2)]
-
+        weighted = sbuf([P, PACK, V], F32, "term0")
+        second = sbuf([P, PACK, V], F32, "term1")
         share = sbuf([P, PACK, V], F32, "share")
 
-        def gather_centre(t, behind=None, into=None):
-            centre[t] = into if into is not None else sbuf([P, V], F32, behind or "centre%d" % t)[:]
-            nc.scalar.activation(centre[t], result[(Y, t)][:].indirect(cen_t[:]), COPY, scale=-1.0)
+        def gather_centre(t, behind):
+            centre[t] = sbuf([P, V], F32, behind)
+            nc.scalar.activation(centre[t][:], result[(Y, t)][:].indirect(cen_t[:]), COPY, scale=-1.0)
 
-        def gather_key(t, d, vector=False, behind=None, into=None):
-            picked = into if into is not None else sbuf([P, V], F32, behind or "key%d_%d" % (t, d))[:]
-            window = result[(E, t)][:].indirect(pos_t[d][:])
-            if vector:
-                nc.vector.tensor_copy(picked, window)
-            else:
-                nc.scalar.activation(picked, window, COPY)
-            key[(t, d)] = picked
+        def gather_on_scalar(into, window):
+            nc.scalar.activation(into, window, COPY)
+
+        def gather_key(t, d, gather=gather_on_scalar, into=None):
+            key[(t, d)] = sbuf([P, V], F32, "key%d_%d" % (t, d))[:] if into is None else into
+            gather(key[(t, d)], result[(E, t)][:].indirect(pos_t[d][:]))
 
         ident = sbuf([P, P], F32, "ident")
         make_identity(nc, ident[:])
@@ -187,7 +182,7 @@ def tile_picked_zpt_tanh_po_kernel(
                         )
 
         def squash(n, into=None):
-            squashed[n] = into if into is not None else sbuf([P, 2, V], F32, "squashed%d" % n)[:]
+            squashed[n] = sbuf([P, 2, V], F32, "squashed%d" % n)[:] if into is None else into
             for d, sign in enumerate((-1.0, 1.0)):
                 nc.scalar.activation(squashed[n][:, d, :], turned[n][:, d * V : (d + 1) * V], SIGMOID, scale=2.0 * sign)
 
@@ -221,20 +216,18 @@ def tile_picked_zpt_tanh_po_kernel(
 
         spread = sbuf([P, PACK, V], F32, "spread")
 
-        def gather_second(t, c0=0, c1=V, vector=False):
-            window = result[(HID, t)][:].indirect(pos_t[1][:, c0 // 16 : c1 // 16])
-            if vector:
-                nc.vector.tensor_copy(terms[1][:, t, c0:c1], window)
-            else:
-                nc.scalar.activation(terms[1][:, t, c0:c1], window, COPY)
+        def picked_values(t, d, c0, c1):
+            return result[(HID, t)][:].indirect(pos_t[d][:, c0 // 16 : c1 // 16])
+
+        def gather_second(t, c0=0, c1=V):
+            gather_on_scalar(second[:, t, c0:c1], picked_values(t, 1, c0, c1))
 
         def gather_spread(t, c0=0, c1=V):
-            window = result[(HID, t)][:].indirect(pos_t[0][:, c0 // 16 : c1 // 16])
-            nc.vector.tensor_tensor(spread[:, t, c0:c1], window, terms[1][:, t, c0:c1], SUB)
+            nc.vector.tensor_tensor(spread[:, t, c0:c1], picked_values(t, 0, c0, c1), second[:, t, c0:c1], SUB)
 
         def weigh(group, c0=0, c1=V):
             part = (slice(0, P), slice(*group), slice(c0, c1))
-            nc.vector.tensor_tensor(terms[0][part], spread[part], share[part], MULT)
+            nc.vector.tensor_tensor(weighted[part], spread[part], share[part], MULT)
 
         out_scales = sbuf([P, V], U8, "out_scales")
         out_codes = sbuf([P, V], U32, "out_codes")
@@ -255,8 +248,8 @@ def tile_picked_zpt_tanh_po_kernel(
                 c0 = g * HALF + c
                 nc.vector.tensor_tensor(
                     z_bf16[g][:, c * PACK : (c + width) * PACK].rearrange("p (c r t) -> p c t r", r=RUN, t=PACK),
-                    terms[0][:, :, c0 : c0 + width].rearrange("p t (c r) -> p c t r", r=RUN),
-                    terms[1][:, :, c0 : c0 + width].rearrange("p t (c r) -> p c t r", r=RUN),
+                    weighted[:, :, c0 : c0 + width].rearrange("p t (c r) -> p c t r", r=RUN),
+                    second[:, :, c0 : c0 + width].rearrange("p t (c r) -> p c t r", r=RUN),
                     ADD,
                 )
 
@@ -283,6 +276,7 @@ def tile_picked_zpt_tanh_po_kernel(
                     stop=True,
                 )
 
+
         nc.vector.tensor_copy(xq[FIRST][:], words[FIRST][:].bitcast(U32).indirect(offs_t[:]))
         for pair in (LOW, HIGH):
             for n in range(2):
@@ -291,16 +285,16 @@ def tile_picked_zpt_tanh_po_kernel(
         quantise_and_multiply(E, FIRST, LOW)
         nc.vector.tensor_copy(xq[LAST][:], words[LAST][:].bitcast(U32).indirect(offs_t[:]))
         quantise_and_multiply(E, FIRST, HIGH)
-        for group in (T0, T1):
+        for group in SINGLES[:2]:
             round_tile(on_vector, E, LAST, group)
-        for group in (T2, T3):
+        for group in SINGLES[2:]:
             round_tile(on_scalar, E, LAST, group)
-        for group in (T0, T1, T2, T3):
+        for group in SINGLES:
             quantise_and_multiply(E, LAST, group)
 
         def whole_pass_on_vector(m, o):
             for pair in (LOW, HIGH):
-                round_pair(on_vector, m, o, pair)
+                round_pair(m, o, pair)
             for pair in (LOW, HIGH):
                 quantise_and_multiply(m, o, pair)
 
@@ -313,7 +307,7 @@ def tile_picked_zpt_tanh_po_kernel(
             for d in range(2):
                 gather_key(t, d)
         whole_pass_on_vector(Y, LAST)
-        gather_key(2, 0, into=terms[1][:, 2, :])
+        gather_key(2, 0, into=second[:, 2, :])
         gather_key(2, 1)
         for t in range(3):
             drain(Y, t)
@@ -328,7 +322,7 @@ def tile_picked_zpt_tanh_po_kernel(
         gather_centre(3, behind=raw_name(HID, LAST))
         late_keys = sbuf([P, 2, V], F32, rounded_name(HID, LAST, LOW))
         for d in range(2):
-            gather_key(3, d, vector=True, into=late_keys[:, d, :])
+            gather_key(3, d, on_vector, into=late_keys[:, d, :])
         first_squashed = sbuf([P, 2, 2, V], F32, rounded_name(HID, LAST, HIGH))
         for n in range(2):
             squash(n, into=first_squashed[:, n])
@@ -336,6 +330,7 @@ def tile_picked_zpt_tanh_po_kernel(
         add_and_turn_back(0)
         add_and_turn_back(1)
         turn(3)
+
         for t in (0, 3):
             drain(HID, t, on_vector)
         for t in (1, 2):

from contextlib import ExitStack

import concourse.mybir as mybir
from concourse.masks import make_identity

K, T, S, V, H, N = 1024, 1024, 512, 256, 512, 512
FLOPS = 2 * (3 * K * N * S + H * N * V)

F32 = mybir.dt.float32
BF16 = mybir.dt.bfloat16
I32 = mybir.dt.int32
U32 = mybir.dt.uint32
U16 = mybir.dt.uint16
U8 = mybir.dt.uint8
FP8X4 = mybir.dt.float8_e4m3fn_x4
SIGMOID = mybir.ActivationFunctionType.Sigmoid
COPY = mybir.ActivationFunctionType.Copy
ADD = mybir.AluOpType.add
SUB = mybir.AluOpType.subtract
MULT = mybir.AluOpType.mult

P = 128
PACK = 4
RUN = 4
RUNS = P // RUN
K_PASS = P * PACK
PASSES = K // K_PASS
HALF = V // 2
Y, E, HID = 0, 1, 2
FIRST, LAST = 0, 1
LOW, HIGH, ALL = (0, 2), (2, 4), (0, 4)
SINGLES = [(t, t + 1) for t in range(PACK)]


def tile_picked_zpt_tanh_po_kernel(
    tc, x_words, x_scales, w1, w2, w3, w4, offs, cen, pos1, pos2, out_0, out_1, out_2
):
    nc = tc.nc
    on_vector, on_scalar = nc.vector.tensor_copy, nc.scalar.copy
    with ExitStack() as ctx:
        keep = ctx.enter_context(tc.tile_pool(name="keep", bufs=1))
        psum = ctx.enter_context(tc.psum_pool(name="psum", bufs=1))

        def sbuf(shape, dtype, name):
            return keep.tile(shape, dtype, name=name, align_bytes=64)

        def bank(n):
            return psum.tile([P, S], F32, name="bank%d" % n)

        def raw_name(m, o):
            return "w%d_raw%d" % (m + 1, o)

        def rounded_name(m, o, group):
            return "bf_%d_%d_%d" % (m, o, group[0])

        def codes_name(m, o, group):
            return "codes_%d_%d_%d" % (m, o, group[0])

        def result_name(m, t):
            return "res_%d_%d" % (m, t)

        def load_list(src, name):
            lst = sbuf(list(src.shape), U16, name)
            nc.sync.dma_start(lst[:], src)
            return lst

        def load_words(o):
            loaded = sbuf([P, T], I32, "x_words%d" % o)
            nc.sync.dma_start(loaded[:], x_words[o].rearrange("p c r -> p (c r)").bitcast(I32))
            return loaded

        raw = {}

        def load_pass(w, m, o):
            raw[(m, o)] = sbuf([P, PACK, N], F32, raw_name(m, o))
            rows = w[o * K_PASS : (o + 1) * K_PASS, :]
            nc.sync.dma_start(raw[(m, o)][:], rows.rearrange("(p j) n -> p j n", j=PACK))

        x_bytes = sbuf([P, T], U8, "x_bytes")
        nc.vector.memset(x_bytes[:].bitcast(I32), 0)

        def load_scale_rows(o):
            rows = x_scales[o].rearrange("(q r) c -> r q c", r=4)
            for r in range(4):
                nc.sync.dma_start(x_bytes[4 * o + r : P : 32, :].bitcast(I32), rows[r].bitcast(I32))

        words = [load_words(FIRST)]
        offs_t = load_list(offs, "offs")
        load_scale_rows(FIRST)
        load_pass(w2, E, FIRST)
        load_scale_rows(LAST)
        words.append(load_words(LAST))
        load_pass(w2, E, LAST)
        load_pass(w1, Y, FIRST)
        pos_t = [load_list(pos1, "pos1"), load_list(pos2, "pos2")]
        load_pass(w1, Y, LAST)
        cen_t = load_list(cen, "cen")
        load_pass(w3, HID, FIRST)
        load_pass(w3, HID, LAST)
        w4_rows = w4.rearrange("(u t r) n -> t u r n", t=PACK, r=RUN)
        w4_raw = sbuf([P, PACK, N], F32, "w4_raw")
        for t in range(PACK):
            nc.sync.dma_start(w4_raw[:, t, :], w4_rows[t])

        warm = sbuf([P, 1], F32, "warm")
        nc.scalar.activation(warm[:], raw[(E, FIRST)][:, 0, 0:1], SIGMOID)

        xq = [sbuf([P, S], U32, "xq%d" % o) for o in range(PASSES)]
        xq_scales = sbuf([P, S], U8, "xq_scales")
        rounded, banks, result = {}, {}, {}

        def rounding_views(m, o, group):
            if (m, o, group) not in rounded:
                rounded[(m, o, group)] = sbuf([P, (group[1] - group[0]) * P * PACK], BF16, rounded_name(m, o, group))
            dst = rounded[(m, o, group)][:].rearrange("p (t u r j) -> p t u j r", u=RUNS, r=RUN, j=PACK)
            src = raw[(m, o)][:].rearrange("p j (u t r) -> p t u j r", t=PACK, r=RUN)
            return dst, src[:, group[0] : group[1]]

        def round_pair(m, o, pair):
            nc.vector.tensor_copy(*rounding_views(m, o, pair))

        def round_tile(copy, m, o, group, n=0):
            dst, src = rounding_views(m, o, group)
            copy(dst[:, n], src[:, n])

        def quantise_and_multiply(m, o, group):
            width = (group[1] - group[0]) * P
            codes = sbuf([P, width], U32, codes_name(m, o, group))
            scales = sbuf([P, width], U8, "scales_%d_%d_%d" % (m, o, group[0]))
            nc.vector.quantize_mx(out=codes[:].bitcast(FP8X4), scales=scales[:], in_=rounded[(m, o, group)][:])
            for t in range(*group):
                if o == FIRST:
                    banks[(m, t)] = bank((PACK if m == Y else 0) + t)
                cols = slice((t - group[0]) * P, (t - group[0] + 1) * P)
                nc.tensor.matmul_mx(
                    out=banks[(m, t)][:],
                    lhsT=codes[:, cols].bitcast(FP8X4),
                    lhsT_scale=scales[:, cols],
                    rhs=xq[o][:].bitcast(FP8X4),
                    rhs_scale=xq_scales[4 * o : P, :],
                    start=(o == FIRST),
                    stop=(o == LAST),
                )

        def drain(m, t, copy=on_scalar, behind=None):
            result[(m, t)] = sbuf([P, S], F32, behind or result_name(m, t))
            copy(result[(m, t)][:], banks[(m, t)][:])

        centre, key, turned, squashed, summed = {}, {}, {}, {}, {}
        weighted = sbuf([P, PACK, V], F32, "term0")
        second = sbuf([P, PACK, V], F32, "term1")
        share = sbuf([P, PACK, V], F32, "share")

        def gather_centre(t, behind):
            centre[t] = sbuf([P, V], F32, behind)
            nc.scalar.activation(centre[t][:], result[(Y, t)][:].indirect(cen_t[:]), COPY, scale=-1.0)

        def gather_on_scalar(into, window):
            nc.scalar.activation(into, window, COPY)

        def gather_key(t, d, gather=gather_on_scalar, into=None):
            key[(t, d)] = sbuf([P, V], F32, "key%d_%d" % (t, d))[:] if into is None else into
            gather(key[(t, d)], result[(E, t)][:].indirect(pos_t[d][:]))

        ident = sbuf([P, P], F32, "ident")
        make_identity(nc, ident[:])

        units = {0: ((0, 0), (0, HALF)), 1: ((1, 0), (1, HALF)), 2: ((2, 0), (3, 0)), 3: ((2, HALF), (3, HALF))}

        def turn(n):
            turned[n] = bank(4 + n)
            for d in range(2):
                for b, (t, c) in reversed(list(enumerate(units[n]))):
                    for first, part in ((True, centre[t]), (False, key[(t, d)])):
                        nc.tensor.matmul(
                            turned[n][:, d * V + b * P : d * V + (b + 1) * P],
                            part[:, c : c + P],
                            ident[:],
                            start=first,
                            stop=not first,
                            is_transpose=True,
                        )

        def squash(n, into=None):
            squashed[n] = sbuf([P, 2, V], F32, "squashed%d" % n)[:] if into is None else into
            for d, sign in enumerate((-1.0, 1.0)):
                nc.scalar.activation(squashed[n][:, d, :], turned[n][:, d * V : (d + 1) * V], SIGMOID, scale=2.0 * sign)

        def add_and_turn_back(n):
            summed[n] = bank(4 + n)
            for c in range(0, V, P):
                for d in range(2):
                    nc.tensor.matmul(
                        summed[n][:, c : c + P],
                        squashed[n][:, d, c : c + P],
                        ident[:],
                        start=(d == 0),
                        stop=(d == 1),
                        is_transpose=True,
                    )

        def shares(n):
            (t0, c0), (t1, c1) = units[n]
            into = share[:, t0 : t1 + 1, c0 : c1 + P]
            src = summed[n][:, :V].rearrange("p (t c) -> p t c", t=t1 + 1 - t0)
            nc.scalar.activation(into, src, SIGMOID, scale=2.0, bias=-2.0)

        w4_bf16 = [sbuf([P, 2 * P * PACK], BF16, "w4_bf16_%d" % a) for a in range(2)]
        w4_codes = sbuf([P, N], U32, "w4_codes")
        w4_scales = sbuf([P, N], U8, "w4_scales")

        def round_w4(a):
            dst = w4_bf16[a][:].rearrange("p (b m j) -> p m j b", b=2, j=PACK)
            src = w4_raw[:].rearrange("p j (m a b) -> p a m j b", a=2, b=2)
            nc.vector.tensor_copy(dst, src[:, a])

        spread = sbuf([P, PACK, V], F32, "spread")

        def picked_values(t, d, c0, c1):
            return result[(HID, t)][:].indirect(pos_t[d][:, c0 // 16 : c1 // 16])

        def gather_second(t, c0=0, c1=V):
            gather_on_scalar(second[:, t, c0:c1], picked_values(t, 1, c0, c1))

        def gather_spread(t, c0=0, c1=V):
            nc.vector.tensor_tensor(spread[:, t, c0:c1], picked_values(t, 0, c0, c1), second[:, t, c0:c1], SUB)

        def weigh(group, c0=0, c1=V):
            part = (slice(0, P), slice(*group), slice(c0, c1))
            nc.vector.tensor_tensor(weighted[part], spread[part], share[part], MULT)

        out_scales = sbuf([P, V], U8, "out_scales")
        out_codes = sbuf([P, V], U32, "out_codes")

        def quantise_w4(a):
            nc.vector.quantize_mx(
                out=w4_codes[:, a * 2 * P : (a + 1) * 2 * P].bitcast(FP8X4),
                scales=w4_scales[:, a * 2 * P : (a + 1) * 2 * P],
                in_=w4_bf16[a][:],
            )

        z_bf16, z_codes, z_scales = {}, {}, {}

        def sum_terms(g, behind, pieces=1):
            z_bf16[g] = sbuf([P, HALF * PACK], BF16, behind)
            width = HALF // pieces
            for c in range(0, HALF, width):
                c0 = g * HALF + c
                nc.vector.tensor_tensor(
                    z_bf16[g][:, c * PACK : (c + width) * PACK].rearrange("p (c r t) -> p c t r", r=RUN, t=PACK),
                    weighted[:, :, c0 : c0 + width].rearrange("p t (c r) -> p c t r", r=RUN),
                    second[:, :, c0 : c0 + width].rearrange("p t (c r) -> p c t r", r=RUN),
                    ADD,
                )

        def quantise_z(g, pieces=1):
            z_codes[g] = sbuf([P, HALF], U32, "z_codes%d" % g)
            z_scales[g] = sbuf([P, HALF], U8, "z_scales%d" % g)
            width = HALF // pieces
            for c in range(0, HALF, width):
                nc.vector.quantize_mx(
                    out=z_codes[g][:, c : c + width].bitcast(FP8X4),
                    scales=z_scales[g][:, c : c + width],
                    in_=z_bf16[g][:, c * PACK : (c + width) * PACK],
                )

        def project(target, g, pair):
            for t in range(*pair):
                nc.tensor.matmul_mx(
                    out=target[:, (t - pair[0]) * HALF : (t - pair[0] + 1) * HALF],
                    lhsT=w4_codes[:, t * P : (t + 1) * P].bitcast(FP8X4),
                    lhsT_scale=w4_scales[:, t * P : (t + 1) * P],
                    rhs=z_codes[g][:].bitcast(FP8X4),
                    rhs_scale=z_scales[g][:],
                    start=True,
                    stop=True,
                )


        nc.vector.tensor_copy(xq[FIRST][:], words[FIRST][:].bitcast(U32).indirect(offs_t[:]))
        for pair in (LOW, HIGH):
            for n in range(2):
                round_tile(on_scalar, E, FIRST, pair, n)
        nc.vector.tensor_copy(xq_scales[:], x_bytes[:].indirect(offs_t[:]))
        quantise_and_multiply(E, FIRST, LOW)
        nc.vector.tensor_copy(xq[LAST][:], words[LAST][:].bitcast(U32).indirect(offs_t[:]))
        quantise_and_multiply(E, FIRST, HIGH)
        for group in SINGLES[:2]:
            round_tile(on_vector, E, LAST, group)
        for group in SINGLES[2:]:
            round_tile(on_scalar, E, LAST, group)
        for group in SINGLES:
            quantise_and_multiply(E, LAST, group)

        def whole_pass_on_vector(m, o):
            for pair in (LOW, HIGH):
                round_pair(m, o, pair)
            for pair in (LOW, HIGH):
                quantise_and_multiply(m, o, pair)

        drain(E, 0, on_vector)
        drain(E, 1)
        drain(E, 2)
        whole_pass_on_vector(Y, FIRST)
        drain(E, 3, on_vector, behind=raw_name(Y, FIRST))
        for t in range(2):
            for d in range(2):
                gather_key(t, d)
        whole_pass_on_vector(Y, LAST)
        gather_key(2, 0, into=second[:, 2, :])
        gather_key(2, 1)
        for t in range(3):
            drain(Y, t)
        whole_pass_on_vector(HID, FIRST)
        drain(Y, 3, on_vector, behind=raw_name(HID, FIRST))
        gather_centre(0, behind=rounded_name(HID, FIRST, LOW))
        turn(0)
        gather_centre(1, behind=rounded_name(HID, FIRST, HIGH))
        turn(1)
        gather_centre(2, behind=codes_name(HID, FIRST, LOW))
        whole_pass_on_vector(HID, LAST)
        gather_centre(3, behind=raw_name(HID, LAST))
        late_keys = sbuf([P, 2, V], F32, rounded_name(HID, LAST, LOW))
        for d in range(2):
            gather_key(3, d, on_vector, into=late_keys[:, d, :])
        first_squashed = sbuf([P, 2, 2, V], F32, rounded_name(HID, LAST, HIGH))
        for n in range(2):
            squash(n, into=first_squashed[:, n])
        turn(2)
        add_and_turn_back(0)
        add_and_turn_back(1)
        turn(3)

        for t in (0, 3):
            drain(HID, t, on_vector)
        for t in (1, 2):
            drain(HID, t)
        for a in range(2):
            round_w4(a)
        gather_second(0)
        gather_second(1)
        for a in range(2):
            quantise_w4(a)
        gather_spread(0)
        gather_spread(1)
        squash(2)
        add_and_turn_back(2)
        for t in range(*HIGH):
            gather_second(t, 0, HALF)
        squash(3)
        add_and_turn_back(3)
        shares(0)
        shares(1)
        weigh(LOW)
        shares(2)
        for t in range(*HIGH):
            gather_second(t, HALF, V)
        shares(3)
        for t in range(*HIGH):
            gather_spread(t, 0, HALF)
        weigh(HIGH, 0, HALF)
        gather_spread(2, HALF, V)
        sum_terms(0, behind="w4_raw")
        gather_spread(3, HALF, V)
        quantise_z(0)
        weigh(HIGH, HALF, V)
        sum_terms(1, behind="w4_bf16_1", pieces=2)
        quantise_z(1, pieces=2)
        projected = {}
        for g in range(2):
            for a, pair in enumerate((LOW, HIGH)):
                projected[(g, a)] = bank(4 + 2 * g + a)
                project(projected[(g, a)], g, pair)

        out_rows = out_0.rearrange("(p t) v -> p t v", t=PACK)

        def round_and_quantise(values, c0, groups):
            as_bf16 = sbuf([P, HALF * PACK], BF16, "out_bf16_%d" % c0)
            dst = as_bf16[:].rearrange("p (c r t) -> p c t r", r=RUN, t=PACK)
            src = values[:].rearrange("p t (c r) -> p c t r", r=RUN)
            for lo, hi in groups[:-1]:
                nc.vector.tensor_copy(dst[:, :, lo:hi], src[:, :, lo:hi])
            lo, hi = groups[-1]
            for runs in (slice(0, RUNS // 2), slice(RUNS // 2, RUNS)):
                nc.vector.tensor_copy(dst[:, runs, lo:hi], src[:, runs, lo:hi])
            for c in (0, HALF // 2):
                cols = slice(c0 + c, c0 + c + HALF // 2)
                nc.vector.quantize_mx(
                    out=out_codes[:, cols].bitcast(FP8X4),
                    scales=out_scales[:, cols],
                    in_=as_bf16[:, c * PACK : (c + HALF // 2) * PACK],
                )

        def copy_out(values, g, a):
            piece = values[:, 2 * a : 2 * a + 2]
            nc.scalar.copy(piece.rearrange("p t v -> p (t v)"), projected[(g, a)][:, : 2 * HALF])
            return piece

        first_values = sbuf([P, PACK, HALF], F32, "first_values")
        for a in range(2):
            copy_out(first_values, 0, a)
        nc.sync.dma_start(out_rows[:, :, :HALF], first_values[:])
        round_and_quantise(first_values, 0, [ALL])
        second_values = sbuf([P, PACK, HALF], F32, "second_values")
        for a in range(2):
            nc.sync.dma_start(out_rows[:, 2 * a : 2 * a + 2, HALF:], copy_out(second_values, 1, a))
        round_and_quantise(second_values, HALF, [LOW, HIGH])
        nc.sync.dma_start(out_1[0].rearrange("p c r -> p (c r)").bitcast(I32), out_codes[:].bitcast(I32))
        for q, queue in enumerate((nc.sync, nc.sync, nc.scalar, nc.scalar)):
            queue.dma_start(out_2[0, 4 * q : 4 * q + 4, :].bitcast(I32), out_scales[32 * q : 32 * q + 4, :].bitcast(I32))
